import numpy as np
import ml_dtypes


def mxq(x, axis, fmt="e4m3"):
    dtype, down = {"e4m3": (ml_dtypes.float8_e4m3fn, 7), "e5m2": (ml_dtypes.float8_e5m2, 14)}[fmt]
    v = np.moveaxis(np.asarray(x, np.float32).astype(ml_dtypes.bfloat16).astype(np.float64), axis, -1)
    blocks = v.reshape(v.shape[:-1] + (-1, 32))
    amax = np.abs(blocks).max(-1, keepdims=True)
    byte = np.maximum(np.where(amax > 0, np.frexp(amax)[1] - 1 + 127, 0) - down, 1)
    scale = np.exp2(byte - 127.0)
    codes = (blocks / scale).astype(np.float32).astype(dtype).astype(np.float64)
    return np.moveaxis((codes * scale).reshape(v.shape), -1, axis)


WIDE = False


def mx_kscale(k):
    if not WIDE:
        return np.ones(k)
    levels = np.array([10, -10, 5, -5, 0])
    if k % 512:
        return np.exp2(np.random.permutation(np.resize(levels, k // 32))).repeat(32)
    a = np.empty((k // 512, 16))
    for p in range(k // 512):
        a[p, :8] = np.random.permutation(np.resize(levels, 8))
        for g in range(8):
            far = levels[np.abs(levels - a[p, g]) >= 10]
            a[p, g + 8] = far[np.random.randint(len(far))]
    return np.exp2(a.ravel()).repeat(32)


def f64(x):
    return np.asarray(x).astype(np.float64)


def striped(idx):
    return np.tile(np.asarray(idx).reshape(-1, 16).T, (8, 1)).astype(np.uint16)


def unstriped(offs):
    return offs[:16].T.reshape(-1).astype(np.int64)


E2M1 = np.array([0.0, 0.5, 1.0, 1.5, 2.0, 3.0, 4.0, 6.0, -0.0, -0.5, -1.0, -1.5, -2.0, -3.0, -4.0, -6.0])


def pack_weight(w, fmt):
    k, n = w.shape
    w = f64(np.asarray(w, np.float32).astype(ml_dtypes.bfloat16)).reshape(k // 32, 32, n)
    amax = np.abs(w).max(1)
    if fmt == "e4m3":
        byte = np.frexp(amax)[1] - 1 + 127 - 7
    else:
        mant, ex = np.frexp(amax / 6.0)
        byte = np.where(mant > 0.5, ex, ex - 1) + 127
    byte = np.clip(np.where(amax > 0, byte, 1), 1, 254)
    scaled = (w * np.exp2(127.0 - byte)[:, None, :]).reshape(k, n).astype(np.float32)
    by_word = np.ascontiguousarray(scaled.reshape(k // 512, 128, 4, n).transpose(0, 1, 3, 2))
    if fmt == "e4m3":
        words = by_word.astype(ml_dtypes.float8_e4m3fn).view(np.uint8)
    else:
        c = by_word.astype(ml_dtypes.float4_e2m1fn).view(np.uint8) & 0xF
        words = (c[..., 0::2] | (c[..., 1::2] << 4)).reshape(k // 512, 128, 2 * n)
    return np.ascontiguousarray(words), np.ascontiguousarray(byte.astype(np.uint8).reshape(k // 512, 16, n))


def unpack_weight(words, scales, fmt):
    g, _, n = scales.shape
    words = np.ascontiguousarray(words).reshape(g, 128, n, -1)
    if fmt == "e4m3":
        vals = words.view(ml_dtypes.float8_e4m3fn).astype(np.float64)
    else:
        nib = np.empty((g, 128, n, 4), np.uint8)
        nib[..., 0::2] = words & 0xF
        nib[..., 1::2] = words >> 4
        vals = E2M1[nib]
    vals = vals * np.repeat(np.exp2(scales.astype(np.float64) - 127.0), 8, axis=1)[..., None]
    return vals.transpose(0, 1, 3, 2).reshape(g * 512, n)


B, N, T, D, DV, NQ = 1, 1024, 2048, 1024, 128, 256


def setup_inputs():
    n = np.random.standard_normal
    idx = np.random.permutation(T)[:B * N]
    s = mx_kscale(D)[:, None]
    u = np.ones(T)
    u[idx] = mx_kscale(B * N)
    r = np.random.uniform(0.5, 2.0, T)
    k = n((D, T)) / s
    v = n((DV, T)) / (u * r)
    kp = pack_weight(k, "e2m1")
    return {
        "qT": (n((B, D, NQ)) * s * (0.80 / np.sqrt(D))).astype(np.float32),
        "k_words": np.ascontiguousarray(kp[0].reshape(D // 1024, 2, 128, T, 2).transpose(0, 2, 3, 1, 4)).reshape(D // 1024, 128, T, 4),
        "k_scales": kp[1],
        "vT": v.astype(np.float32),
        "vs": np.tile(u * r, (128, 1)).astype(np.float32),
        "kb": np.tile(n(T), (128, 1)).astype(np.float32),
        "og": n((B, NQ, DV)).astype(np.float32),
        "offs": striped(idx),
    }


def reference(qT, k_words, k_scales, vT, vs, kb, og, offs):
    idx = unstriped(offs)
    k = unpack_weight(k_words.reshape(D // 1024, 128, T, 2, 2).transpose(0, 3, 1, 2, 4).reshape(D // 512, 128, 2 * T), k_scales, "e2m1")
    v = f64(vT)
    pick = lambda x: x[:, idx].reshape(x.shape[0], B, N).transpose(1, 0, 2)
    q = f64(qT)
    score = mxq(q, 1, "e4m3").transpose(0, 2, 1) @ pick(k)
    score = score + pick(f64(kb))[:, :1, :]
    p = score / (1.0 + np.exp(-score))
    w = p * pick(f64(vs))[:, :1, :]
    y = mxq(w, 2, "e4m3") @ mxq(pick(v).transpose(0, 2, 1), 1, "e4m3")
    y = y / 16.0
    y = y / (1.0 + np.exp(-f64(og)))
    return y

@@ -1,0 +1,210 @@
+from contextlib import ExitStack
+
+import concourse.mybir as mybir
+from concourse.masks import make_identity
+
+T, N, D, DV, NQ = 2048, 1024, 1024, 128, 256
+FLOPS = 2 * NQ * N * (D + DV)
+BYTES = 4 * D * NQ + 128 * T * 4 + 32 * T + 4 * DV * T + 2 * 4 * T + 2 * 4 * NQ * DV + 128 * 64 * 2
+
+F32 = mybir.dt.float32
+BF16 = mybir.dt.bfloat16
+I32 = mybir.dt.int32
+U32 = mybir.dt.uint32
+U16 = mybir.dt.uint16
+U8 = mybir.dt.uint8
+FP8X4 = mybir.dt.float8_e4m3fn_x4
+FP4X4 = mybir.dt.float4_e2m1fn_x4
+ACT = mybir.ActivationFunctionType
+ALU = mybir.AluOpType
+P = 128
+
+
+def tile_attend_silu_kb_gate_topkq256n1024t2048_kernel(tc, qT, k_words, k_scales, vT, vs, kb, og, offs, out):
+    nc = tc.nc
+    with ExitStack() as ctx:
+        sb = ctx.enter_context(tc.tile_pool(name="sb", bufs=1))
+        ps = ctx.enter_context(tc.psum_pool(name="ps", bufs=1))
+        aux = ctx.enter_context(tc.psum_pool(name="aux", bufs=2))
+
+        def tile(name, shape, dtype):
+            return sb.tile(shape, dtype, name=name, align_bytes=64)
+
+        offsets = sb.tile([P, N // 16], U16, name="offsets")
+        nc.sync.dma_start(offsets[:], offs)
+
+        zero = tile("zero", [P, 1], F32)
+        nc.vector.memset(zero[:], 0.0)
+        silu0 = tile("silu0", [P, 1], F32)
+        nc.scalar.activation(silu0[:], zero[:], ACT.Silu)
+
+        s_pool = tile("s_pool", [P, T], U8)
+        nc.vector.memset(s_pool[:].bitcast(I32), 0)
+        kb_pool = tile("kb_pool", [P, T], F32)
+        nc.vector.memset(kb_pool[0 : P - 1, :], 0.0)
+        nc.sync.dma_start(kb_pool[P - 1 : P, :], kb[0:1, :])
+
+        def load_q(o):
+            raw = tile(f"q_raw{o}", [P, 4, NQ], F32)
+            nc.sync.dma_start(raw[:], qT[0, 512 * o : 512 * (o + 1), :].rearrange("(p j) n -> p j n", j=4))
+            return raw
+
+        q_raw = [load_q(0)]
+        for quad in range(4):
+            nc.sync.dma_start(
+                s_pool[32 * quad : 32 * quad + 8, :].bitcast(I32),
+                k_scales[:, 4 * quad : 4 * quad + 4, :].bitcast(I32),
+            )
+        ident = tile("ident", [P, P], F32)
+        make_identity(nc, ident[:])
+        vs_pool = tile("vs_pool", [P, T], F32)
+        nc.gpsimd.memset(vs_pool[0 : P - 1, :], 0.0)
+        nc.sync.dma_start(vs_pool[P - 1 : P, :], vs[0:1, :])
+        s_second = tile("s_second", [P, N], U8)
+        nc.gpsimd.memset(s_second[:].bitcast(I32), 0)
+        q_raw.append(load_q(1))
+        og_sb = tile("og_sb", [P, 2, DV], F32)
+        nc.sync.dma_start(og_sb[:], og[0].rearrange("(h p) e -> p h e", h=2))
+        v_raw = tile("v_raw", [P, T], F32)
+        nc.sync.dma_start(v_raw[:], vT)
+        k_pool = tile("k_pool", [P, T], I32)
+        nc.sync.dma_start(k_pool[:], k_words[0].rearrange("p t b -> p (t b)").bitcast(I32))
+
+        def to_columns(name, got):
+            bank = aux.tile([P, 4, P], F32, name="aux_bank")
+            for t in range(4):
+                nc.tensor.transpose(bank[:, t, :], got[:, t : 512 : 4], ident[:])
+            cols = tile(name, [P, 4], F32)
+            nc.scalar.copy(cols[:], bank[:, :, P - 1])
+            return cols
+
+        kb_got = tile("kb_got", [P, N], F32)
+        nc.vector.tensor_copy(kb_got[:], kb_pool[:].indirect(offsets[:]))
+        kb_cols = [to_columns(f"kb_cols{g}", kb_got[:, 512 * g : 512 * (g + 1)]) for g in range(2)]
+
+        def gather_vs(g):
+            vs_got = tile(f"vs_got{g}", [P, 512], F32)
+            nc.vector.tensor_copy(vs_got[:], vs_pool[:].indirect(offsets[:, 32 * g : 32 * (g + 1)]))
+            return to_columns(f"vs_cols{g}", vs_got)
+
+        s_got = tile("s_got", [P, N], U8)
+        nc.vector.tensor_copy(s_got[:], s_pool[:].indirect(offsets[:]))
+        s_first = tile("s_first", [P, N], U8)
+        nc.vector.tensor_copy(
+            s_first[:].rearrange("p (g t m) -> p g t m", g=2, t=4),
+            s_got[:].rearrange("p (g m t) -> p g t m", g=2, t=4),
+        )
+        for quad in range(4):
+            nc.sync.dma_start(
+                s_second[32 * quad : 32 * quad + 4, :].bitcast(I32),
+                s_first[32 * quad + 4 : 32 * quad + 8, :].bitcast(I32),
+            )
+        k_planes = [s_first, s_second]
+
+        vs_cols = [gather_vs(0)]
+
+        q_bf = tile("q_bf", [P, 2, NQ, 4], BF16)
+        for o in range(2):
+            nc.scalar.copy(
+                q_bf[:, o].rearrange("p (c i) t -> p c t i", i=4),
+                q_raw[o][:].rearrange("p t (c i) -> p c t i", i=4),
+            )
+        q_codes = tile("q_codes", [P, 2 * NQ], U32)
+        q_plane = tile("q_plane", [P, 2 * NQ], U8)
+        nc.vector.quantize_mx(out=q_codes[:].bitcast(FP8X4), scales=q_plane[:], in_=q_bf[:].rearrange("p o n t -> p (o n t)"))
+
+        tanh = tile("tanh", [P, 2 * DV], F32)
+        nc.scalar.activation(tanh[:], og_sb[:].rearrange("p h e -> p (h e)"), ACT.Tanh, bias=silu0[:], scale=0.5)
+        gate = tile("gate", [P, 2 * DV], F32)
+        nc.scalar.activation(gate[:], tanh[:], ACT.Copy, bias=1.0 / 32.0, scale=1.0 / 32.0)
+
+        v_pool = tile("v_pool", [P, T], BF16)
+        nc.scalar.copy(v_pool[:], v_raw[:])
+        v_got = tile("v_got", [P, 2, 256, 2], BF16)
+        nc.scalar.activation(v_got[:].rearrange("p u s e -> p s u e"), v_pool[:].indirect(offsets[:]), ACT.Copy)
+        v_words = v_got[:].rearrange("p u s e -> p (u s e)").bitcast(F32)
+        v_bank = aux.tile([P, 4, P], F32, name="aux_bank")
+        for g in range(2):
+            for u in range(2):
+                nc.tensor.transpose(v_bank[:, 2 * g + u, :], v_words[:, 256 * u + 128 * g : 256 * u + 128 * (g + 1)], ident[:])
+        v_bf = tile("v_bf", [P, 2 * DV * 4], BF16)
+        nc.scalar.copy(
+            v_bf[:].bitcast(F32).rearrange("p (g e u) -> p g e u", g=2, u=2),
+            v_bank[:].rearrange("p (g u) e -> p g e u", g=2),
+        )
+
+        p_f32 = []
+        for g in range(2):
+            k_got = tile(f"k_got{g}", [P, 4, P], U32)
+            nc.vector.tensor_copy(
+                k_got[:].rearrange("p t m -> p m t"),
+                k_pool[:].bitcast(U32).indirect(offsets[:, 32 * g : 32 * (g + 1)]),
+            )
+            k_split = tile(f"k_split{g}", [P, 2 * 512 * 2], U8)
+            nc.vector.tensor_copy(
+                k_split[:].bitcast(U16).rearrange("p (o x) -> p o x", o=2),
+                k_got[:].rearrange("p t m -> p (t m)").bitcast(U16).rearrange("p (x o) -> p o x", o=2),
+            )
+            p_g = tile(f"p{g}", [P, 4, NQ], F32)
+            for t in range(4):
+                score = ps.tile([P, NQ], F32, name=f"score{t}")
+                for h in range(2):
+                    for o in range(2):
+                        k0 = 1024 * o + 256 * t
+                        s0 = 512 * g + 128 * t
+                        q0 = NQ * o + 128 * h
+                        nc.tensor.matmul_mx(
+                            out=score[:, 128 * h : 128 * (h + 1)],
+                            lhsT=k_split[:, k0 : k0 + 256].bitcast(FP4X4),
+                            lhsT_scale=k_planes[o][:, s0 : s0 + 128],
+                            rhs=q_codes[:, q0 : q0 + 128].bitcast(FP8X4),
+                            rhs_scale=q_plane[:, q0 : q0 + 128],
+                            start=(o == 0),
+                            stop=(o == 1),
+                        )
+                nc.scalar.activation(p_g[:, t, :], score[:], ACT.Silu, bias=kb_cols[g][:, t : t + 1])
+            p_f32.append(p_g)
+
+        vs_cols.append(gather_vs(1))
+
+        v_codes = tile("v_codes", [P, 2 * DV], U32)
+        v_plane = tile("v_plane", [P, 2 * DV], U8)
+        nc.vector.quantize_mx(out=v_codes[:].bitcast(FP8X4), scales=v_plane[:], in_=v_bf[:])
+
+        w_codes = {}
+        w_plane = {}
+        for g in range(2):
+            w_bf = {}
+            for h in range(2):
+                w_bf[h] = tile(f"w_bf{g}{h}", [P, 128, 4], BF16)
+                nc.vector.tensor_tensor(
+                    w_bf[h][:].rearrange("p (c i) t -> p c t i", i=4),
+                    p_f32[g][:, :, 128 * h : 128 * (h + 1)].rearrange("p t (c i) -> p c t i", i=4),
+                    vs_cols[g][:].unsqueeze(1).unsqueeze(3).to_broadcast([P, 32, 4, 4]),
+                    ALU.mult,
+                )
+            for h in range(2):
+                w_codes[g, h] = tile(f"w_codes{g}{h}", [P, 128], U32)
+                w_plane[g, h] = tile(f"w_plane{g}{h}", [P, 128], U8)
+                nc.vector.quantize_mx(
+                    out=w_codes[g, h][:].bitcast(FP8X4),
+                    scales=w_plane[g, h][:],
+                    in_=w_bf[h][:].rearrange("p n t -> p (n t)"),
+                )
+
+        for h in range(2):
+            y = ps.tile([P, DV], F32, name=f"y{h}")
+            for g in range(2):
+                nc.tensor.matmul_mx(
+                    out=y[:],
+                    lhsT=w_codes[g, h][:].bitcast(FP8X4),
+                    lhsT_scale=w_plane[g, h][:],
+                    rhs=v_codes[:, DV * g : DV * (g + 1)].bitcast(FP8X4),
+                    rhs_scale=v_plane[:, DV * g : DV * (g + 1)],
+                    start=(g == 0),
+                    stop=(g == 1),
+                )
+            res = tile(f"res{h}", [P, DV], F32)
+            nc.vector.tensor_tensor(res[:], y[:], gate[:, DV * h : DV * (h + 1)], ALU.mult)
+            queue = nc.sync if h == 0 else nc.scalar
+            queue.dma_start(out[0, 128 * h : 128 * (h + 1), :], res[:])

@@ -25,7 +25,6 @@ def tile_attend_silu_kb_gate_topkq256n1024t2048_kernel(tc, qT, k_words, k_scales
     with ExitStack() as ctx:
         sb = ctx.enter_context(tc.tile_pool(name="sb", bufs=1))
         ps = ctx.enter_context(tc.psum_pool(name="ps", bufs=1))
-        aux = ctx.enter_context(tc.psum_pool(name="aux", bufs=2))
 
         def tile(name, shape, dtype):
             return sb.tile(shape, dtype, name=name, align_bytes=64)
@@ -33,36 +32,33 @@ def tile_attend_silu_kb_gate_topkq256n1024t2048_kernel(tc, qT, k_words, k_scales
         offsets = sb.tile([P, N // 16], U16, name="offsets")
         nc.sync.dma_start(offsets[:], offs)
 
+        s_pool = tile("s_pool", [P, T], U8)
+        nc.vector.memset(s_pool[:].bitcast(I32), 0)
         zero = tile("zero", [P, 1], F32)
         nc.vector.memset(zero[:], 0.0)
         silu0 = tile("silu0", [P, 1], F32)
         nc.scalar.activation(silu0[:], zero[:], ACT.Silu)
 
-        s_pool = tile("s_pool", [P, T], U8)
-        nc.vector.memset(s_pool[:].bitcast(I32), 0)
         kb_pool = tile("kb_pool", [P, T], F32)
-        nc.vector.memset(kb_pool[0 : P - 1, :], 0.0)
+        nc.vector.memset(kb_pool[0 : P - 1, :].bitcast(I32), 0)
         nc.sync.dma_start(kb_pool[P - 1 : P, :], kb[0:1, :])
+        vs_pool = tile("vs_pool", [P, T], F32)
+        nc.vector.memset(vs_pool[0 : P - 1, :].bitcast(I32), 0)
+        nc.gpsimd.dma_start(vs_pool[P - 1 : P, :], vs[0:1, :])
 
-        def load_q(o):
-            raw = tile(f"q_raw{o}", [P, 4, NQ], F32)
-            nc.sync.dma_start(raw[:], qT[0, 512 * o : 512 * (o + 1), :].rearrange("(p j) n -> p j n", j=4))
-            return raw
-
-        q_raw = [load_q(0)]
+        q_raw = [tile(f"q_raw{o}", [P, 4, NQ], F32) for o in range(2)]
+        q_rows = qT[0].rearrange("(o p j) n -> o p j n", o=2, j=4)
+        nc.sync.dma_start(q_raw[0][:], q_rows[0])
         for quad in range(4):
             nc.sync.dma_start(
                 s_pool[32 * quad : 32 * quad + 8, :].bitcast(I32),
                 k_scales[:, 4 * quad : 4 * quad + 4, :].bitcast(I32),
             )
+        nc.sync.dma_start(q_raw[1][:], q_rows[1])
         ident = tile("ident", [P, P], F32)
         make_identity(nc, ident[:])
-        vs_pool = tile("vs_pool", [P, T], F32)
-        nc.gpsimd.memset(vs_pool[0 : P - 1, :], 0.0)
-        nc.sync.dma_start(vs_pool[P - 1 : P, :], vs[0:1, :])
         s_second = tile("s_second", [P, N], U8)
         nc.gpsimd.memset(s_second[:].bitcast(I32), 0)
-        q_raw.append(load_q(1))
         og_sb = tile("og_sb", [P, 2, DV], F32)
         nc.sync.dma_start(og_sb[:], og[0].rearrange("(h p) e -> p h e", h=2))
         v_raw = tile("v_raw", [P, T], F32)
@@ -70,38 +66,37 @@ def tile_attend_silu_kb_gate_topkq256n1024t2048_kernel(tc, qT, k_words, k_scales
         k_pool = tile("k_pool", [P, T], I32)
         nc.sync.dma_start(k_pool[:], k_words[0].rearrange("p t b -> p (t b)").bitcast(I32))
 
-        def to_columns(name, got):
-            bank = aux.tile([P, 4, P], F32, name="aux_bank")
+        def turn(got, bank_name):
+            bank = ps.tile([P, 4, P], F32, name=bank_name)
             for t in range(4):
                 nc.tensor.transpose(bank[:, t, :], got[:, t : 512 : 4], ident[:])
+            return bank
+
+        def last_column(name, bank):
             cols = tile(name, [P, 4], F32)
             nc.scalar.copy(cols[:], bank[:, :, P - 1])
             return cols
 
         kb_got = tile("kb_got", [P, N], F32)
         nc.vector.tensor_copy(kb_got[:], kb_pool[:].indirect(offsets[:]))
-        kb_cols = [to_columns(f"kb_cols{g}", kb_got[:, 512 * g : 512 * (g + 1)]) for g in range(2)]
+        kb_cols = [last_column(f"kb_cols{g}", turn(kb_got[:, 512 * g : 512 * (g + 1)], f"turn{g}")) for g in range(2)]
 
-        def gather_vs(g):
-            vs_got = tile(f"vs_got{g}", [P, 512], F32)
+        def gather_vs(g, name, bank_name):
+            vs_got = tile(name, [P, 512], F32)
             nc.vector.tensor_copy(vs_got[:], vs_pool[:].indirect(offsets[:, 32 * g : 32 * (g + 1)]))
-            return to_columns(f"vs_cols{g}", vs_got)
+            return turn(vs_got, bank_name)
 
-        s_got = tile("s_got", [P, N], U8)
+        s_got = tile("kb_pool", [P, N], U8)
         nc.vector.tensor_copy(s_got[:], s_pool[:].indirect(offsets[:]))
         s_first = tile("s_first", [P, N], U8)
         nc.vector.tensor_copy(
             s_first[:].rearrange("p (g t m) -> p g t m", g=2, t=4),
             s_got[:].rearrange("p (g m t) -> p g t m", g=2, t=4),
         )
-        for quad in range(4):
-            nc.sync.dma_start(
-                s_second[32 * quad : 32 * quad + 4, :].bitcast(I32),
-                s_first[32 * quad + 4 : 32 * quad + 8, :].bitcast(I32),
-            )
+        nc.sync.dma_start(s_second[0:112, :].bitcast(I32), s_first[4:116, :].bitcast(I32))
         k_planes = [s_first, s_second]
 
-        vs_cols = [gather_vs(0)]
+        vs_bank = gather_vs(0, "s_pool", "turn0")
 
         q_bf = tile("q_bf", [P, 2, NQ, 4], BF16)
         for o in range(2):
@@ -109,33 +104,24 @@ def tile_attend_silu_kb_gate_topkq256n1024t2048_kernel(tc, qT, k_words, k_scales
                 q_bf[:, o].rearrange("p (c i) t -> p c t i", i=4),
                 q_raw[o][:].rearrange("p t (c i) -> p c t i", i=4),
             )
-        q_codes = tile("q_codes", [P, 2 * NQ], U32)
+        q_codes = tile("kb_pool", [P, 2 * NQ], U32)
         q_plane = tile("q_plane", [P, 2 * NQ], U8)
         nc.vector.quantize_mx(out=q_codes[:].bitcast(FP8X4), scales=q_plane[:], in_=q_bf[:].rearrange("p o n t -> p (o n t)"))
 
         tanh = tile("tanh", [P, 2 * DV], F32)
         nc.scalar.activation(tanh[:], og_sb[:].rearrange("p h e -> p (h e)"), ACT.Tanh, bias=silu0[:], scale=0.5)
         gate = tile("gate", [P, 2 * DV], F32)
-        nc.scalar.activation(gate[:], tanh[:], ACT.Copy, bias=1.0 / 32.0, scale=1.0 / 32.0)
+        nc.gpsimd.tensor_scalar(gate[:], tanh[:], 1.0 / 32.0, 1.0 / 32.0, ALU.mult, ALU.add)
 
         v_pool = tile("v_pool", [P, T], BF16)
         nc.scalar.copy(v_pool[:], v_raw[:])
         v_got = tile("v_got", [P, 2, 256, 2], BF16)
         nc.scalar.activation(v_got[:].rearrange("p u s e -> p s u e"), v_pool[:].indirect(offsets[:]), ACT.Copy)
-        v_words = v_got[:].rearrange("p u s e -> p (u s e)").bitcast(F32)
-        v_bank = aux.tile([P, 4, P], F32, name="aux_bank")
-        for g in range(2):
-            for u in range(2):
-                nc.tensor.transpose(v_bank[:, 2 * g + u, :], v_words[:, 256 * u + 128 * g : 256 * u + 128 * (g + 1)], ident[:])
-        v_bf = tile("v_bf", [P, 2 * DV * 4], BF16)
-        nc.scalar.copy(
-            v_bf[:].bitcast(F32).rearrange("p (g e u) -> p g e u", g=2, u=2),
-            v_bank[:].rearrange("p (g u) e -> p g e u", g=2),
-        )
+        vs_cols = [last_column("vs_cols0", vs_bank)]
 
         p_f32 = []
         for g in range(2):
-            k_got = tile(f"k_got{g}", [P, 4, P], U32)
+            k_got = tile("q_bf", [P, 4, P], U32)
             nc.vector.tensor_copy(
                 k_got[:].rearrange("p t m -> p m t"),
                 k_pool[:].bitcast(U32).indirect(offsets[:, 32 * g : 32 * (g + 1)]),
@@ -165,7 +151,19 @@ def tile_attend_silu_kb_gate_topkq256n1024t2048_kernel(tc, qT, k_words, k_scales
                 nc.scalar.activation(p_g[:, t, :], score[:], ACT.Silu, bias=kb_cols[g][:, t : t + 1])
             p_f32.append(p_g)
 
-        vs_cols.append(gather_vs(1))
+        vs_cols.append(last_column("vs_cols1", gather_vs(1, "q_bf", "score1")))
+
+        v_words = v_got[:].rearrange("p u s e -> p (u s e)").bitcast(F32)
+        v_bank = ps.tile([P, 4, P], F32, name="score2")
+        for g in range(2):
+            for u in range(2):
+                nc.tensor.transpose(v_bank[:, 2 * g + u, :], v_words[:, 256 * u + 128 * g : 256 * u + 128 * (g + 1)], ident[:])
+        v_bf = tile("v_bf", [P, 2 * DV * 4], BF16)
+        nc.scalar.copy(
+            v_bf[:].bitcast(F32).rearrange("p (g e u) -> p g e u", g=2, u=2),
+            v_bank[:].rearrange("p (g u) e -> p g e u", g=2),
+        )
+
 
         v_codes = tile("v_codes", [P, 2 * DV], U32)
         v_plane = tile("v_plane", [P, 2 * DV], U8)

@@ -44,7 +44,6 @@ def tile_attend_silu_kb_gate_topkq256n1024t2048_kernel(tc, qT, k_words, k_scales
         nc.sync.dma_start(kb_pool[P - 1 : P, :], kb[0:1, :])
         vs_pool = tile("vs_pool", [P, T], F32)
         nc.vector.memset(vs_pool[0 : P - 1, :].bitcast(I32), 0)
-        nc.gpsimd.dma_start(vs_pool[P - 1 : P, :], vs[0:1, :])
 
         q_raw = [tile(f"q_raw{o}", [P, 4, NQ], F32) for o in range(2)]
         q_rows = qT[0].rearrange("(o p j) n -> o p j n", o=2, j=4)
@@ -56,57 +55,67 @@ def tile_attend_silu_kb_gate_topkq256n1024t2048_kernel(tc, qT, k_words, k_scales
             )
         nc.sync.dma_start(q_raw[1][:], q_rows[1])
         ident = tile("ident", [P, P], F32)
-        make_identity(nc, ident[:])
+        nc.vector.memset(ident[:], 0.0)
+        make_identity(nc, ident[:], nomemset=True)
+        ident_bf = tile("ident_bf", [P, P], BF16)
+        nc.gpsimd.tensor_copy(ident_bf[:], ident[:])
         s_second = tile("s_second", [P, N], U8)
-        nc.gpsimd.memset(s_second[:].bitcast(I32), 0)
+        nc.vector.memset(s_second[:].bitcast(I32), 0)
         og_sb = tile("og_sb", [P, 2, DV], F32)
         nc.sync.dma_start(og_sb[:], og[0].rearrange("(h p) e -> p h e", h=2))
         v_raw = tile("v_raw", [P, T], F32)
         nc.sync.dma_start(v_raw[:], vT)
+        nc.sync.dma_start(vs_pool[P - 1 : P, :], vs[0:1, :])
         k_pool = tile("k_pool", [P, T], I32)
         nc.sync.dma_start(k_pool[:], k_words[0].rearrange("p t b -> p (t b)").bitcast(I32))
 
         def turn(got, bank_name):
             bank = ps.tile([P, 4, P], F32, name=bank_name)
             for t in range(4):
-                nc.tensor.transpose(bank[:, t, :], got[:, t : 512 : 4], ident[:])
+                nc.tensor.transpose(bank[:, t, :], got[:, P * t : P * (t + 1)], ident[:])
             return bank
 
-        def last_column(name, bank):
-            cols = tile(name, [P, 4], F32)
-            nc.scalar.copy(cols[:], bank[:, :, P - 1])
+        def last_column(cols, bank):
+            nc.scalar.copy(cols, bank[:, :, P - 1])
             return cols
 
         kb_got = tile("kb_got", [P, N], F32)
-        nc.vector.tensor_copy(kb_got[:], kb_pool[:].indirect(offsets[:]))
-        kb_cols = [last_column(f"kb_cols{g}", turn(kb_got[:, 512 * g : 512 * (g + 1)], f"turn{g}")) for g in range(2)]
+        nc.vector.tensor_copy(
+            kb_got[:].bitcast(U32).rearrange("p (g t b r) -> p g b t r", g=2, t=4, r=8),
+            kb_pool[:].bitcast(U32).indirect(offsets[:]),
+        )
+        kb_banks = [turn(kb_got[:, 512 * g : 512 * (g + 1)], f"turn{g}") for g in range(2)]
 
         def gather_vs(g, name, bank_name):
             vs_got = tile(name, [P, 512], F32)
-            nc.vector.tensor_copy(vs_got[:], vs_pool[:].indirect(offsets[:, 32 * g : 32 * (g + 1)]))
+            nc.vector.tensor_copy(
+                vs_got[:].bitcast(U32).rearrange("p (t b r) -> p b t r", t=4, r=8),
+                vs_pool[:].bitcast(U32).indirect(offsets[:, 32 * g : 32 * (g + 1)]),
+            )
             return turn(vs_got, bank_name)
 
-        s_got = tile("kb_pool", [P, N], U8)
+        s_got = tile("s_got", [P, N], U8)
         nc.vector.tensor_copy(s_got[:], s_pool[:].indirect(offsets[:]))
         s_first = tile("s_first", [P, N], U8)
         nc.vector.tensor_copy(
-            s_first[:].rearrange("p (g t m) -> p g t m", g=2, t=4),
-            s_got[:].rearrange("p (g m t) -> p g t m", g=2, t=4),
+            s_first[:].bitcast(I32).rearrange("p (g t b w) -> p g t b w", g=2, t=4, w=2),
+            s_got[:].bitcast(I32).rearrange("p (g b t w) -> p g t b w", g=2, t=4, w=2),
         )
         nc.sync.dma_start(s_second[0:112, :].bitcast(I32), s_first[4:116, :].bitcast(I32))
         k_planes = [s_first, s_second]
 
-        vs_bank = gather_vs(0, "s_pool", "turn0")
 
         q_bf = tile("q_bf", [P, 2, NQ, 4], BF16)
         for o in range(2):
             nc.scalar.copy(
-                q_bf[:, o].rearrange("p (c i) t -> p c t i", i=4),
-                q_raw[o][:].rearrange("p t (c i) -> p c t i", i=4),
+                q_bf[:, o].rearrange("p (c i) t -> p c t i", i=2),
+                q_raw[o][:].rearrange("p t (c i) -> p c t i", i=2),
             )
         q_codes = tile("kb_pool", [P, 2 * NQ], U32)
         q_plane = tile("q_plane", [P, 2 * NQ], U8)
         nc.vector.quantize_mx(out=q_codes[:].bitcast(FP8X4), scales=q_plane[:], in_=q_bf[:].rearrange("p o n t -> p (o n t)"))
+
+        vs_bank = gather_vs(0, "q_bf", "y0")
 
         tanh = tile("tanh", [P, 2 * DV], F32)
         nc.scalar.activation(tanh[:], og_sb[:].rearrange("p h e -> p (h e)"), ACT.Tanh, bias=silu0[:], scale=0.5)
@@ -115,22 +124,27 @@ def tile_attend_silu_kb_gate_topkq256n1024t2048_kernel(tc, qT, k_words, k_scales
 
         v_pool = tile("v_pool", [P, T], BF16)
         nc.scalar.copy(v_pool[:], v_raw[:])
-        v_got = tile("v_got", [P, 2, 256, 2], BF16)
-        nc.scalar.activation(v_got[:].rearrange("p u s e -> p s u e"), v_pool[:].indirect(offsets[:]), ACT.Copy)
-        vs_cols = [last_column("vs_cols0", vs_bank)]
+        v_got = tile("v_got", [P, 4, 256], BF16)
+        nc.scalar.activation(v_got[:].rearrange("p t (b r) -> p b t r", r=8), v_pool[:].indirect(offsets[:]), ACT.Copy)
+        columns = tile("v_raw", [P, 4, 4], F32)
+        kb_cols = [last_column(columns[:, g, :], kb_banks[g]) for g in range(2)]
+        vs_cols = [last_column(columns[:, 2, :], vs_bank)]
 
         p_f32 = []
         for g in range(2):
-            k_got = tile("q_bf", [P, 4, P], U32)
-            nc.vector.tensor_copy(
-                k_got[:].rearrange("p t m -> p m t"),
-                k_pool[:].bitcast(U32).indirect(offsets[:, 32 * g : 32 * (g + 1)]),
-            )
+            k_got = [tile(name, [P, 4, 64], U32) for name in ("s_got", "s_pool")]
+            for half in range(2):
+                c0 = 32 * g + 16 * half
+                nc.vector.tensor_copy(
+                    k_got[half][:].rearrange("p t (b r) -> p b t r", r=8),
+                    k_pool[:].bitcast(U32).indirect(offsets[:, c0 : c0 + 16]),
+                )
             k_split = tile(f"k_split{g}", [P, 2 * 512 * 2], U8)
-            nc.vector.tensor_copy(
-                k_split[:].bitcast(U16).rearrange("p (o x) -> p o x", o=2),
-                k_got[:].rearrange("p t m -> p (t m)").bitcast(U16).rearrange("p (x o) -> p o x", o=2),
-            )
+            for half in range(2):
+                nc.vector.tensor_copy(
+                    k_split[:].bitcast(U16).rearrange("p (o t m) -> p o t m", o=2, t=4)[:, :, :, 64 * half : 64 * (half + 1)],
+                    k_got[half][:].rearrange("p t m -> p (t m)").bitcast(U16).rearrange("p (t m o) -> p o t m", o=2, t=4),
+                )
             p_g = tile(f"p{g}", [P, 4, NQ], F32)
             for t in range(4):
                 score = ps.tile([P, NQ], F32, name=f"score{t}")
@@ -151,19 +165,17 @@ def tile_attend_silu_kb_gate_topkq256n1024t2048_kernel(tc, qT, k_words, k_scales
                 nc.scalar.activation(p_g[:, t, :], score[:], ACT.Silu, bias=kb_cols[g][:, t : t + 1])
             p_f32.append(p_g)
 
-        vs_cols.append(last_column("vs_cols1", gather_vs(1, "q_bf", "score1")))
+        vs_cols.append(last_column(columns[:, 3, :], gather_vs(1, "s_got", "score1")))
 
-        v_words = v_got[:].rearrange("p u s e -> p (u s e)").bitcast(F32)
-        v_bank = ps.tile([P, 4, P], F32, name="score2")
+        v_bank = ps.tile([P, 2, 4, P], BF16, name="score0")
         for g in range(2):
-            for u in range(2):
-                nc.tensor.transpose(v_bank[:, 2 * g + u, :], v_words[:, 256 * u + 128 * g : 256 * u + 128 * (g + 1)], ident[:])
+            for t in range(4):
+                nc.tensor.transpose(v_bank[:, g, t, :], v_got[:, t, P * g : P * (g + 1)], ident_bf[:])
         v_bf = tile("v_bf", [P, 2 * DV * 4], BF16)
         nc.scalar.copy(
-            v_bf[:].bitcast(F32).rearrange("p (g e u) -> p g e u", g=2, u=2),
-            v_bank[:].rearrange("p (g u) e -> p g e u", g=2),
+            v_bf[:].rearrange("p (g e t) -> p g e t", g=2, t=4),
+            v_bank[:].rearrange("p g t e -> p g e t"),
         )
-
 
         v_codes = tile("v_codes", [P, 2 * DV], U32)
         v_plane = tile("v_plane", [P, 2 * DV], U8)
@@ -176,9 +188,9 @@ def tile_attend_silu_kb_gate_topkq256n1024t2048_kernel(tc, qT, k_words, k_scales
             for h in range(2):
                 w_bf[h] = tile(f"w_bf{g}{h}", [P, 128, 4], BF16)
                 nc.vector.tensor_tensor(
-                    w_bf[h][:].rearrange("p (c i) t -> p c t i", i=4),
-                    p_f32[g][:, :, 128 * h : 128 * (h + 1)].rearrange("p t (c i) -> p c t i", i=4),
-                    vs_cols[g][:].unsqueeze(1).unsqueeze(3).to_broadcast([P, 32, 4, 4]),
+                    w_bf[h][:].rearrange("p (c i) t -> p c t i", i=2),
+                    p_f32[g][:, :, 128 * h : 128 * (h + 1)].rearrange("p t (c i) -> p c t i", i=2),
+                    vs_cols[g].unsqueeze(1).unsqueeze(3).to_broadcast([P, 64, 4, 2]),
                     ALU.mult,
                 )
             for h in range(2):

@@ -32,22 +32,24 @@ def tile_attend_silu_kb_gate_topkq256n1024t2048_kernel(tc, qT, k_words, k_scales
         offsets = sb.tile([P, N // 16], U16, name="offsets")
         nc.sync.dma_start(offsets[:], offs)
 
+        q_raw = [tile(f"q_raw{o}", [P, 4, NQ], F32) for o in range(2)]
+        q_rows = qT[0].rearrange("(o p j) n -> o p j n", o=2, j=4)
+
         s_pool = tile("s_pool", [P, T], U8)
-        nc.vector.memset(s_pool[:].bitcast(I32), 0)
+        nc.gpsimd.memset(s_pool[:].bitcast(I32), 0)
         zero = tile("zero", [P, 1], F32)
         nc.vector.memset(zero[:], 0.0)
         silu0 = tile("silu0", [P, 1], F32)
         nc.scalar.activation(silu0[:], zero[:], ACT.Silu)
 
         kb_pool = tile("kb_pool", [P, T], F32)
-        nc.vector.memset(kb_pool[0 : P - 1, :].bitcast(I32), 0)
+        nc.vector.memset(kb_pool[0 : P - 1, 0:1280].bitcast(I32), 0)
+        nc.gpsimd.memset(kb_pool[0 : P - 1, 1280:T].bitcast(I32), 0)
         nc.sync.dma_start(kb_pool[P - 1 : P, :], kb[0:1, :])
-        vs_pool = tile("vs_pool", [P, T], F32)
-        nc.vector.memset(vs_pool[0 : P - 1, :].bitcast(I32), 0)
-
-        q_raw = [tile(f"q_raw{o}", [P, 4, NQ], F32) for o in range(2)]
-        q_rows = qT[0].rearrange("(o p j) n -> o p j n", o=2, j=4)
         nc.sync.dma_start(q_raw[0][:], q_rows[0])
+        vs_pool = tile("vs_pool", [P, T], F32)
+        nc.gpsimd.memset(vs_pool[0 : P - 1, :].bitcast(I32), 0)
+
         for quad in range(4):
             nc.sync.dma_start(
                 s_pool[32 * quad : 32 * quad + 8, :].bitcast(I32),
@@ -55,19 +57,19 @@ def tile_attend_silu_kb_gate_topkq256n1024t2048_kernel(tc, qT, k_words, k_scales
             )
         nc.sync.dma_start(q_raw[1][:], q_rows[1])
         ident = tile("ident", [P, P], F32)
-        nc.vector.memset(ident[:], 0.0)
-        make_identity(nc, ident[:], nomemset=True)
+        make_identity(nc, ident[:])
         ident_bf = tile("ident_bf", [P, P], BF16)
         nc.gpsimd.tensor_copy(ident_bf[:], ident[:])
         s_second = tile("s_second", [P, N], U8)
-        nc.vector.memset(s_second[:].bitcast(I32), 0)
-        og_sb = tile("og_sb", [P, 2, DV], F32)
-        nc.sync.dma_start(og_sb[:], og[0].rearrange("(h p) e -> p h e", h=2))
-        v_raw = tile("v_raw", [P, T], F32)
-        nc.sync.dma_start(v_raw[:], vT)
+        nc.gpsimd.memset(s_second[:].bitcast(I32), 0)
+        v_raw = [tile(f"v_raw{half}", [P, T // 2], F32) for half in range(2)]
+        nc.sync.dma_start(v_raw[0][:], vT[:, 0 : T // 2])
         nc.sync.dma_start(vs_pool[P - 1 : P, :], vs[0:1, :])
+        nc.sync.dma_start(v_raw[1][:], vT[:, T // 2 : T])
         k_pool = tile("k_pool", [P, T], I32)
         nc.sync.dma_start(k_pool[:], k_words[0].rearrange("p t b -> p (t b)").bitcast(I32))
+        og_sb = tile("og_sb", [P, 2, DV], F32)
+        nc.sync.dma_start(og_sb[:], og[0].rearrange("(h p) e -> p h e", h=2))
 
         def turn(got, bank_name):
             bank = ps.tile([P, 4, P], F32, name=bank_name)
@@ -115,24 +117,35 @@ def tile_attend_silu_kb_gate_topkq256n1024t2048_kernel(tc, qT, k_words, k_scales
         q_plane = tile("q_plane", [P, 2 * NQ], U8)
         nc.vector.quantize_mx(out=q_codes[:].bitcast(FP8X4), scales=q_plane[:], in_=q_bf[:].rearrange("p o n t -> p (o n t)"))
 
-        vs_bank = gather_vs(0, "q_bf", "y0")
+        vs_bank = gather_vs(0, "s_got", "y0")
+
+        v_pool = tile("v_pool", [P, T], BF16)
+        for half in range(2):
+            nc.scalar.copy(v_pool[:, T // 2 * half : T // 2 * (half + 1)], v_raw[half][:])
+        v_got = tile("v_got", [P, 4, 256], BF16)
+        nc.scalar.activation(v_got[:].rearrange("p t (b r) -> p b t r", r=8), v_pool[:].indirect(offsets[:]), ACT.Copy)
+        columns = tile("v_raw1", [P, 4, 4], F32)
+        kb_cols = [last_column(columns[:, g, :], kb_banks[g]) for g in range(2)]
+        vs_cols = [last_column(columns[:, 2, :], vs_bank)]
 
         tanh = tile("tanh", [P, 2 * DV], F32)
         nc.scalar.activation(tanh[:], og_sb[:].rearrange("p h e -> p (h e)"), ACT.Tanh, bias=silu0[:], scale=0.5)
         gate = tile("gate", [P, 2 * DV], F32)
         nc.gpsimd.tensor_scalar(gate[:], tanh[:], 1.0 / 32.0, 1.0 / 32.0, ALU.mult, ALU.add)
 
-        v_pool = tile("v_pool", [P, T], BF16)
-        nc.scalar.copy(v_pool[:], v_raw[:])
-        v_got = tile("v_got", [P, 4, 256], BF16)
-        nc.scalar.activation(v_got[:].rearrange("p t (b r) -> p b t r", r=8), v_pool[:].indirect(offsets[:]), ACT.Copy)
-        columns = tile("v_raw", [P, 4, 4], F32)
-        kb_cols = [last_column(columns[:, g, :], kb_banks[g]) for g in range(2)]
-        vs_cols = [last_column(columns[:, 2, :], vs_bank)]
+        v_bank = ps.tile([P, 2, 4, P], BF16, name="y1")
+        for g in range(2):
+            for t in range(4):
+                nc.tensor.transpose(v_bank[:, g, t, :], v_got[:, t, P * g : P * (g + 1)], ident_bf[:])
+        v_bf = tile("v_bf", [P, 2 * DV * 4], BF16)
+        nc.scalar.copy(
+            v_bf[:].rearrange("p (g e t) -> p g e t", g=2, t=4),
+            v_bank[:].rearrange("p g t e -> p g e t"),
+        )
 
         p_f32 = []
         for g in range(2):
-            k_got = [tile(name, [P, 4, 64], U32) for name in ("s_got", "s_pool")]
+            k_got = [tile(name, [P, 4, 64], U32) for name in ("q_bf", "s_pool")]
             for half in range(2):
                 c0 = 32 * g + 16 * half
                 nc.vector.tensor_copy(
@@ -165,17 +178,7 @@ def tile_attend_silu_kb_gate_topkq256n1024t2048_kernel(tc, qT, k_words, k_scales
                 nc.scalar.activation(p_g[:, t, :], score[:], ACT.Silu, bias=kb_cols[g][:, t : t + 1])
             p_f32.append(p_g)
 
-        vs_cols.append(last_column(columns[:, 3, :], gather_vs(1, "s_got", "score1")))
-
-        v_bank = ps.tile([P, 2, 4, P], BF16, name="score0")
-        for g in range(2):
-            for t in range(4):
-                nc.tensor.transpose(v_bank[:, g, t, :], v_got[:, t, P * g : P * (g + 1)], ident_bf[:])
-        v_bf = tile("v_bf", [P, 2 * DV * 4], BF16)
-        nc.scalar.copy(
-            v_bf[:].rearrange("p (g e t) -> p g e t", g=2, t=4),
-            v_bank[:].rearrange("p g t e -> p g e t"),
-        )
+        vs_cols.append(last_column(columns[:, 3, :], gather_vs(1, "q_bf", "score1")))
 
         v_codes = tile("v_codes", [P, 2 * DV], U32)
         v_plane = tile("v_plane", [P, 2 * DV], U8)

@@ -43,25 +43,19 @@ def tile_attend_silu_kb_gate_topkq256n1024t2048_kernel(tc, qT, k_words, k_scales
         nc.scalar.activation(silu0[:], zero[:], ACT.Silu)
 
         kb_pool = tile("kb_pool", [P, T], F32)
-        nc.vector.memset(kb_pool[0 : P - 1, 0:1280].bitcast(I32), 0)
-        nc.gpsimd.memset(kb_pool[0 : P - 1, 1280:T].bitcast(I32), 0)
+        nc.vector.memset(kb_pool[0 : P - 1, :].bitcast(I32), 0)
         nc.sync.dma_start(kb_pool[P - 1 : P, :], kb[0:1, :])
         nc.sync.dma_start(q_raw[0][:], q_rows[0])
         vs_pool = tile("vs_pool", [P, T], F32)
-        nc.gpsimd.memset(vs_pool[0 : P - 1, :].bitcast(I32), 0)
+        nc.vector.memset(vs_pool[0 : P - 1, 0:512].bitcast(I32), 0)
+        nc.gpsimd.memset(vs_pool[0 : P - 1, 512:T].bitcast(I32), 0)
 
-        for quad in range(4):
-            nc.sync.dma_start(
-                s_pool[32 * quad : 32 * quad + 8, :].bitcast(I32),
-                k_scales[:, 4 * quad : 4 * quad + 4, :].bitcast(I32),
-            )
+        nc.sync.dma_start(s_pool[0:32, :].bitcast(I32), k_scales.rearrange("o f t -> f o t").bitcast(I32))
         nc.sync.dma_start(q_raw[1][:], q_rows[1])
         ident = tile("ident", [P, P], F32)
         make_identity(nc, ident[:])
         ident_bf = tile("ident_bf", [P, P], BF16)
-        nc.gpsimd.tensor_copy(ident_bf[:], ident[:])
-        s_second = tile("s_second", [P, N], U8)
-        nc.gpsimd.memset(s_second[:].bitcast(I32), 0)
+        nc.scalar.copy(ident_bf[:], ident[:])
         v_raw = [tile(f"v_raw{half}", [P, T // 2], F32) for half in range(2)]
         nc.sync.dma_start(v_raw[0][:], vT[:, 0 : T // 2])
         nc.sync.dma_start(vs_pool[P - 1 : P, :], vs[0:1, :])
@@ -103,15 +97,19 @@ def tile_attend_silu_kb_gate_topkq256n1024t2048_kernel(tc, qT, k_words, k_scales
             s_first[:].bitcast(I32).rearrange("p (g t b w) -> p g t b w", g=2, t=4, w=2),
             s_got[:].bitcast(I32).rearrange("p (g b t w) -> p g t b w", g=2, t=4, w=2),
         )
-        nc.sync.dma_start(s_second[0:112, :].bitcast(I32), s_first[4:116, :].bitcast(I32))
-        k_planes = [s_first, s_second]
+        k_planes = tile("k_planes", [P, 2, N], U8)
+        for quad in range(4):
+            nc.sync.dma_start(
+                k_planes[32 * quad : 32 * (quad + 1)].bitcast(I32),
+                s_first[8 * quad : 8 * quad + 64, :].bitcast(I32),
+            )
 
 
         q_bf = tile("q_bf", [P, 2, NQ, 4], BF16)
         for o in range(2):
             nc.scalar.copy(
-                q_bf[:, o].rearrange("p (c i) t -> p c t i", i=2),
-                q_raw[o][:].rearrange("p t (c i) -> p c t i", i=2),
+                q_bf[:, o].rearrange("p (c i) t -> p c t i", i=4),
+                q_raw[o][:].rearrange("p t (c i) -> p c t i", i=4),
             )
         q_codes = tile("kb_pool", [P, 2 * NQ], U32)
         q_plane = tile("q_plane", [P, 2 * NQ], U8)
@@ -131,7 +129,7 @@ def tile_attend_silu_kb_gate_topkq256n1024t2048_kernel(tc, qT, k_words, k_scales
         tanh = tile("tanh", [P, 2 * DV], F32)
         nc.scalar.activation(tanh[:], og_sb[:].rearrange("p h e -> p (h e)"), ACT.Tanh, bias=silu0[:], scale=0.5)
         gate = tile("gate", [P, 2 * DV], F32)
-        nc.gpsimd.tensor_scalar(gate[:], tanh[:], 1.0 / 32.0, 1.0 / 32.0, ALU.mult, ALU.add)
+        nc.scalar.activation(gate[:], tanh[:], ACT.Copy, bias=1.0 / 32.0, scale=1.0 / 32.0)
 
         v_bank = ps.tile([P, 2, 4, P], BF16, name="y1")
         for g in range(2):
@@ -169,7 +167,7 @@ def tile_attend_silu_kb_gate_topkq256n1024t2048_kernel(tc, qT, k_words, k_scales
                         nc.tensor.matmul_mx(
                             out=score[:, 128 * h : 128 * (h + 1)],
                             lhsT=k_split[:, k0 : k0 + 256].bitcast(FP4X4),
-                            lhsT_scale=k_planes[o][:, s0 : s0 + 128],
+                            lhsT_scale=k_planes[:, o, s0 : s0 + 128],
                             rhs=q_codes[:, q0 : q0 + 128].bitcast(FP8X4),
                             rhs_scale=q_plane[:, q0 : q0 + 128],
                             start=(o == 0),
@@ -191,9 +189,9 @@ def tile_attend_silu_kb_gate_topkq256n1024t2048_kernel(tc, qT, k_words, k_scales
             for h in range(2):
                 w_bf[h] = tile(f"w_bf{g}{h}", [P, 128, 4], BF16)
                 nc.vector.tensor_tensor(
-                    w_bf[h][:].rearrange("p (c i) t -> p c t i", i=2),
-                    p_f32[g][:, :, 128 * h : 128 * (h + 1)].rearrange("p t (c i) -> p c t i", i=2),
-                    vs_cols[g].unsqueeze(1).unsqueeze(3).to_broadcast([P, 64, 4, 2]),
+                    w_bf[h][:].rearrange("p (c i) t -> p c t i", i=4),
+                    p_f32[g][:, :, 128 * h : 128 * (h + 1)].rearrange("p t (c i) -> p c t i", i=4),
+                    vs_cols[g].unsqueeze(1).unsqueeze(3).to_broadcast([P, 32, 4, 4]),
                     ALU.mult,
                 )
             for h in range(2):

@@ -143,18 +143,18 @@ def tile_attend_silu_kb_gate_topkq256n1024t2048_kernel(tc, qT, k_words, k_scales
 
         p_f32 = []
         for g in range(2):
-            k_got = [tile(name, [P, 4, 64], U32) for name in ("q_bf", "s_pool")]
+            k_got = [tile(name, [P, 256], U32) for name in ("q_bf", "s_pool")]
             for half in range(2):
                 c0 = 32 * g + 16 * half
                 nc.vector.tensor_copy(
-                    k_got[half][:].rearrange("p t (b r) -> p b t r", r=8),
+                    k_got[half][:],
                     k_pool[:].bitcast(U32).indirect(offsets[:, c0 : c0 + 16]),
                 )
             k_split = tile(f"k_split{g}", [P, 2 * 512 * 2], U8)
             for half in range(2):
                 nc.vector.tensor_copy(
-                    k_split[:].bitcast(U16).rearrange("p (o t m) -> p o t m", o=2, t=4)[:, :, :, 64 * half : 64 * (half + 1)],
-                    k_got[half][:].rearrange("p t m -> p (t m)").bitcast(U16).rearrange("p (t m o) -> p o t m", o=2, t=4),
+                    k_split[:].bitcast(U16).rearrange("p (o t b r) -> p o t b r", o=2, t=4, r=8)[:, :, :, 8 * half : 8 * (half + 1), :],
+                    k_got[half][:].bitcast(U16).rearrange("p (b t r o) -> p o t b r", o=2, t=4, r=8),
                 )
             p_g = tile(f"p{g}", [P, 4, NQ], F32)
             for t in range(4):

@@ -46,14 +46,12 @@ def tile_attend_silu_kb_gate_topkq256n1024t2048_kernel(tc, qT, k_words, k_scales
         nc.vector.memset(kb_pool[0 : P - 1, :].bitcast(I32), 0)
         nc.sync.dma_start(kb_pool[P - 1 : P, :], kb[0:1, :])
         nc.sync.dma_start(q_raw[0][:], q_rows[0])
-        vs_pool = tile("vs_pool", [P, T], F32)
-        nc.vector.memset(vs_pool[0 : P - 1, 0:512].bitcast(I32), 0)
-        nc.gpsimd.memset(vs_pool[0 : P - 1, 512:T].bitcast(I32), 0)
-
         nc.sync.dma_start(s_pool[0:32, :].bitcast(I32), k_scales.rearrange("o f t -> f o t").bitcast(I32))
         nc.sync.dma_start(q_raw[1][:], q_rows[1])
         ident = tile("ident", [P, P], F32)
         make_identity(nc, ident[:])
+        vs_pool = tile("zero", [P, T], F32)
+        nc.gpsimd.memset(vs_pool[0 : P - 1, :].bitcast(I32), 0)
         ident_bf = tile("ident_bf", [P, P], BF16)
         nc.scalar.copy(ident_bf[:], ident[:])
         v_raw = [tile(f"v_raw{half}", [P, T // 2], F32) for half in range(2)]

@@ -113,31 +113,27 @@ def tile_attend_silu_kb_gate_topkq256n1024t2048_kernel(tc, qT, k_words, k_scales
         q_plane = tile("q_plane", [P, 2 * NQ], U8)
         nc.vector.quantize_mx(out=q_codes[:].bitcast(FP8X4), scales=q_plane[:], in_=q_bf[:].rearrange("p o n t -> p (o n t)"))
 
-        vs_bank = gather_vs(0, "s_got", "y0")
+        vs_banks = [gather_vs(0, "s_got", "y0")]
 
         v_pool = tile("v_pool", [P, T], BF16)
         for half in range(2):
             nc.scalar.copy(v_pool[:, T // 2 * half : T // 2 * (half + 1)], v_raw[half][:])
-        v_got = tile("v_got", [P, 4, 256], BF16)
-        nc.scalar.activation(v_got[:].rearrange("p t (b r) -> p b t r", r=8), v_pool[:].indirect(offsets[:]), ACT.Copy)
-        columns = tile("v_raw1", [P, 4, 4], F32)
-        kb_cols = [last_column(columns[:, g, :], kb_banks[g]) for g in range(2)]
-        vs_cols = [last_column(columns[:, 2, :], vs_bank)]
-
-        tanh = tile("tanh", [P, 2 * DV], F32)
-        nc.scalar.activation(tanh[:], og_sb[:].rearrange("p h e -> p (h e)"), ACT.Tanh, bias=silu0[:], scale=0.5)
-        gate = tile("gate", [P, 2 * DV], F32)
-        nc.scalar.activation(gate[:], tanh[:], ACT.Copy, bias=1.0 / 32.0, scale=1.0 / 32.0)
-
-        v_bank = ps.tile([P, 2, 4, P], BF16, name="y1")
+        v_got = [tile(f"v_got{g}", [P, 4, P], BF16) for g in range(2)]
         for g in range(2):
+            nc.scalar.activation(
+                v_got[g][:].rearrange("p t (b r) -> p b t r", r=8),
+                v_pool[:].indirect(offsets[:, 32 * g : 32 * (g + 1)]),
+                ACT.Copy,
+            )
+        columns = tile("v_raw1", [P, 2, 4], F32)
+        kb_cols = [last_column(columns[:, g, :], kb_banks[g]) for g in range(2)]
+
+        v_bf = tile("v_bf", [P, 2, DV, 4], BF16)
+        for g in range(2):
+            v_bank = ps.tile([P, 4, P], BF16, name=("y1", "score3")[g])
             for t in range(4):
-                nc.tensor.transpose(v_bank[:, g, t, :], v_got[:, t, P * g : P * (g + 1)], ident_bf[:])
-        v_bf = tile("v_bf", [P, 2 * DV * 4], BF16)
-        nc.scalar.copy(
-            v_bf[:].rearrange("p (g e t) -> p g e t", g=2, t=4),
-            v_bank[:].rearrange("p g t e -> p g e t"),
-        )
+                nc.tensor.transpose(v_bank[:, t, :], v_got[g][:, t, :], ident_bf[:])
+            nc.scalar.copy(v_bf[:, g], v_bank[:].rearrange("p t e -> p e t"))
 
         p_f32 = []
         for g in range(2):
@@ -174,11 +170,11 @@ def tile_attend_silu_kb_gate_topkq256n1024t2048_kernel(tc, qT, k_words, k_scales
                 nc.scalar.activation(p_g[:, t, :], score[:], ACT.Silu, bias=kb_cols[g][:, t : t + 1])
             p_f32.append(p_g)
 
-        vs_cols.append(last_column(columns[:, 3, :], gather_vs(1, "q_bf", "score1")))
+        vs_banks.append(gather_vs(1, "q_bf", "score0"))
 
         v_codes = tile("v_codes", [P, 2 * DV], U32)
         v_plane = tile("v_plane", [P, 2 * DV], U8)
-        nc.vector.quantize_mx(out=v_codes[:].bitcast(FP8X4), scales=v_plane[:], in_=v_bf[:])
+        nc.vector.quantize_mx(out=v_codes[:].bitcast(FP8X4), scales=v_plane[:], in_=v_bf[:].rearrange("p g e t -> p (g e t)"))
 
         w_codes = {}
         w_plane = {}
@@ -189,7 +185,7 @@ def tile_attend_silu_kb_gate_topkq256n1024t2048_kernel(tc, qT, k_words, k_scales
                 nc.vector.tensor_tensor(
                     w_bf[h][:].rearrange("p (c i) t -> p c t i", i=4),
                     p_f32[g][:, :, 128 * h : 128 * (h + 1)].rearrange("p t (c i) -> p c t i", i=4),
-                    vs_cols[g].unsqueeze(1).unsqueeze(3).to_broadcast([P, 32, 4, 4]),
+                    vs_banks[g][:, :, P - 1].unsqueeze(1).unsqueeze(3).to_broadcast([P, 32, 4, 4]),
                     ALU.mult,
                 )
             for h in range(2):
@@ -200,6 +196,11 @@ def tile_attend_silu_kb_gate_topkq256n1024t2048_kernel(tc, qT, k_words, k_scales
                     scales=w_plane[g, h][:],
                     in_=w_bf[h][:].rearrange("p n t -> p (n t)"),
                 )
+
+        tanh = tile("p0", [P, 2 * DV], F32)
+        nc.scalar.activation(tanh[:], og_sb[:].rearrange("p h e -> p (h e)"), ACT.Tanh, bias=silu0[:], scale=0.5)
+        gate = tile("gate", [P, 2 * DV], F32)
+        nc.scalar.activation(gate[:], tanh[:], ACT.Copy, bias=1.0 / 32.0, scale=1.0 / 32.0)
 
         for h in range(2):
             y = ps.tile([P, DV], F32, name=f"y{h}")

@@ -36,28 +36,29 @@ def tile_attend_silu_kb_gate_topkq256n1024t2048_kernel(tc, qT, k_words, k_scales
         q_rows = qT[0].rearrange("(o p j) n -> o p j n", o=2, j=4)
 
         s_pool = tile("s_pool", [P, T], U8)
-        nc.gpsimd.memset(s_pool[:].bitcast(I32), 0)
+        nc.gpsimd.memset(s_pool[64:P, :].bitcast(I32), 0)
+        nc.gpsimd.memset(s_pool[32:64, :].bitcast(I32), 0)
         zero = tile("zero", [P, 1], F32)
         nc.vector.memset(zero[:], 0.0)
         silu0 = tile("silu0", [P, 1], F32)
         nc.scalar.activation(silu0[:], zero[:], ACT.Silu)
 
+        nc.sync.dma_start(s_pool[0:32, :].bitcast(I32), k_scales.rearrange("o f t -> f o t").bitcast(I32))
         kb_pool = tile("kb_pool", [P, T], F32)
         nc.vector.memset(kb_pool[0 : P - 1, :].bitcast(I32), 0)
         nc.sync.dma_start(kb_pool[P - 1 : P, :], kb[0:1, :])
-        nc.sync.dma_start(q_raw[0][:], q_rows[0])
-        nc.sync.dma_start(s_pool[0:32, :].bitcast(I32), k_scales.rearrange("o f t -> f o t").bitcast(I32))
-        nc.sync.dma_start(q_raw[1][:], q_rows[1])
+        v_raw = [tile(f"v_raw{half}", [P, T // 2], F32) for half in range(2)]
+        for half in range(2):
+            nc.sync.dma_start(v_raw[half][:], vT[:, T // 2 * half : T // 2 * (half + 1)])
         ident = tile("ident", [P, P], F32)
         make_identity(nc, ident[:])
         vs_pool = tile("zero", [P, T], F32)
         nc.gpsimd.memset(vs_pool[0 : P - 1, :].bitcast(I32), 0)
         ident_bf = tile("ident_bf", [P, P], BF16)
         nc.scalar.copy(ident_bf[:], ident[:])
-        v_raw = [tile(f"v_raw{half}", [P, T // 2], F32) for half in range(2)]
-        nc.sync.dma_start(v_raw[0][:], vT[:, 0 : T // 2])
+        nc.sync.dma_start(q_raw[0][:], q_rows[0])
         nc.sync.dma_start(vs_pool[P - 1 : P, :], vs[0:1, :])
-        nc.sync.dma_start(v_raw[1][:], vT[:, T // 2 : T])
+        nc.sync.dma_start(q_raw[1][:], q_rows[1])
         k_pool = tile("k_pool", [P, T], I32)
         nc.sync.dma_start(k_pool[:], k_words[0].rearrange("p t b -> p (t b)").bitcast(I32))
         og_sb = tile("og_sb", [P, 2, DV], F32)
@@ -73,6 +74,8 @@ def tile_attend_silu_kb_gate_topkq256n1024t2048_kernel(tc, qT, k_words, k_scales
             nc.scalar.copy(cols, bank[:, :, P - 1])
             return cols
 
+        s_got = tile("s_got", [P, N], U8)
+        nc.vector.tensor_copy(s_got[:], s_pool[:].indirect(offsets[:]))
         kb_got = tile("kb_got", [P, N], F32)
         nc.vector.tensor_copy(
             kb_got[:].bitcast(U32).rearrange("p (g t b r) -> p g b t r", g=2, t=4, r=8),
@@ -88,8 +91,6 @@ def tile_attend_silu_kb_gate_topkq256n1024t2048_kernel(tc, qT, k_words, k_scales
             )
             return turn(vs_got, bank_name)
 
-        s_got = tile("s_got", [P, N], U8)
-        nc.vector.tensor_copy(s_got[:], s_pool[:].indirect(offsets[:]))
         s_first = tile("s_first", [P, N], U8)
         nc.vector.tensor_copy(
             s_first[:].bitcast(I32).rearrange("p (g t b w) -> p g t b w", g=2, t=4, w=2),
@@ -103,17 +104,16 @@ def tile_attend_silu_kb_gate_topkq256n1024t2048_kernel(tc, qT, k_words, k_scales
             )
 
 
-        q_bf = tile("q_bf", [P, 2, NQ, 4], BF16)
-        for o in range(2):
-            nc.scalar.copy(
-                q_bf[:, o].rearrange("p (c i) t -> p c t i", i=4),
-                q_raw[o][:].rearrange("p t (c i) -> p c t i", i=4),
-            )
-        q_codes = tile("kb_pool", [P, 2 * NQ], U32)
-        q_plane = tile("q_plane", [P, 2 * NQ], U8)
-        nc.vector.quantize_mx(out=q_codes[:].bitcast(FP8X4), scales=q_plane[:], in_=q_bf[:].rearrange("p o n t -> p (o n t)"))
+        vs_banks = [gather_vs(0, "s_pool", "y0")]
 
-        vs_banks = [gather_vs(0, "s_got", "y0")]
+        q_bf = tile("s_got", [P, 2, NQ, 4], BF16)
+        for o in range(2):
+            nc.gpsimd.tensor_scalar(q_bf[:, o], q_raw[o][:].rearrange("p t n -> p n t"), 1.0, 0.0, ALU.mult, ALU.add)
+        q_codes = tile("q_codes", [P, 2 * NQ], U32)
+        q_plane = tile("q_plane", [P, 2 * NQ], U8)
+        nc.vector.quantize_mx(
+            out=q_codes[:].bitcast(FP8X4), scales=q_plane[:], in_=q_bf[:].rearrange("p o n t -> p (o n t)")
+        )
 
         v_pool = tile("v_pool", [P, T], BF16)
         for half in range(2):
@@ -125,7 +125,8 @@ def tile_attend_silu_kb_gate_topkq256n1024t2048_kernel(tc, qT, k_words, k_scales
                 v_pool[:].indirect(offsets[:, 32 * g : 32 * (g + 1)]),
                 ACT.Copy,
             )
-        columns = tile("v_raw1", [P, 2, 4], F32)
+
+        columns = tile("v_pool", [P, 2, 4], F32)
         kb_cols = [last_column(columns[:, g, :], kb_banks[g]) for g in range(2)]
 
         v_bf = tile("v_bf", [P, 2, DV, 4], BF16)
@@ -137,7 +138,7 @@ def tile_attend_silu_kb_gate_topkq256n1024t2048_kernel(tc, qT, k_words, k_scales
 
         p_f32 = []
         for g in range(2):
-            k_got = [tile(name, [P, 256], U32) for name in ("q_bf", "s_pool")]
+            k_got = [tile(name, [P, 256], U32) for name in (("k_got0", "k_got1"), ("k_got0", "k_got1"))[g]]
             for half in range(2):
                 c0 = 32 * g + 16 * half
                 nc.vector.tensor_copy(
@@ -170,9 +171,9 @@ def tile_attend_silu_kb_gate_topkq256n1024t2048_kernel(tc, qT, k_words, k_scales
                 nc.scalar.activation(p_g[:, t, :], score[:], ACT.Silu, bias=kb_cols[g][:, t : t + 1])
             p_f32.append(p_g)
 
-        vs_banks.append(gather_vs(1, "q_bf", "score0"))
+        vs_banks.append(gather_vs(1, "k_got0", "score0"))
 
-        v_codes = tile("v_codes", [P, 2 * DV], U32)
+        v_codes = tile("k_got1", [P, 2 * DV], U32)
         v_plane = tile("v_plane", [P, 2 * DV], U8)
         nc.vector.quantize_mx(out=v_codes[:].bitcast(FP8X4), scales=v_plane[:], in_=v_bf[:].rearrange("p g e t -> p (g e t)"))
 

@@ -26,13 +26,18 @@ def tile_attend_silu_kb_gate_topkq256n1024t2048_kernel(tc, qT, k_words, k_scales
         sb = ctx.enter_context(tc.tile_pool(name="sb", bufs=1))
         ps = ctx.enter_context(tc.psum_pool(name="ps", bufs=1))
 
+        relay = ctx.enter_context(tc.tile_pool(name="relay", bufs=1))
+
+        def relay_tile(name, shape, dtype, offset):
+            return relay.tile(shape, dtype, name=name, align_bytes=64, offset=offset)
+
         def tile(name, shape, dtype):
             return sb.tile(shape, dtype, name=name, align_bytes=64)
 
         offsets = sb.tile([P, N // 16], U16, name="offsets")
         nc.sync.dma_start(offsets[:], offs)
 
-        q_raw = [tile(f"q_raw{o}", [P, 4, NQ], F32) for o in range(2)]
+        q_raw = [tile("q_raw0", [P, 4, NQ], F32), relay_tile("q_raw1", [P, 8, NQ], F32, 4096)[:, 0:4]]
         q_rows = qT[0].rearrange("(o p j) n -> o p j n", o=2, j=4)
 
         s_pool = tile("s_pool", [P, T], U8)
@@ -47,7 +52,7 @@ def tile_attend_silu_kb_gate_topkq256n1024t2048_kernel(tc, qT, k_words, k_scales
         kb_pool = tile("kb_pool", [P, T], F32)
         nc.vector.memset(kb_pool[0 : P - 1, :].bitcast(I32), 0)
         nc.sync.dma_start(kb_pool[P - 1 : P, :], kb[0:1, :])
-        v_raw = [tile(f"v_raw{half}", [P, T // 2], F32) for half in range(2)]
+        v_raw = [tile("v_raw0", [P, T // 2], F32), relay_tile("v_raw1", [P, T // 2], F32, 0)]
         for half in range(2):
             nc.sync.dma_start(v_raw[half][:], vT[:, T // 2 * half : T // 2 * (half + 1)])
         ident = tile("ident", [P, P], F32)
@@ -58,9 +63,9 @@ def tile_attend_silu_kb_gate_topkq256n1024t2048_kernel(tc, qT, k_words, k_scales
         nc.scalar.copy(ident_bf[:], ident[:])
         nc.sync.dma_start(q_raw[0][:], q_rows[0])
         nc.sync.dma_start(vs_pool[P - 1 : P, :], vs[0:1, :])
-        nc.sync.dma_start(q_raw[1][:], q_rows[1])
         k_pool = tile("k_pool", [P, T], I32)
         nc.sync.dma_start(k_pool[:], k_words[0].rearrange("p t b -> p (t b)").bitcast(I32))
+        nc.sync.dma_start(q_raw[1], q_rows[1])
         og_sb = tile("og_sb", [P, 2, DV], F32)
         nc.sync.dma_start(og_sb[:], og[0].rearrange("(h p) e -> p h e", h=2))
 
@@ -83,15 +88,18 @@ def tile_attend_silu_kb_gate_topkq256n1024t2048_kernel(tc, qT, k_words, k_scales
         )
         kb_banks = [turn(kb_got[:, 512 * g : 512 * (g + 1)], f"turn{g}") for g in range(2)]
 
-        def gather_vs(g, name, bank_name):
-            vs_got = tile(name, [P, 512], F32)
+        def gather_vs(g, vs_got, bank_name):
             nc.vector.tensor_copy(
                 vs_got[:].bitcast(U32).rearrange("p (t b r) -> p b t r", t=4, r=8),
                 vs_pool[:].bitcast(U32).indirect(offsets[:, 32 * g : 32 * (g + 1)]),
             )
             return turn(vs_got, bank_name)
 
-        s_first = tile("s_first", [P, N], U8)
+        v_pool = tile("v_pool", [P, T], BF16)
+        for half in range(2):
+            nc.scalar.copy(v_pool[:, T // 2 * half : T // 2 * (half + 1)], v_raw[half][:])
+
+        s_first = relay_tile("s_first", [P, N], U8, 0)
         nc.vector.tensor_copy(
             s_first[:].bitcast(I32).rearrange("p (g t b w) -> p g t b w", g=2, t=4, w=2),
             s_got[:].bitcast(I32).rearrange("p (g b t w) -> p g t b w", g=2, t=4, w=2),
@@ -103,21 +111,11 @@ def tile_attend_silu_kb_gate_topkq256n1024t2048_kernel(tc, qT, k_words, k_scales
                 s_first[8 * quad : 8 * quad + 64, :].bitcast(I32),
             )
 
-
-        vs_banks = [gather_vs(0, "s_pool", "y0")]
+        vs_banks = [gather_vs(0, relay_tile("vs_got0", [P, 512], F32, 2048), "y0")]
 
         q_bf = tile("s_got", [P, 2, NQ, 4], BF16)
-        for o in range(2):
-            nc.gpsimd.tensor_scalar(q_bf[:, o], q_raw[o][:].rearrange("p t n -> p n t"), 1.0, 0.0, ALU.mult, ALU.add)
-        q_codes = tile("q_codes", [P, 2 * NQ], U32)
-        q_plane = tile("q_plane", [P, 2 * NQ], U8)
-        nc.vector.quantize_mx(
-            out=q_codes[:].bitcast(FP8X4), scales=q_plane[:], in_=q_bf[:].rearrange("p o n t -> p (o n t)")
-        )
+        nc.gpsimd.tensor_scalar(q_bf[:, 0], q_raw[0][:].rearrange("p t n -> p n t"), 1.0, 0.0, ALU.mult, ALU.add)
 
-        v_pool = tile("v_pool", [P, T], BF16)
-        for half in range(2):
-            nc.scalar.copy(v_pool[:, T // 2 * half : T // 2 * (half + 1)], v_raw[half][:])
         v_got = [tile(f"v_got{g}", [P, 4, P], BF16) for g in range(2)]
         for g in range(2):
             nc.scalar.activation(
@@ -126,31 +124,54 @@ def tile_attend_silu_kb_gate_topkq256n1024t2048_kernel(tc, qT, k_words, k_scales
                 ACT.Copy,
             )
 
-        columns = tile("v_pool", [P, 2, 4], F32)
+        nc.scalar.copy(
+            q_bf[:, 1].rearrange("p (c i) t -> p c t i", i=4),
+            q_raw[1].rearrange("p t (c i) -> p c t i", i=4),
+        )
+        columns = relay_tile("columns", [P, 2, 4], F32, 4096 + 7168)
         kb_cols = [last_column(columns[:, g, :], kb_banks[g]) for g in range(2)]
 
-        v_bf = tile("v_bf", [P, 2, DV, 4], BF16)
+        v_bf = relay_tile("v_bf", [P, 2, DV, 4], BF16, 4096 + 4096)
         for g in range(2):
             v_bank = ps.tile([P, 4, P], BF16, name=("y1", "score3")[g])
             for t in range(4):
                 nc.tensor.transpose(v_bank[:, t, :], v_got[g][:, t, :], ident_bf[:])
             nc.scalar.copy(v_bf[:, g], v_bank[:].rearrange("p t e -> p e t"))
 
+        k_got = [tile(f"k_got{quarter}", [P, 256], U32) for quarter in range(3)]
+        k_got.append(relay_tile("k_got3", [P, 256], U32, 4096))
+        k_splits = [tile("k_split0", [P, 2048], U8), relay_tile("k_split1", [P, 2048], U8, 4096 + 2048)]
+
+        def gather_keys(quarter):
+            nc.vector.tensor_copy(
+                k_got[quarter][:], k_pool[:].bitcast(U32).indirect(offsets[:, 16 * quarter : 16 * (quarter + 1)])
+            )
+
+        def split_keys(quarter):
+            g, half = divmod(quarter, 2)
+            nc.vector.tensor_copy(
+                k_splits[g][:].bitcast(U16).rearrange("p (o t b r) -> p o t b r", o=2, t=4, r=8)[
+                    :, :, :, 8 * half : 8 * (half + 1), :
+                ],
+                k_got[quarter][:].bitcast(U16).rearrange("p (b t r o) -> p o t b r", o=2, t=4, r=8),
+            )
+
+        for quarter in range(3):
+            gather_keys(quarter)
+        for quarter in range(2):
+            split_keys(quarter)
+        q_codes = tile("q_codes", [P, 2 * NQ], U32)
+        q_plane = tile("q_plane", [P, 2 * NQ], U8)
+        nc.vector.quantize_mx(
+            out=q_codes[:].bitcast(FP8X4), scales=q_plane[:], in_=q_bf[:].rearrange("p o n t -> p (o n t)")
+        )
+        gather_keys(3)
+        for quarter in range(2, 4):
+            split_keys(quarter)
+
         p_f32 = []
         for g in range(2):
-            k_got = [tile(name, [P, 256], U32) for name in (("k_got0", "k_got1"), ("k_got0", "k_got1"))[g]]
-            for half in range(2):
-                c0 = 32 * g + 16 * half
-                nc.vector.tensor_copy(
-                    k_got[half][:],
-                    k_pool[:].bitcast(U32).indirect(offsets[:, c0 : c0 + 16]),
-                )
-            k_split = tile(f"k_split{g}", [P, 2 * 512 * 2], U8)
-            for half in range(2):
-                nc.vector.tensor_copy(
-                    k_split[:].bitcast(U16).rearrange("p (o t b r) -> p o t b r", o=2, t=4, r=8)[:, :, :, 8 * half : 8 * (half + 1), :],
-                    k_got[half][:].bitcast(U16).rearrange("p (b t r o) -> p o t b r", o=2, t=4, r=8),
-                )
+            k_split = k_splits[g]
             p_g = tile(f"p{g}", [P, 4, NQ], F32)
             for t in range(4):
                 score = ps.tile([P, NQ], F32, name=f"score{t}")
@@ -171,9 +192,9 @@ def tile_attend_silu_kb_gate_topkq256n1024t2048_kernel(tc, qT, k_words, k_scales
                 nc.scalar.activation(p_g[:, t, :], score[:], ACT.Silu, bias=kb_cols[g][:, t : t + 1])
             p_f32.append(p_g)
 
-        vs_banks.append(gather_vs(1, "k_got0", "score0"))
+        vs_banks.append(gather_vs(1, tile("k_got2", [P, 512], F32), "score0"))
 
-        v_codes = tile("k_got1", [P, 2 * DV], U32)
+        v_codes = relay_tile("v_codes", [P, 2 * DV], U32, 4096)
         v_plane = tile("v_plane", [P, 2 * DV], U8)
         nc.vector.quantize_mx(out=v_codes[:].bitcast(FP8X4), scales=v_plane[:], in_=v_bf[:].rearrange("p g e t -> p (g e t)"))
 

@@ -66,8 +66,6 @@ def tile_attend_silu_kb_gate_topkq256n1024t2048_kernel(tc, qT, k_words, k_scales
         k_pool = tile("k_pool", [P, T], I32)
         nc.sync.dma_start(k_pool[:], k_words[0].rearrange("p t b -> p (t b)").bitcast(I32))
         nc.sync.dma_start(q_raw[1], q_rows[1])
-        og_sb = tile("og_sb", [P, 2, DV], F32)
-        nc.sync.dma_start(og_sb[:], og[0].rearrange("(h p) e -> p h e", h=2))
 
         def turn(got, bank_name):
             bank = ps.tile([P, 4, P], F32, name=bank_name)
@@ -111,6 +109,9 @@ def tile_attend_silu_kb_gate_topkq256n1024t2048_kernel(tc, qT, k_words, k_scales
                 s_first[8 * quad : 8 * quad + 64, :].bitcast(I32),
             )
 
+        og_sb = tile("kb_got", [P, 2, DV], F32)
+        nc.sync.dma_start(og_sb[:], og[0].rearrange("(h p) e -> p h e", h=2))
+
         vs_banks = [gather_vs(0, relay_tile("vs_got0", [P, 512], F32, 2048), "y0")]
 
         q_bf = tile("s_got", [P, 2, NQ, 4], BF16)
@@ -132,17 +133,17 @@ def tile_attend_silu_kb_gate_topkq256n1024t2048_kernel(tc, qT, k_words, k_scales
         kb_cols = [last_column(columns[:, g, :], kb_banks[g]) for g in range(2)]
 
         v_bf = relay_tile("v_bf", [P, 2, DV, 4], BF16, 4096 + 4096)
+        v_bank = ps.tile([P, 2, 4, P], BF16, name="y1")
         for g in range(2):
-            v_bank = ps.tile([P, 4, P], BF16, name=("y1", "score3")[g])
             for t in range(4):
-                nc.tensor.transpose(v_bank[:, t, :], v_got[g][:, t, :], ident_bf[:])
-            nc.scalar.copy(v_bf[:, g], v_bank[:].rearrange("p t e -> p e t"))
+                nc.tensor.transpose(v_bank[:, g, t, :], v_got[g][:, t, :], ident_bf[:])
+        nc.scalar.copy(v_bf[:], v_bank[:].rearrange("p g t e -> p g e t"))
 
-        k_got = [tile(f"k_got{quarter}", [P, 256], U32) for quarter in range(3)]
-        k_got.append(relay_tile("k_got3", [P, 256], U32, 4096))
+        k_got = {}
         k_splits = [tile("k_split0", [P, 2048], U8), relay_tile("k_split1", [P, 2048], U8, 4096 + 2048)]
 
-        def gather_keys(quarter):
+        def gather_keys(quarter, got):
+            k_got[quarter] = got
             nc.vector.tensor_copy(
                 k_got[quarter][:], k_pool[:].bitcast(U32).indirect(offsets[:, 16 * quarter : 16 * (quarter + 1)])
             )
@@ -156,16 +157,23 @@ def tile_attend_silu_kb_gate_topkq256n1024t2048_kernel(tc, qT, k_words, k_scales
                 k_got[quarter][:].bitcast(U16).rearrange("p (b t r o) -> p o t b r", o=2, t=4, r=8),
             )
 
-        for quarter in range(3):
-            gather_keys(quarter)
+        def quantise_queries(o):
+            nc.vector.quantize_mx(
+                out=q_codes[:, NQ * o : NQ * (o + 1)].bitcast(FP8X4),
+                scales=q_plane[:, NQ * o : NQ * (o + 1)],
+                in_=q_bf[:, o].rearrange("p n t -> p (n t)"),
+            )
+
+        for quarter in range(2):
+            gather_keys(quarter, tile(f"k_got{quarter}", [P, 256], U32))
         for quarter in range(2):
             split_keys(quarter)
-        q_codes = tile("q_codes", [P, 2 * NQ], U32)
+        q_codes = tile("k_got0", [P, 2 * NQ], U32)
         q_plane = tile("q_plane", [P, 2 * NQ], U8)
-        nc.vector.quantize_mx(
-            out=q_codes[:].bitcast(FP8X4), scales=q_plane[:], in_=q_bf[:].rearrange("p o n t -> p (o n t)")
-        )
-        gather_keys(3)
+        quantise_queries(0)
+        gather_keys(2, tile("k_got1", [P, 256], U32))
+        quantise_queries(1)
+        gather_keys(3, relay_tile("k_got3", [P, 256], U32, 4096))
         for quarter in range(2, 4):
             split_keys(quarter)
 
@@ -173,26 +181,35 @@ def tile_attend_silu_kb_gate_topkq256n1024t2048_kernel(tc, qT, k_words, k_scales
         for g in range(2):
             k_split = k_splits[g]
             p_g = tile(f"p{g}", [P, 4, NQ], F32)
+            scores = [ps.tile([P, NQ], F32, name=f"score{t}") for t in range(4)]
+
+            def score_pass(t, h, o):
+                k0 = 1024 * o + 256 * t
+                s0 = 512 * g + 128 * t
+                q0 = NQ * o + 128 * h
+                nc.tensor.matmul_mx(
+                    out=scores[t][:, 128 * h : 128 * (h + 1)],
+                    lhsT=k_split[:, k0 : k0 + 256].bitcast(FP4X4),
+                    lhsT_scale=k_planes[:, o, s0 : s0 + 128],
+                    rhs=q_codes[:, q0 : q0 + 128].bitcast(FP8X4),
+                    rhs_scale=q_plane[:, q0 : q0 + 128],
+                    start=(o == 0),
+                    stop=(o == 1),
+                )
+
+            if g == 0:
+                for t in range(4):
+                    score_pass(t, 0, 0)
             for t in range(4):
-                score = ps.tile([P, NQ], F32, name=f"score{t}")
-                for h in range(2):
-                    for o in range(2):
-                        k0 = 1024 * o + 256 * t
-                        s0 = 512 * g + 128 * t
-                        q0 = NQ * o + 128 * h
-                        nc.tensor.matmul_mx(
-                            out=score[:, 128 * h : 128 * (h + 1)],
-                            lhsT=k_split[:, k0 : k0 + 256].bitcast(FP4X4),
-                            lhsT_scale=k_planes[:, o, s0 : s0 + 128],
-                            rhs=q_codes[:, q0 : q0 + 128].bitcast(FP8X4),
-                            rhs_scale=q_plane[:, q0 : q0 + 128],
-                            start=(o == 0),
-                            stop=(o == 1),
-                        )
-                nc.scalar.activation(p_g[:, t, :], score[:], ACT.Silu, bias=kb_cols[g][:, t : t + 1])
+                if g == 1:
+                    score_pass(t, 0, 0)
+                score_pass(t, 0, 1)
+                score_pass(t, 1, 0)
+                score_pass(t, 1, 1)
+                nc.scalar.activation(p_g[:, t, :], scores[t][:], ACT.Silu, bias=kb_cols[g][:, t : t + 1])
             p_f32.append(p_g)
 
-        vs_banks.append(gather_vs(1, tile("k_got2", [P, 512], F32), "score0"))
+        vs_banks.append(gather_vs(1, tile("k_got1", [P, 512], F32), "score0"))
 
         v_codes = relay_tile("v_codes", [P, 2 * DV], U32, 4096)
         v_plane = tile("v_plane", [P, 2 * DV], U8)

@@ -37,7 +37,7 @@ def tile_attend_silu_kb_gate_topkq256n1024t2048_kernel(tc, qT, k_words, k_scales
         offsets = sb.tile([P, N // 16], U16, name="offsets")
         nc.sync.dma_start(offsets[:], offs)
 
-        q_raw = [tile("q_raw0", [P, 4, NQ], F32), relay_tile("q_raw1", [P, 8, NQ], F32, 4096)[:, 0:4]]
+        q_raw = [tile("q_raw0", [P, 4, NQ], F32), relay_tile("q_raw1", [P, 10, NQ], F32, 4096)[:, 0:4]]
         q_rows = qT[0].rearrange("(o p j) n -> o p j n", o=2, j=4)
 
         s_pool = tile("s_pool", [P, T], U8)
@@ -129,7 +129,7 @@ def tile_attend_silu_kb_gate_topkq256n1024t2048_kernel(tc, qT, k_words, k_scales
             q_bf[:, 1].rearrange("p (c i) t -> p c t i", i=4),
             q_raw[1].rearrange("p t (c i) -> p c t i", i=4),
         )
-        columns = relay_tile("columns", [P, 2, 4], F32, 4096 + 7168)
+        columns = relay_tile("columns", [P, 2, 4], F32, 4096 + 9216)
         kb_cols = [last_column(columns[:, g, :], kb_banks[g]) for g in range(2)]
 
         v_bf = relay_tile("v_bf", [P, 2, DV, 4], BF16, 4096 + 4096)
@@ -171,8 +171,8 @@ def tile_attend_silu_kb_gate_topkq256n1024t2048_kernel(tc, qT, k_words, k_scales
         q_codes = tile("k_got0", [P, 2 * NQ], U32)
         q_plane = tile("q_plane", [P, 2 * NQ], U8)
         quantise_queries(0)
-        gather_keys(2, tile("k_got1", [P, 256], U32))
         quantise_queries(1)
+        gather_keys(2, relay_tile("k_got2", [P, 256], U32, 4096 + 6144))
         gather_keys(3, relay_tile("k_got3", [P, 256], U32, 4096))
         for quarter in range(2, 4):
             split_keys(quarter)
@@ -209,37 +209,48 @@ def tile_attend_silu_kb_gate_topkq256n1024t2048_kernel(tc, qT, k_words, k_scales
                 nc.scalar.activation(p_g[:, t, :], scores[t][:], ACT.Silu, bias=kb_cols[g][:, t : t + 1])
             p_f32.append(p_g)
 
-        vs_banks.append(gather_vs(1, tile("k_got1", [P, 512], F32), "score0"))
+        vs_banks.append(gather_vs(1, relay_tile("vs_got1", [P, 512], F32, 4096 + 6144), "score0"))
 
         v_codes = relay_tile("v_codes", [P, 2 * DV], U32, 4096)
         v_plane = tile("v_plane", [P, 2 * DV], U8)
         nc.vector.quantize_mx(out=v_codes[:].bitcast(FP8X4), scales=v_plane[:], in_=v_bf[:].rearrange("p g e t -> p (g e t)"))
 
+        w_bf = {}
         w_codes = {}
         w_plane = {}
-        for g in range(2):
-            w_bf = {}
-            for h in range(2):
-                w_bf[h] = tile(f"w_bf{g}{h}", [P, 128, 4], BF16)
-                nc.vector.tensor_tensor(
-                    w_bf[h][:].rearrange("p (c i) t -> p c t i", i=4),
-                    p_f32[g][:, :, 128 * h : 128 * (h + 1)].rearrange("p t (c i) -> p c t i", i=4),
-                    vs_banks[g][:, :, P - 1].unsqueeze(1).unsqueeze(3).to_broadcast([P, 32, 4, 4]),
-                    ALU.mult,
-                )
-            for h in range(2):
-                w_codes[g, h] = tile(f"w_codes{g}{h}", [P, 128], U32)
-                w_plane[g, h] = tile(f"w_plane{g}{h}", [P, 128], U8)
-                nc.vector.quantize_mx(
-                    out=w_codes[g, h][:].bitcast(FP8X4),
-                    scales=w_plane[g, h][:],
-                    in_=w_bf[h][:].rearrange("p n t -> p (n t)"),
-                )
+
+        def weigh(g, h):
+            w_bf[g, h] = tile(f"w_bf{g}{h}", [P, 128, 4], BF16)
+            nc.vector.tensor_tensor(
+                w_bf[g, h][:].rearrange("p (c i) t -> p c t i", i=4),
+                p_f32[g][:, :, 128 * h : 128 * (h + 1)].rearrange("p t (c i) -> p c t i", i=4),
+                vs_banks[g][:, :, P - 1].unsqueeze(1).unsqueeze(3).to_broadcast([P, 32, 4, 4]),
+                ALU.mult,
+            )
+
+        def quantise_weights(g, h, name):
+            w_codes[g, h] = tile(name, [P, 128], U32)
+            w_plane[g, h] = tile(f"w_plane{g}{h}", [P, 128], U8)
+            nc.vector.quantize_mx(
+                out=w_codes[g, h][:].bitcast(FP8X4),
+                scales=w_plane[g, h][:],
+                in_=w_bf[g, h][:].rearrange("p n t -> p (n t)"),
+            )
+
+        weigh(0, 0)
+        weigh(0, 1)
+        quantise_weights(0, 0, "w_codes00")
 
         tanh = tile("p0", [P, 2 * DV], F32)
         nc.scalar.activation(tanh[:], og_sb[:].rearrange("p h e -> p (h e)"), ACT.Tanh, bias=silu0[:], scale=0.5)
         gate = tile("gate", [P, 2 * DV], F32)
         nc.scalar.activation(gate[:], tanh[:], ACT.Copy, bias=1.0 / 32.0, scale=1.0 / 32.0)
+
+        weigh(1, 0)
+        weigh(1, 1)
+        quantise_weights(1, 0, "w_codes10")
+        quantise_weights(0, 1, "p0")
+        quantise_weights(1, 1, "w_codes11")
 
         for h in range(2):
             y = ps.tile([P, DV], F32, name=f"y{h}")

@@ -180,7 +180,7 @@ def tile_attend_silu_kb_gate_topkq256n1024t2048_kernel(tc, qT, k_words, k_scales
         p_f32 = []
         for g in range(2):
             k_split = k_splits[g]
-            p_g = tile(f"p{g}", [P, 4, NQ], F32)
+            p_g = tile(f"p{g}", [P, NQ // 4, 4, 4], F32)
             scores = [ps.tile([P, NQ], F32, name=f"score{t}") for t in range(4)]
 
             def score_pass(t, h, o):
@@ -206,7 +206,12 @@ def tile_attend_silu_kb_gate_topkq256n1024t2048_kernel(tc, qT, k_words, k_scales
                 score_pass(t, 0, 1)
                 score_pass(t, 1, 0)
                 score_pass(t, 1, 1)
-                nc.scalar.activation(p_g[:, t, :], scores[t][:], ACT.Silu, bias=kb_cols[g][:, t : t + 1])
+                nc.scalar.activation(
+                    p_g[:, :, t, :],
+                    scores[t][:].rearrange("p (c i) -> p c i", i=4),
+                    ACT.Silu,
+                    bias=kb_cols[g][:, t : t + 1],
+                )
             p_f32.append(p_g)
 
         vs_banks.append(gather_vs(1, relay_tile("vs_got1", [P, 512], F32, 4096 + 6144), "score0"))
@@ -223,7 +228,7 @@ def tile_attend_silu_kb_gate_topkq256n1024t2048_kernel(tc, qT, k_words, k_scales
             w_bf[g, h] = tile(f"w_bf{g}{h}", [P, 128, 4], BF16)
             nc.vector.tensor_tensor(
                 w_bf[g, h][:].rearrange("p (c i) t -> p c t i", i=4),
-                p_f32[g][:, :, 128 * h : 128 * (h + 1)].rearrange("p t (c i) -> p c t i", i=4),
+                p_f32[g][:, 32 * h : 32 * (h + 1)],
                 vs_banks[g][:, :, P - 1].unsqueeze(1).unsqueeze(3).to_broadcast([P, 32, 4, 4]),
                 ALU.mult,
             )

@@ -50,13 +50,13 @@ def tile_attend_silu_kb_gate_topkq256n1024t2048_kernel(tc, qT, k_words, k_scales
 
         nc.sync.dma_start(s_pool[0:32, :].bitcast(I32), k_scales.rearrange("o f t -> f o t").bitcast(I32))
         kb_pool = tile("kb_pool", [P, T], F32)
-        nc.vector.memset(kb_pool[0 : P - 1, :].bitcast(I32), 0)
+        ident = tile("ident", [P, P], F32)
+        make_identity(nc, ident[:])
+        nc.gpsimd.memset(kb_pool[0 : P - 1, :].bitcast(I32), 0)
         nc.sync.dma_start(kb_pool[P - 1 : P, :], kb[0:1, :])
         v_raw = [tile("v_raw0", [P, T // 2], F32), relay_tile("v_raw1", [P, T // 2], F32, 0)]
         for half in range(2):
             nc.sync.dma_start(v_raw[half][:], vT[:, T // 2 * half : T // 2 * (half + 1)])
-        ident = tile("ident", [P, P], F32)
-        make_identity(nc, ident[:])
         vs_pool = tile("zero", [P, T], F32)
         nc.gpsimd.memset(vs_pool[0 : P - 1, :].bitcast(I32), 0)
         ident_bf = tile("ident_bf", [P, P], BF16)

@@ -59,13 +59,13 @@ def tile_attend_silu_kb_gate_topkq256n1024t2048_kernel(tc, qT, k_words, k_scales
             nc.sync.dma_start(v_raw[half][:], vT[:, T // 2 * half : T // 2 * (half + 1)])
         vs_pool = tile("zero", [P, T], F32)
         nc.gpsimd.memset(vs_pool[0 : P - 1, :].bitcast(I32), 0)
-        ident_bf = tile("ident_bf", [P, P], BF16)
-        nc.scalar.copy(ident_bf[:], ident[:])
         nc.sync.dma_start(q_raw[0][:], q_rows[0])
         nc.sync.dma_start(vs_pool[P - 1 : P, :], vs[0:1, :])
         k_pool = tile("k_pool", [P, T], I32)
         nc.sync.dma_start(k_pool[:], k_words[0].rearrange("p t b -> p (t b)").bitcast(I32))
         nc.sync.dma_start(q_raw[1], q_rows[1])
+        og_sb = tile("og_sb", [P, 2, DV], F32)
+        nc.sync.dma_start(og_sb[:], og[0].rearrange("(h p) e -> p h e", h=2))
 
         def turn(got, bank_name):
             bank = ps.tile([P, 4, P], F32, name=bank_name)
@@ -109,18 +109,15 @@ def tile_attend_silu_kb_gate_topkq256n1024t2048_kernel(tc, qT, k_words, k_scales
                 s_first[8 * quad : 8 * quad + 64, :].bitcast(I32),
             )
 
-        og_sb = tile("kb_got", [P, 2, DV], F32)
-        nc.sync.dma_start(og_sb[:], og[0].rearrange("(h p) e -> p h e", h=2))
-
         vs_banks = [gather_vs(0, relay_tile("vs_got0", [P, 512], F32, 2048), "y0")]
 
         q_bf = tile("s_got", [P, 2, NQ, 4], BF16)
         nc.gpsimd.tensor_scalar(q_bf[:, 0], q_raw[0][:].rearrange("p t n -> p n t"), 1.0, 0.0, ALU.mult, ALU.add)
 
-        v_got = [tile(f"v_got{g}", [P, 4, P], BF16) for g in range(2)]
+        v_got = [tile(f"v_got{g}", [P, P, 4], BF16) for g in range(2)]
         for g in range(2):
             nc.scalar.activation(
-                v_got[g][:].rearrange("p t (b r) -> p b t r", r=8),
+                v_got[g][:].rearrange("p (b r) t -> p b t r", r=8),
                 v_pool[:].indirect(offsets[:, 32 * g : 32 * (g + 1)]),
                 ACT.Copy,
             )
@@ -129,15 +126,24 @@ def tile_attend_silu_kb_gate_topkq256n1024t2048_kernel(tc, qT, k_words, k_scales
             q_bf[:, 1].rearrange("p (c i) t -> p c t i", i=4),
             q_raw[1].rearrange("p t (c i) -> p c t i", i=4),
         )
-        columns = relay_tile("columns", [P, 2, 4], F32, 4096 + 9216)
-        kb_cols = [last_column(columns[:, g, :], kb_banks[g]) for g in range(2)]
+        columns = relay_tile("columns", [P, 3, 4], F32, 4096 + 9216)
+        early_cols = relay_tile("early_cols", [P, 3], F32, 4096 + 7168)
+        last_column(columns[:, 0, :], kb_banks[0])
+        nc.scalar.copy(early_cols[:], kb_banks[1][:, 0:3, P - 1])
+        nc.scalar.copy(columns[:, 1, 3:4], kb_banks[1][:, 3, P - 1 : P])
+        kb_cols = [[columns[:, 0, t : t + 1] for t in range(4)], [early_cols[:, t : t + 1] for t in range(3)] + [columns[:, 1, 3:4]]]
 
+        tanh = tile("q_raw0", [P, 2 * DV], F32)
+        nc.scalar.activation(tanh[:], og_sb[:].rearrange("p h e -> p (h e)"), ACT.Tanh, bias=silu0[:], scale=0.5)
         v_bf = relay_tile("v_bf", [P, 2, DV, 4], BF16, 4096 + 4096)
-        v_bank = ps.tile([P, 2, 4, P], BF16, name="y1")
+        v_bank = ps.tile([P, 2, 2, P], F32, name="y1")
         for g in range(2):
-            for t in range(4):
-                nc.tensor.transpose(v_bank[:, g, t, :], v_got[g][:, t, :], ident_bf[:])
-        nc.scalar.copy(v_bf[:], v_bank[:].rearrange("p g t e -> p g e t"))
+            pairs = v_got[g][:].bitcast(F32)
+            for u in range(2):
+                nc.tensor.transpose(v_bank[:, g, u, :], pairs[:, :, u], ident[:])
+        nc.scalar.copy(v_bf[:].bitcast(F32), v_bank[:].rearrange("p g u e -> p g e u"))
+        gate = tile("gate", [P, 2 * DV], F32)
+        nc.scalar.activation(gate[:], tanh[:], ACT.Copy, bias=1.0 / 32.0, scale=1.0 / 32.0)
 
         k_got = {}
         k_splits = [tile("k_split0", [P, 2048], U8), relay_tile("k_split1", [P, 2048], U8, 4096 + 2048)]
@@ -172,16 +178,17 @@ def tile_attend_silu_kb_gate_topkq256n1024t2048_kernel(tc, qT, k_words, k_scales
         q_plane = tile("q_plane", [P, 2 * NQ], U8)
         quantise_queries(0)
         quantise_queries(1)
-        gather_keys(2, relay_tile("k_got2", [P, 256], U32, 4096 + 6144))
+        gather_keys(2, relay_tile("k_got2", [P, 1536], U32, 4096 + 9728)[:, 0:256])
         gather_keys(3, relay_tile("k_got3", [P, 256], U32, 4096))
         for quarter in range(2, 4):
             split_keys(quarter)
 
         p_f32 = []
+        score_banks = [[f"score{t}" for t in range(4)], ["turn0", "turn1", "y1", "score0"]]
         for g in range(2):
             k_split = k_splits[g]
             p_g = tile(f"p{g}", [P, NQ // 4, 4, 4], F32)
-            scores = [ps.tile([P, NQ], F32, name=f"score{t}") for t in range(4)]
+            scores = [ps.tile([P, NQ], F32, name=score_banks[g][t]) for t in range(4)]
 
             def score_pass(t, h, o):
                 k0 = 1024 * o + 256 * t
@@ -210,11 +217,13 @@ def tile_attend_silu_kb_gate_topkq256n1024t2048_kernel(tc, qT, k_words, k_scales
                     p_g[:, :, t, :],
                     scores[t][:].rearrange("p (c i) -> p c i", i=4),
                     ACT.Silu,
-                    bias=kb_cols[g][:, t : t + 1],
+                    bias=kb_cols[g][t],
                 )
             p_f32.append(p_g)
+            if g == 0:
+                vs_cols = last_column(columns[:, 2, :], vs_banks[0])
 
-        vs_banks.append(gather_vs(1, relay_tile("vs_got1", [P, 512], F32, 4096 + 6144), "score0"))
+        vs_banks.append(gather_vs(1, relay_tile("vs_got1", [P, 512], F32, 16384), "score1"))
 
         v_codes = relay_tile("v_codes", [P, 2 * DV], U32, 4096)
         v_plane = tile("v_plane", [P, 2 * DV], U8)
@@ -243,22 +252,29 @@ def tile_attend_silu_kb_gate_topkq256n1024t2048_kernel(tc, qT, k_words, k_scales
             )
 
         weigh(0, 0)
-        weigh(0, 1)
-        quantise_weights(0, 0, "w_codes00")
-
-        tanh = tile("p0", [P, 2 * DV], F32)
-        nc.scalar.activation(tanh[:], og_sb[:].rearrange("p h e -> p (h e)"), ACT.Tanh, bias=silu0[:], scale=0.5)
-        gate = tile("gate", [P, 2 * DV], F32)
-        nc.scalar.activation(gate[:], tanh[:], ACT.Copy, bias=1.0 / 32.0, scale=1.0 / 32.0)
+        w_places = relay_tile("w_places", [P, 4, 128], BF16, 4096 + 7168)
+        for t in range(4):
+            nc.scalar.activation(
+                w_places[:, t, :].rearrange("p (c i) -> p c i", i=4),
+                p_f32[0][:, 32:64, t, :],
+                ACT.Copy,
+                scale=vs_cols[:, t : t + 1],
+            )
+        w_bf[0, 1] = tile("w_bf01", [P, 128, 4], BF16)
+        nc.scalar.copy(
+            w_bf[0, 1][:].rearrange("p (c i) t -> p c t i", i=4),
+            w_places[:].rearrange("p t (c i) -> p c t i", i=4),
+        )
 
         weigh(1, 0)
         weigh(1, 1)
+        quantise_weights(0, 0, "w_codes00")
         quantise_weights(1, 0, "w_codes10")
-        quantise_weights(0, 1, "p0")
+        quantise_weights(0, 1, "p1")
         quantise_weights(1, 1, "w_codes11")
 
         for h in range(2):
-            y = ps.tile([P, DV], F32, name=f"y{h}")
+            y = ps.tile([P, DV], F32, name=f"score{2 + h}")
             for g in range(2):
                 nc.tensor.matmul_mx(
                     out=y[:],

@@ -18,6 +18,7 @@ FP4X4 = mybir.dt.float4_e2m1fn_x4
 ACT = mybir.ActivationFunctionType
 ALU = mybir.AluOpType
 P = 128
+VECTOR_QUERIES = 160
 
 
 def tile_attend_silu_kb_gate_topkq256n1024t2048_kernel(tc, qT, k_words, k_scales, vT, vs, kb, og, offs, out):
@@ -127,11 +128,7 @@ def tile_attend_silu_kb_gate_topkq256n1024t2048_kernel(tc, qT, k_words, k_scales
             q_raw[1].rearrange("p t (c i) -> p c t i", i=4),
         )
         columns = relay_tile("columns", [P, 3, 4], F32, 4096 + 9216)
-        early_cols = relay_tile("early_cols", [P, 3], F32, 4096 + 7168)
-        last_column(columns[:, 0, :], kb_banks[0])
-        nc.scalar.copy(early_cols[:], kb_banks[1][:, 0:3, P - 1])
-        nc.scalar.copy(columns[:, 1, 3:4], kb_banks[1][:, 3, P - 1 : P])
-        kb_cols = [[columns[:, 0, t : t + 1] for t in range(4)], [early_cols[:, t : t + 1] for t in range(3)] + [columns[:, 1, 3:4]]]
+        kb_cols = [last_column(columns[:, g, :], kb_banks[g]) for g in range(2)]
 
         tanh = tile("q_raw0", [P, 2 * DV], F32)
         nc.scalar.activation(tanh[:], og_sb[:].rearrange("p h e -> p (h e)"), ACT.Tanh, bias=silu0[:], scale=0.5)
@@ -217,7 +214,7 @@ def tile_attend_silu_kb_gate_topkq256n1024t2048_kernel(tc, qT, k_words, k_scales
                     p_g[:, :, t, :],
                     scores[t][:].rearrange("p (c i) -> p c i", i=4),
                     ACT.Silu,
-                    bias=kb_cols[g][t],
+                    bias=kb_cols[g][:, t : t + 1],
                 )
             p_f32.append(p_g)
             if g == 0:
@@ -229,16 +226,15 @@ def tile_attend_silu_kb_gate_topkq256n1024t2048_kernel(tc, qT, k_words, k_scales
         v_plane = tile("v_plane", [P, 2 * DV], U8)
         nc.vector.quantize_mx(out=v_codes[:].bitcast(FP8X4), scales=v_plane[:], in_=v_bf[:].rearrange("p g e t -> p (g e t)"))
 
-        w_bf = {}
+        w_bf = [tile(f"w_bf{g}", [P, NQ, 4], BF16) for g in range(2)]
         w_codes = {}
         w_plane = {}
 
-        def weigh(g, h):
-            w_bf[g, h] = tile(f"w_bf{g}{h}", [P, 128, 4], BF16)
+        def weigh(g, q0, q1):
             nc.vector.tensor_tensor(
-                w_bf[g, h][:].rearrange("p (c i) t -> p c t i", i=4),
-                p_f32[g][:, 32 * h : 32 * (h + 1)],
-                vs_banks[g][:, :, P - 1].unsqueeze(1).unsqueeze(3).to_broadcast([P, 32, 4, 4]),
+                w_bf[g][:, q0:q1].rearrange("p (c i) t -> p c t i", i=4),
+                p_f32[g][:, q0 // 4 : q1 // 4],
+                vs_banks[g][:, :, P - 1].unsqueeze(1).unsqueeze(3).to_broadcast([P, (q1 - q0) // 4, 4, 4]),
                 ALU.mult,
             )
 
@@ -248,26 +244,25 @@ def tile_attend_silu_kb_gate_topkq256n1024t2048_kernel(tc, qT, k_words, k_scales
             nc.vector.quantize_mx(
                 out=w_codes[g, h][:].bitcast(FP8X4),
                 scales=w_plane[g, h][:],
-                in_=w_bf[g, h][:].rearrange("p n t -> p (n t)"),
+                in_=w_bf[g][:, 128 * h : 128 * (h + 1)].rearrange("p n t -> p (n t)"),
             )
 
-        weigh(0, 0)
-        w_places = relay_tile("w_places", [P, 4, 128], BF16, 4096 + 7168)
+        weigh(0, 0, VECTOR_QUERIES)
+        w_places = relay_tile("w_places", [P, 4, NQ - VECTOR_QUERIES], BF16, 16384)
         for t in range(4):
             nc.scalar.activation(
                 w_places[:, t, :].rearrange("p (c i) -> p c i", i=4),
-                p_f32[0][:, 32:64, t, :],
+                p_f32[0][:, VECTOR_QUERIES // 4 :, t, :],
                 ACT.Copy,
                 scale=vs_cols[:, t : t + 1],
             )
-        w_bf[0, 1] = tile("w_bf01", [P, 128, 4], BF16)
         nc.scalar.copy(
-            w_bf[0, 1][:].rearrange("p (c i) t -> p c t i", i=4),
+            w_bf[0][:, VECTOR_QUERIES:].rearrange("p (c i) t -> p c t i", i=4),
             w_places[:].rearrange("p t (c i) -> p c t i", i=4),
         )
 
-        weigh(1, 0)
-        weigh(1, 1)
+        weigh(1, 0, 128)
+        weigh(1, 128, NQ)
         quantise_weights(0, 0, "w_codes00")
         quantise_weights(1, 0, "w_codes10")
         quantise_weights(0, 1, "p1")

@@ -127,8 +127,8 @@ def tile_attend_silu_kb_gate_topkq256n1024t2048_kernel(tc, qT, k_words, k_scales
             q_bf[:, 1].rearrange("p (c i) t -> p c t i", i=4),
             q_raw[1].rearrange("p t (c i) -> p c t i", i=4),
         )
-        columns = relay_tile("columns", [P, 3, 4], F32, 4096 + 9216)
-        kb_cols = [last_column(columns[:, g, :], kb_banks[g]) for g in range(2)]
+        kb_cols = [last_column(relay_tile(f"kb_cols{g}", [P, 4], F32, 11264 + 2048 * g)[:], kb_banks[g]) for g in range(2)]
+        vs_cols = last_column(relay_tile("vs_cols", [P, 4], F32, 12288)[:], vs_banks[0])
 
         tanh = tile("q_raw0", [P, 2 * DV], F32)
         nc.scalar.activation(tanh[:], og_sb[:].rearrange("p h e -> p (h e)"), ACT.Tanh, bias=silu0[:], scale=0.5)
@@ -217,14 +217,8 @@ def tile_attend_silu_kb_gate_topkq256n1024t2048_kernel(tc, qT, k_words, k_scales
                     bias=kb_cols[g][:, t : t + 1],
                 )
             p_f32.append(p_g)
-            if g == 0:
-                vs_cols = last_column(columns[:, 2, :], vs_banks[0])
 
         vs_banks.append(gather_vs(1, relay_tile("vs_got1", [P, 512], F32, 16384), "score1"))
-
-        v_codes = relay_tile("v_codes", [P, 2 * DV], U32, 4096)
-        v_plane = tile("v_plane", [P, 2 * DV], U8)
-        nc.vector.quantize_mx(out=v_codes[:].bitcast(FP8X4), scales=v_plane[:], in_=v_bf[:].rearrange("p g e t -> p (g e t)"))
 
         w_bf = [tile(f"w_bf{g}", [P, NQ, 4], BF16) for g in range(2)]
         w_codes = {}
@@ -248,6 +242,9 @@ def tile_attend_silu_kb_gate_topkq256n1024t2048_kernel(tc, qT, k_words, k_scales
             )
 
         weigh(0, 0, VECTOR_QUERIES)
+        v_codes = relay_tile("v_codes", [P, 2 * DV], U32, 11264)
+        v_plane = tile("v_plane", [P, 2 * DV], U8)
+        nc.vector.quantize_mx(out=v_codes[:].bitcast(FP8X4), scales=v_plane[:], in_=v_bf[:].rearrange("p g e t -> p (g e t)"))
         w_places = relay_tile("w_places", [P, 4, NQ - VECTOR_QUERIES], BF16, 16384)
         for t in range(4):
             nc.scalar.activation(

@@ -104,10 +104,11 @@ def tile_attend_silu_kb_gate_topkq256n1024t2048_kernel(tc, qT, k_words, k_scales
             s_got[:].bitcast(I32).rearrange("p (g b t w) -> p g t b w", g=2, t=4, w=2),
         )
         k_planes = tile("k_planes", [P, 2, N], U8)
+        nc.vector.memset(k_planes[:].bitcast(I32), 0)
         for quad in range(4):
             nc.sync.dma_start(
-                k_planes[32 * quad : 32 * (quad + 1)].bitcast(I32),
-                s_first[8 * quad : 8 * quad + 64, :].bitcast(I32),
+                k_planes[32 * quad : 32 * quad + 4].bitcast(I32),
+                s_first[8 * quad : 8 * quad + 8, :].bitcast(I32),
             )
 
         vs_banks = [gather_vs(0, relay_tile("vs_got0", [P, 512], F32, 2048), "y0")]

@@ -42,14 +42,13 @@ def tile_attend_silu_kb_gate_topkq256n1024t2048_kernel(tc, qT, k_words, k_scales
         q_rows = qT[0].rearrange("(o p j) n -> o p j n", o=2, j=4)
 
         s_pool = tile("s_pool", [P, T], U8)
-        nc.gpsimd.memset(s_pool[64:P, :].bitcast(I32), 0)
-        nc.gpsimd.memset(s_pool[32:64, :].bitcast(I32), 0)
+        nc.gpsimd.memset(s_pool[0:96, :].bitcast(I32), 0)
         zero = tile("zero", [P, 1], F32)
         nc.vector.memset(zero[:], 0.0)
         silu0 = tile("silu0", [P, 1], F32)
         nc.scalar.activation(silu0[:], zero[:], ACT.Silu)
 
-        nc.sync.dma_start(s_pool[0:32, :].bitcast(I32), k_scales.rearrange("o f t -> f o t").bitcast(I32))
+        nc.sync.dma_start(s_pool[96:P, :].bitcast(I32), k_scales.rearrange("o f t -> f o t").bitcast(I32))
         kb_pool = tile("kb_pool", [P, T], F32)
         ident = tile("ident", [P, P], F32)
         make_identity(nc, ident[:])
@@ -103,12 +102,13 @@ def tile_attend_silu_kb_gate_topkq256n1024t2048_kernel(tc, qT, k_words, k_scales
             s_first[:].bitcast(I32).rearrange("p (g t b w) -> p g t b w", g=2, t=4, w=2),
             s_got[:].bitcast(I32).rearrange("p (g b t w) -> p g t b w", g=2, t=4, w=2),
         )
-        k_planes = tile("k_planes", [P, 2, N], U8)
-        nc.vector.memset(k_planes[:].bitcast(I32), 0)
+        k_planes_all = tile("k_planes", [P, 2 * N + 4], U8)
+        nc.vector.memset(k_planes_all[:].bitcast(I32), 0)
+        k_planes = k_planes_all[:, 0 : 2 * N].rearrange("p (o n) -> p o n", o=2)
         for quad in range(4):
             nc.sync.dma_start(
                 k_planes[32 * quad : 32 * quad + 4].bitcast(I32),
-                s_first[8 * quad : 8 * quad + 8, :].bitcast(I32),
+                s_first[96 + 8 * quad : 96 + 8 * quad + 8, :].bitcast(I32),
             )
 
         vs_banks = [gather_vs(0, relay_tile("vs_got0", [P, 512], F32, 2048), "y0")]
@@ -280,5 +280,5 @@ def tile_attend_silu_kb_gate_topkq256n1024t2048_kernel(tc, qT, k_words, k_scales
                 )
             res = tile(f"res{h}", [P, DV], F32)
             nc.vector.tensor_tensor(res[:], y[:], gate[:, DV * h : DV * (h + 1)], ALU.mult)
-            queue = nc.sync if h == 0 else nc.scalar
+            queue = nc.scalar if h == 0 else nc.sync
             queue.dma_start(out[0, 128 * h : 128 * (h + 1), :], res[:])

@@ -20,17 +20,52 @@ ALU = mybir.AluOpType
 P = 128
 VECTOR_QUERIES = 160
 
+NESTED = {
+    "v_raw1": (4096, None),
+    "s_first": (1024, "v_raw1"),
+    "vs_got0": (2048, "v_raw1"),
+    "q_raw0": (4096, None),
+    "v_got1": (1024, "q_raw0"),
+    "k_got0": (1024, "q_raw0"),
+    "k_got2": (1024, "k_got0"),
+    "vs_got1": (2048, "k_got2"),
+    "w_places": (1024, "vs_got1"),
+    "tanh": (1024, "vs_got1"),
+    "k_got1": (1024, "q_raw0"),
+    "q_raw1": (4096, None),
+    "k_split1": (2048, "q_raw1"),
+    "k_got3": (1024, "q_raw1"),
+    "vs_cols0": (64, "q_raw1"),
+    "kb_cols0": (64, "q_raw1"),
+    "v_bf": (2048, "kb_cols0"),
+    "kb_cols1": (64, "q_raw1"),
+    "kb_last": (64, "q_raw1"),
+    "p0": (4096, "q_raw1"),
+}
+
+
+def nested_bytes(name):
+    return NESTED[name][0] + sum(nested_bytes(c) for c in NESTED if NESTED[c][1] == name)
+
+
+def nested_offset(name):
+    parent = NESTED[name][1]
+    names = list(NESTED)
+    before = [c for c in names[: names.index(name)] if NESTED[c][1] == parent]
+    start = 0 if parent is None else nested_offset(parent) + NESTED[parent][0]
+    return start + sum(nested_bytes(c) for c in before)
+
 
 def tile_attend_silu_kb_gate_topkq256n1024t2048_kernel(tc, qT, k_words, k_scales, vT, vs, kb, og, offs, out):
     nc = tc.nc
     with ExitStack() as ctx:
         sb = ctx.enter_context(tc.tile_pool(name="sb", bufs=1))
         ps = ctx.enter_context(tc.psum_pool(name="ps", bufs=1))
-
         relay = ctx.enter_context(tc.tile_pool(name="relay", bufs=1))
 
-        def relay_tile(name, shape, dtype, offset):
-            return relay.tile(shape, dtype, name=name, align_bytes=64, offset=offset)
+        def nested(name, dtype, size):
+            whole = relay.tile([P, nested_bytes(name) // size], dtype, name=name, align_bytes=64, offset=nested_offset(name))
+            return whole[:, 0 : NESTED[name][0] // size]
 
         def tile(name, shape, dtype):
             return sb.tile(shape, dtype, name=name, align_bytes=64)
@@ -38,28 +73,31 @@ def tile_attend_silu_kb_gate_topkq256n1024t2048_kernel(tc, qT, k_words, k_scales
         offsets = sb.tile([P, N // 16], U16, name="offsets")
         nc.sync.dma_start(offsets[:], offs)
 
-        q_raw = [tile("q_raw0", [P, 4, NQ], F32), relay_tile("q_raw1", [P, 10, NQ], F32, 4096)[:, 0:4]]
-        q_rows = qT[0].rearrange("(o p j) n -> o p j n", o=2, j=4)
-
-        s_pool = tile("s_pool", [P, T], U8)
-        nc.gpsimd.memset(s_pool[0:96, :].bitcast(I32), 0)
         zero = tile("zero", [P, 1], F32)
         nc.vector.memset(zero[:], 0.0)
         silu0 = tile("silu0", [P, 1], F32)
         nc.scalar.activation(silu0[:], zero[:], ACT.Silu)
 
+        s_pool = tile("s_pool", [P, T], U8)
+        nc.gpsimd.memset(s_pool[0:96, :].bitcast(I32), 0)
         nc.sync.dma_start(s_pool[96:P, :].bitcast(I32), k_scales.rearrange("o f t -> f o t").bitcast(I32))
         kb_pool = tile("kb_pool", [P, T], F32)
-        ident = tile("ident", [P, P], F32)
-        make_identity(nc, ident[:])
         nc.gpsimd.memset(kb_pool[0 : P - 1, :].bitcast(I32), 0)
         nc.sync.dma_start(kb_pool[P - 1 : P, :], kb[0:1, :])
-        v_raw = [tile("v_raw0", [P, T // 2], F32), relay_tile("v_raw1", [P, T // 2], F32, 0)]
-        for half in range(2):
-            nc.sync.dma_start(v_raw[half][:], vT[:, T // 2 * half : T // 2 * (half + 1)])
+        k_planes_all = tile("k_planes", [P, 2 * N + 4], U8)
+        nc.vector.memset(k_planes_all[:].bitcast(I32), 0)
+        k_planes = k_planes_all[:, 0 : 2 * N].rearrange("p (o n) -> p o n", o=2)
+        ident = tile("ident", [P, P], F32)
+        make_identity(nc, ident[:])
+
+        v_raw = [tile("v_raw0", [P, T // 2], F32)[:], nested("v_raw1", F32, 4)]
+        for c in range(2):
+            nc.sync.dma_start(v_raw[c], vT[:, T // 2 * c : T // 2 * (c + 1)])
+        q_raw = [nested(f"q_raw{o}", F32, 4).rearrange("p (j n) -> p j n", j=4) for o in range(2)]
+        q_rows = qT[0].rearrange("(o p j) n -> o p j n", o=2, j=4)
+        nc.sync.dma_start(q_raw[0], q_rows[0])
         vs_pool = tile("zero", [P, T], F32)
         nc.gpsimd.memset(vs_pool[0 : P - 1, :].bitcast(I32), 0)
-        nc.sync.dma_start(q_raw[0][:], q_rows[0])
         nc.sync.dma_start(vs_pool[P - 1 : P, :], vs[0:1, :])
         k_pool = tile("k_pool", [P, T], I32)
         nc.sync.dma_start(k_pool[:], k_words[0].rearrange("p t b -> p (t b)").bitcast(I32))
@@ -77,202 +115,212 @@ def tile_attend_silu_kb_gate_topkq256n1024t2048_kernel(tc, qT, k_words, k_scales
             nc.scalar.copy(cols, bank[:, :, P - 1])
             return cols
 
-        s_got = tile("s_got", [P, N], U8)
-        nc.vector.tensor_copy(s_got[:], s_pool[:].indirect(offsets[:]))
+        def gather_row(pool, g, got):
+            nc.vector.tensor_copy(
+                got.bitcast(U32).rearrange("p (t b r) -> p b t r", t=4, r=8),
+                pool[:].bitcast(U32).indirect(offsets[:, 32 * g : 32 * (g + 1)]),
+            )
+            return got
+
+        s_got = tile("s_got", [P, N], U8)[:]
+        nc.vector.tensor_copy(s_got, s_pool[:].indirect(offsets[:]))
         kb_got = tile("kb_got", [P, N], F32)
         nc.vector.tensor_copy(
             kb_got[:].bitcast(U32).rearrange("p (g t b r) -> p g b t r", g=2, t=4, r=8),
             kb_pool[:].bitcast(U32).indirect(offsets[:]),
         )
-        kb_banks = [turn(kb_got[:, 512 * g : 512 * (g + 1)], f"turn{g}") for g in range(2)]
-
-        def gather_vs(g, vs_got, bank_name):
-            nc.vector.tensor_copy(
-                vs_got[:].bitcast(U32).rearrange("p (t b r) -> p b t r", t=4, r=8),
-                vs_pool[:].bitcast(U32).indirect(offsets[:, 32 * g : 32 * (g + 1)]),
-            )
-            return turn(vs_got, bank_name)
+        kb_banks = [turn(kb_got[:, 512 * g : 512 * (g + 1)], ("bank_a", "bank_c")[g]) for g in range(2)]
 
         v_pool = tile("v_pool", [P, T], BF16)
-        for half in range(2):
-            nc.scalar.copy(v_pool[:, T // 2 * half : T // 2 * (half + 1)], v_raw[half][:])
-
-        s_first = relay_tile("s_first", [P, N], U8, 0)
+        for c in range(2):
+            nc.scalar.copy(v_pool[:, T // 2 * c : T // 2 * (c + 1)], v_raw[c])
+        s_first = nested("s_first", U8, 1)
         nc.vector.tensor_copy(
-            s_first[:].bitcast(I32).rearrange("p (g t b w) -> p g t b w", g=2, t=4, w=2),
-            s_got[:].bitcast(I32).rearrange("p (g b t w) -> p g t b w", g=2, t=4, w=2),
+            s_first.bitcast(I32).rearrange("p (g t b w) -> p g t b w", g=2, t=4, w=2),
+            s_got.bitcast(I32).rearrange("p (g b t w) -> p g t b w", g=2, t=4, w=2),
         )
-        k_planes_all = tile("k_planes", [P, 2 * N + 4], U8)
-        nc.vector.memset(k_planes_all[:].bitcast(I32), 0)
-        k_planes = k_planes_all[:, 0 : 2 * N].rearrange("p (o n) -> p o n", o=2)
         for quad in range(4):
             nc.sync.dma_start(
                 k_planes[32 * quad : 32 * quad + 4].bitcast(I32),
                 s_first[96 + 8 * quad : 96 + 8 * quad + 8, :].bitcast(I32),
             )
+        vs_bank0 = turn(gather_row(vs_pool, 0, nested("vs_got0", F32, 4)), "bank_b")
 
-        vs_banks = [gather_vs(0, relay_tile("vs_got0", [P, 512], F32, 2048), "y0")]
+        q_bf = [tile(f"q_bf{o}", [P, NQ, 4], BF16) for o in range(2)]
+        q_codes = tile("q_codes", [P, 2 * NQ], U32)
+        q_plane = tile("q_plane", [P, 2 * NQ], U8)
+        v_got = [tile("v_got0", [P, 512], BF16)[:]]
+        v_bank = ps.tile([P, 2, 2, P], F32, name="bank_d")
 
-        q_bf = tile("s_got", [P, 2, NQ, 4], BF16)
-        nc.gpsimd.tensor_scalar(q_bf[:, 0], q_raw[0][:].rearrange("p t n -> p n t"), 1.0, 0.0, ALU.mult, ALU.add)
-
-        v_got = [tile(f"v_got{g}", [P, P, 4], BF16) for g in range(2)]
-        for g in range(2):
-            nc.scalar.activation(
-                v_got[g][:].rearrange("p (b r) t -> p b t r", r=8),
-                v_pool[:].indirect(offsets[:, 32 * g : 32 * (g + 1)]),
-                ACT.Copy,
-            )
-
-        nc.scalar.copy(
-            q_bf[:, 1].rearrange("p (c i) t -> p c t i", i=4),
-            q_raw[1].rearrange("p t (c i) -> p c t i", i=4),
-        )
-        kb_cols = [last_column(relay_tile(f"kb_cols{g}", [P, 4], F32, 11264 + 2048 * g)[:], kb_banks[g]) for g in range(2)]
-        vs_cols = last_column(relay_tile("vs_cols", [P, 4], F32, 12288)[:], vs_banks[0])
-
-        tanh = tile("q_raw0", [P, 2 * DV], F32)
-        nc.scalar.activation(tanh[:], og_sb[:].rearrange("p h e -> p (h e)"), ACT.Tanh, bias=silu0[:], scale=0.5)
-        v_bf = relay_tile("v_bf", [P, 2, DV, 4], BF16, 4096 + 4096)
-        v_bank = ps.tile([P, 2, 2, P], F32, name="y1")
-        for g in range(2):
-            pairs = v_got[g][:].bitcast(F32)
-            for u in range(2):
-                nc.tensor.transpose(v_bank[:, g, u, :], pairs[:, :, u], ident[:])
-        nc.scalar.copy(v_bf[:].bitcast(F32), v_bank[:].rearrange("p g u e -> p g e u"))
-        gate = tile("gate", [P, 2 * DV], F32)
-        nc.scalar.activation(gate[:], tanh[:], ACT.Copy, bias=1.0 / 32.0, scale=1.0 / 32.0)
-
-        k_got = {}
-        k_splits = [tile("k_split0", [P, 2048], U8), relay_tile("k_split1", [P, 2048], U8, 4096 + 2048)]
-
-        def gather_keys(quarter, got):
-            k_got[quarter] = got
-            nc.vector.tensor_copy(
-                k_got[quarter][:], k_pool[:].bitcast(U32).indirect(offsets[:, 16 * quarter : 16 * (quarter + 1)])
-            )
-
-        def split_keys(quarter):
-            g, half = divmod(quarter, 2)
-            nc.vector.tensor_copy(
-                k_splits[g][:].bitcast(U16).rearrange("p (o t b r) -> p o t b r", o=2, t=4, r=8)[
-                    :, :, :, 8 * half : 8 * (half + 1), :
-                ],
-                k_got[quarter][:].bitcast(U16).rearrange("p (b t r o) -> p o t b r", o=2, t=4, r=8),
+        def cast_queries(o):
+            nc.scalar.copy(
+                q_bf[o][:].rearrange("p (c i) t -> p c t i", i=4),
+                q_raw[o].rearrange("p t (c i) -> p c t i", i=4),
             )
 
         def quantise_queries(o):
             nc.vector.quantize_mx(
                 out=q_codes[:, NQ * o : NQ * (o + 1)].bitcast(FP8X4),
                 scales=q_plane[:, NQ * o : NQ * (o + 1)],
-                in_=q_bf[:, o].rearrange("p n t -> p (n t)"),
+                in_=q_bf[o][:].rearrange("p n t -> p (n t)"),
             )
 
-        for quarter in range(2):
-            gather_keys(quarter, tile(f"k_got{quarter}", [P, 256], U32))
-        for quarter in range(2):
-            split_keys(quarter)
-        q_codes = tile("k_got0", [P, 2 * NQ], U32)
-        q_plane = tile("q_plane", [P, 2 * NQ], U8)
+        def gather_values(g):
+            nc.scalar.activation(
+                v_got[g].rearrange("p (b r t) -> p b t r", r=8, t=4),
+                v_pool[:].indirect(offsets[:, 32 * g : 32 * (g + 1)]),
+                ACT.Copy,
+            )
+            pairs = v_got[g].bitcast(F32).rearrange("p (s u) -> p s u", u=2)
+            for u in range(2):
+                nc.tensor.transpose(v_bank[:, g, u, :], pairs[:, :, u], ident[:])
+
+        gather_values(0)
+        cast_queries(0)
         quantise_queries(0)
+        v_got.append(nested("v_got1", BF16, 2))
+        gather_values(1)
+        cast_queries(1)
+        kb_first = last_column(nested("kb_cols0", F32, 4)[:, 0:3], kb_banks[0][:, 0:3])
+        kb_last = last_column(nested("kb_last", F32, 4)[:, 0:1], kb_banks[0][:, 3:4])
+        kb_second = last_column(nested("kb_cols1", F32, 4)[:, 0:4], kb_banks[1])
+        kb_cols = [[kb_first[:, t : t + 1] for t in range(3)] + [kb_last], [kb_second[:, t : t + 1] for t in range(4)]]
+        vs_cols0 = last_column(nested("vs_cols0", F32, 4)[:, 0:4], vs_bank0)
+
+        k_got = {}
+        k_splits = [tile("k_split0", [P, 2048], U8)[:], nested("k_split1", U8, 1)]
+
+        def gather_keys(quarter, got):
+            k_got[quarter] = got
+            nc.vector.tensor_copy(got, k_pool[:].bitcast(U32).indirect(offsets[:, 16 * quarter : 16 * (quarter + 1)]))
+
+        def split_keys(quarter):
+            g, half = divmod(quarter, 2)
+            nc.vector.tensor_copy(
+                k_splits[g].bitcast(U16).rearrange("p (o t b r) -> p o t b r", o=2, t=4, r=8)[
+                    :, :, :, 8 * half : 8 * (half + 1), :
+                ],
+                k_got[quarter].bitcast(U16).rearrange("p (b t r o) -> p o t b r", o=2, t=4, r=8),
+            )
+
+        def score_tile(g, t, scores, passes):
+            for h, o in passes:
+                if True:
+                    k0 = 1024 * o + 256 * t
+                    s0 = 512 * g + 128 * t
+                    q0 = NQ * o + 128 * h
+                    nc.tensor.matmul_mx(
+                        out=scores[:, 128 * h : 128 * (h + 1)],
+                        lhsT=k_splits[g][:, k0 : k0 + 256].bitcast(FP4X4),
+                        lhsT_scale=k_planes[:, o, s0 : s0 + 128],
+                        rhs=q_codes[:, q0 : q0 + 128].bitcast(FP8X4),
+                        rhs_scale=q_plane[:, q0 : q0 + 128],
+                        start=(o == 0),
+                        stop=(o == 1),
+                    )
+            return scores
+
+        def silu(p_g, scores, g, t, q0, q1):
+            nc.scalar.activation(
+                p_g[:, q0 // 4 : q1 // 4, t, :],
+                scores[:, q0:q1].rearrange("p (c i) -> p c i", i=4),
+                ACT.Silu,
+                bias=kb_cols[g][t],
+            )
+
+        warm = ps.tile([P, 2, NQ], F32, name="score3")
+        for i in range(4):
+            nc.tensor.matmul_mx(
+                out=warm[:, i % 2, :],
+                lhsT=q_codes[:, 128 * (i % 2) : 128 * (i % 2 + 1)].bitcast(FP8X4),
+                lhsT_scale=q_plane[:, 128 * (i % 2) : 128 * (i % 2 + 1)],
+                rhs=q_codes[:, 0:NQ].bitcast(FP8X4),
+                rhs_scale=q_plane[:, 0:NQ],
+                start=True,
+                stop=True,
+            )
+        gather_keys(0, nested("k_got0", U32, 4))
+        gather_keys(1, nested("k_got1", U32, 4))
+        split_keys(0)
+        split_keys(1)
+        gather_keys(2, nested("k_got2", U32, 4))
         quantise_queries(1)
-        gather_keys(2, relay_tile("k_got2", [P, 1536], U32, 4096 + 9728)[:, 0:256])
-        gather_keys(3, relay_tile("k_got3", [P, 256], U32, 4096))
-        for quarter in range(2, 4):
-            split_keys(quarter)
+        gather_keys(3, nested("k_got3", U32, 4))
+        split_keys(2)
+        split_keys(3)
+        vs_got1 = gather_row(vs_pool, 1, nested("vs_got1", F32, 4))
 
-        p_f32 = []
-        score_banks = [[f"score{t}" for t in range(4)], ["turn0", "turn1", "y1", "score0"]]
-        for g in range(2):
-            k_split = k_splits[g]
-            p_g = tile(f"p{g}", [P, NQ // 4, 4, 4], F32)
-            scores = [ps.tile([P, NQ], F32, name=score_banks[g][t]) for t in range(4)]
+        p0 = nested("p0", F32, 4).rearrange("p (c t i) -> p c t i", t=4, i=4)
+        scores = [ps.tile([P, NQ], F32, name=f"score{t}") for t in range(4)]
+        for t in range(4):
+            score_tile(0, t, scores[t], [(0, 0)])
+        for t in range(4):
+            score_tile(0, t, scores[t], [(0, 1), (1, 0), (1, 1)])
+            silu(p0, scores[t], 0, t, 0, NQ)
+        v_bf = nested("v_bf", BF16, 2)
+        nc.scalar.copy(v_bf.bitcast(F32).rearrange("p (g e u) -> p g e u", g=2, u=2), v_bank[:].rearrange("p g u e -> p g e u"))
+        scores = [ps.tile([P, NQ], F32, name=("bank_a", "bank_c", "score0", "score1")[t]) for t in range(4)]
+        for t in range(4):
+            score_tile(1, t, scores[t], [(0, 0), (0, 1), (1, 0), (1, 1)])
+        p1 = tile("p1", [P, NQ // 4, 4, 4], F32)[:]
+        for t in range(4):
+            silu(p1, scores[t], 1, t, 0, NQ)
+        vs_bank1 = turn(vs_got1, "score2")
 
-            def score_pass(t, h, o):
-                k0 = 1024 * o + 256 * t
-                s0 = 512 * g + 128 * t
-                q0 = NQ * o + 128 * h
-                nc.tensor.matmul_mx(
-                    out=scores[t][:, 128 * h : 128 * (h + 1)],
-                    lhsT=k_split[:, k0 : k0 + 256].bitcast(FP4X4),
-                    lhsT_scale=k_planes[:, o, s0 : s0 + 128],
-                    rhs=q_codes[:, q0 : q0 + 128].bitcast(FP8X4),
-                    rhs_scale=q_plane[:, q0 : q0 + 128],
-                    start=(o == 0),
-                    stop=(o == 1),
-                )
+        w_bf0 = tile("w_bf0", [P, 4 * NQ], BF16)[:]
+        nc.vector.tensor_tensor(
+            w_bf0[:, 0 : 4 * VECTOR_QUERIES].rearrange("p (c i t) -> p c t i", i=4, t=4),
+            p0[:, 0 : VECTOR_QUERIES // 4],
+            vs_bank0[:, :, P - 1].unsqueeze(1).unsqueeze(3).to_broadcast([P, VECTOR_QUERIES // 4, 4, 4]),
+            ALU.mult,
+        )
+        w_places = nested("w_places", BF16, 2)[:, 0 : 4 * (NQ - VECTOR_QUERIES)].rearrange("p (t c i) -> p t c i", t=4, i=4)
+        for t in range(4):
+            nc.scalar.activation(w_places[:, t], p0[:, VECTOR_QUERIES // 4 :, t, :], ACT.Copy, scale=vs_cols0[:, t : t + 1])
+        tanh = nested("tanh", F32, 4)
+        nc.scalar.activation(tanh, og_sb[:].rearrange("p h e -> p (h e)"), ACT.Tanh, bias=silu0[:], scale=0.5)
+        nc.scalar.copy(
+            w_bf0[:, 4 * VECTOR_QUERIES :].rearrange("p (c i t) -> p c t i", i=4, t=4),
+            w_places.rearrange("p t c i -> p c t i"),
+        )
+        gate = tile("gate", [P, 2 * DV], F32)
+        nc.scalar.activation(gate[:], tanh, ACT.Copy, bias=1.0 / 32.0, scale=1.0 / 32.0)
+        v_codes = tile("s_got", [P, 2 * DV], U32)[:]
+        v_plane = tile("v_plane", [P, 2 * DV], U8)
+        nc.vector.quantize_mx(out=v_codes.bitcast(FP8X4), scales=v_plane[:], in_=v_bf)
+        w_codes = [tile(f"w_codes{g}", [P, NQ], U32) for g in range(2)]
+        w_plane = [tile(f"w_plane{g}", [P, NQ], U8) for g in range(2)]
+        w_bf = [w_bf0, tile("w_bf1", [P, 4 * NQ], BF16)[:]]
 
-            if g == 0:
-                for t in range(4):
-                    score_pass(t, 0, 0)
-            for t in range(4):
-                if g == 1:
-                    score_pass(t, 0, 0)
-                score_pass(t, 0, 1)
-                score_pass(t, 1, 0)
-                score_pass(t, 1, 1)
-                nc.scalar.activation(
-                    p_g[:, :, t, :],
-                    scores[t][:].rearrange("p (c i) -> p c i", i=4),
-                    ACT.Silu,
-                    bias=kb_cols[g][:, t : t + 1],
-                )
-            p_f32.append(p_g)
-
-        vs_banks.append(gather_vs(1, relay_tile("vs_got1", [P, 512], F32, 16384), "score1"))
-
-        w_bf = [tile(f"w_bf{g}", [P, NQ, 4], BF16) for g in range(2)]
-        w_codes = {}
-        w_plane = {}
-
-        def weigh(g, q0, q1):
+        def weigh(h):
             nc.vector.tensor_tensor(
-                w_bf[g][:, q0:q1].rearrange("p (c i) t -> p c t i", i=4),
-                p_f32[g][:, q0 // 4 : q1 // 4],
-                vs_banks[g][:, :, P - 1].unsqueeze(1).unsqueeze(3).to_broadcast([P, (q1 - q0) // 4, 4, 4]),
+                w_bf[1][:, 512 * h : 512 * (h + 1)].rearrange("p (c i t) -> p c t i", i=4, t=4),
+                p1[:, 32 * h : 32 * (h + 1)],
+                vs_bank1[:, :, P - 1].unsqueeze(1).unsqueeze(3).to_broadcast([P, 32, 4, 4]),
                 ALU.mult,
             )
 
-        def quantise_weights(g, h, name):
-            w_codes[g, h] = tile(name, [P, 128], U32)
-            w_plane[g, h] = tile(f"w_plane{g}{h}", [P, 128], U8)
+        def quantise_weights(g, h):
             nc.vector.quantize_mx(
-                out=w_codes[g, h][:].bitcast(FP8X4),
-                scales=w_plane[g, h][:],
-                in_=w_bf[g][:, 128 * h : 128 * (h + 1)].rearrange("p n t -> p (n t)"),
+                out=w_codes[g][:, 128 * h : 128 * (h + 1)].bitcast(FP8X4),
+                scales=w_plane[g][:, 128 * h : 128 * (h + 1)],
+                in_=w_bf[g][:, 512 * h : 512 * (h + 1)],
             )
 
-        weigh(0, 0, VECTOR_QUERIES)
-        v_codes = relay_tile("v_codes", [P, 2 * DV], U32, 11264)
-        v_plane = tile("v_plane", [P, 2 * DV], U8)
-        nc.vector.quantize_mx(out=v_codes[:].bitcast(FP8X4), scales=v_plane[:], in_=v_bf[:].rearrange("p g e t -> p (g e t)"))
-        w_places = relay_tile("w_places", [P, 4, NQ - VECTOR_QUERIES], BF16, 16384)
-        for t in range(4):
-            nc.scalar.activation(
-                w_places[:, t, :].rearrange("p (c i) -> p c i", i=4),
-                p_f32[0][:, VECTOR_QUERIES // 4 :, t, :],
-                ACT.Copy,
-                scale=vs_cols[:, t : t + 1],
-            )
-        nc.scalar.copy(
-            w_bf[0][:, VECTOR_QUERIES:].rearrange("p (c i) t -> p c t i", i=4),
-            w_places[:].rearrange("p t (c i) -> p c t i", i=4),
-        )
-
-        weigh(1, 0, 128)
-        weigh(1, 128, NQ)
-        quantise_weights(0, 0, "w_codes00")
-        quantise_weights(1, 0, "w_codes10")
-        quantise_weights(0, 1, "p1")
-        quantise_weights(1, 1, "w_codes11")
+        weigh(0)
+        weigh(1)
+        quantise_weights(0, 0)
+        quantise_weights(1, 0)
+        quantise_weights(0, 1)
+        quantise_weights(1, 1)
 
         for h in range(2):
-            y = ps.tile([P, DV], F32, name=f"score{2 + h}")
+            y = ps.tile([P, DV], F32, name=("score3", "bank_d")[h])
             for g in range(2):
                 nc.tensor.matmul_mx(
                     out=y[:],
-                    lhsT=w_codes[g, h][:].bitcast(FP8X4),
-                    lhsT_scale=w_plane[g, h][:],
+                    lhsT=w_codes[g][:, 128 * h : 128 * (h + 1)].bitcast(FP8X4),
+                    lhsT_scale=w_plane[g][:, 128 * h : 128 * (h + 1)],
                     rhs=v_codes[:, DV * g : DV * (g + 1)].bitcast(FP8X4),
                     rhs_scale=v_plane[:, DV * g : DV * (g + 1)],
                     start=(g == 0),

@@ -21,26 +21,27 @@ P = 128
 VECTOR_QUERIES = 160
 
 NESTED = {
+    "v_raw0": (4096, None),
+    "s_first": (1024, "v_raw0"),
+    "kb_got1": (2048, "v_raw0"),
     "v_raw1": (4096, None),
-    "s_first": (1024, "v_raw1"),
     "vs_got0": (2048, "v_raw1"),
-    "q_raw0": (4096, None),
-    "v_got1": (1024, "q_raw0"),
-    "k_got0": (1024, "q_raw0"),
-    "k_got2": (1024, "k_got0"),
+    "s_got": (1024, None),
+    "q_bf0": (2048, "s_got"),
+    "k_got0": (1024, None),
+    "q_codes": (2048, "k_got0"),
+    "q_raw1": (4096, None),
+    "k_got2": (1024, "q_raw1"),
     "vs_got1": (2048, "k_got2"),
     "w_places": (1024, "vs_got1"),
-    "tanh": (1024, "vs_got1"),
-    "k_got1": (1024, "q_raw0"),
-    "q_raw1": (4096, None),
-    "k_split1": (2048, "q_raw1"),
     "k_got3": (1024, "q_raw1"),
-    "vs_cols0": (64, "q_raw1"),
+    "k_split1": (2048, "q_raw1"),
     "kb_cols0": (64, "q_raw1"),
-    "v_bf": (2048, "kb_cols0"),
+    "v_codes": (1024, "kb_cols0"),
     "kb_cols1": (64, "q_raw1"),
-    "kb_last": (64, "q_raw1"),
-    "p0": (4096, "q_raw1"),
+    "vs_cols0": (64, "q_raw1"),
+    "tanh": (1024, "q_raw1"),
+    "v_bf": (2048, "q_raw1"),
 }
 
 
@@ -90,10 +91,10 @@ def tile_attend_silu_kb_gate_topkq256n1024t2048_kernel(tc, qT, k_words, k_scales
         ident = tile("ident", [P, P], F32)
         make_identity(nc, ident[:])
 
-        v_raw = [tile("v_raw0", [P, T // 2], F32)[:], nested("v_raw1", F32, 4)]
+        v_raw = [nested(f"v_raw{c}", F32, 4) for c in range(2)]
         for c in range(2):
             nc.sync.dma_start(v_raw[c], vT[:, T // 2 * c : T // 2 * (c + 1)])
-        q_raw = [nested(f"q_raw{o}", F32, 4).rearrange("p (j n) -> p j n", j=4) for o in range(2)]
+        q_raw = [tile("q_raw0", [P, 4, NQ], F32)[:], nested("q_raw1", F32, 4).rearrange("p (j n) -> p j n", j=4)]
         q_rows = qT[0].rearrange("(o p j) n -> o p j n", o=2, j=4)
         nc.sync.dma_start(q_raw[0], q_rows[0])
         vs_pool = tile("zero", [P, T], F32)
@@ -102,8 +103,8 @@ def tile_attend_silu_kb_gate_topkq256n1024t2048_kernel(tc, qT, k_words, k_scales
         k_pool = tile("k_pool", [P, T], I32)
         nc.sync.dma_start(k_pool[:], k_words[0].rearrange("p t b -> p (t b)").bitcast(I32))
         nc.sync.dma_start(q_raw[1], q_rows[1])
-        og_sb = tile("og_sb", [P, 2, DV], F32)
-        nc.sync.dma_start(og_sb[:], og[0].rearrange("(h p) e -> p h e", h=2))
+        og_sb = tile("og_sb", [P, 2 * DV], F32)[:]
+        nc.sync.dma_start(og_sb.rearrange("p (h e) -> p h e", h=2), og[0].rearrange("(h p) e -> p h e", h=2))
 
         def turn(got, bank_name):
             bank = ps.tile([P, 4, P], F32, name=bank_name)
@@ -122,14 +123,9 @@ def tile_attend_silu_kb_gate_topkq256n1024t2048_kernel(tc, qT, k_words, k_scales
             )
             return got
 
-        s_got = tile("s_got", [P, N], U8)[:]
+        s_got = nested("s_got", U8, 1)
         nc.vector.tensor_copy(s_got, s_pool[:].indirect(offsets[:]))
-        kb_got = tile("kb_got", [P, N], F32)
-        nc.vector.tensor_copy(
-            kb_got[:].bitcast(U32).rearrange("p (g t b r) -> p g b t r", g=2, t=4, r=8),
-            kb_pool[:].bitcast(U32).indirect(offsets[:]),
-        )
-        kb_banks = [turn(kb_got[:, 512 * g : 512 * (g + 1)], ("bank_a", "bank_c")[g]) for g in range(2)]
+        kb_banks = [turn(gather_row(kb_pool, 0, tile("kb_got0", [P, 512], F32)[:]), "bank_a")]
 
         v_pool = tile("v_pool", [P, T], BF16)
         for c in range(2):
@@ -144,17 +140,18 @@ def tile_attend_silu_kb_gate_topkq256n1024t2048_kernel(tc, qT, k_words, k_scales
                 k_planes[32 * quad : 32 * quad + 4].bitcast(I32),
                 s_first[96 + 8 * quad : 96 + 8 * quad + 8, :].bitcast(I32),
             )
+        kb_banks.append(turn(gather_row(kb_pool, 1, nested("kb_got1", F32, 4)), "bank_c"))
         vs_bank0 = turn(gather_row(vs_pool, 0, nested("vs_got0", F32, 4)), "bank_b")
 
-        q_bf = [tile(f"q_bf{o}", [P, NQ, 4], BF16) for o in range(2)]
-        q_codes = tile("q_codes", [P, 2 * NQ], U32)
+        q_bf = [nested("q_bf0", BF16, 2).rearrange("p (n t) -> p n t", t=4), tile("q_bf1", [P, NQ, 4], BF16)[:]]
+        nc.gpsimd.tensor_scalar(q_bf[0], q_raw[0].rearrange("p t n -> p n t"), 1.0, 0.0, ALU.mult, ALU.add)
         q_plane = tile("q_plane", [P, 2 * NQ], U8)
-        v_got = [tile("v_got0", [P, 512], BF16)[:]]
+        v_got = [tile(f"v_got{g}", [P, 512], BF16)[:] for g in range(2)]
         v_bank = ps.tile([P, 2, 2, P], F32, name="bank_d")
 
         def cast_queries(o):
             nc.scalar.copy(
-                q_bf[o][:].rearrange("p (c i) t -> p c t i", i=4),
+                q_bf[o].rearrange("p (c i) t -> p c t i", i=4),
                 q_raw[o].rearrange("p t (c i) -> p c t i", i=4),
             )
 
@@ -162,7 +159,7 @@ def tile_attend_silu_kb_gate_topkq256n1024t2048_kernel(tc, qT, k_words, k_scales
             nc.vector.quantize_mx(
                 out=q_codes[:, NQ * o : NQ * (o + 1)].bitcast(FP8X4),
                 scales=q_plane[:, NQ * o : NQ * (o + 1)],
-                in_=q_bf[o][:].rearrange("p n t -> p (n t)"),
+                in_=q_bf[o].rearrange("p n t -> p (n t)"),
             )
 
         def gather_values(g):
@@ -176,16 +173,18 @@ def tile_attend_silu_kb_gate_topkq256n1024t2048_kernel(tc, qT, k_words, k_scales
                 nc.tensor.transpose(v_bank[:, g, u, :], pairs[:, :, u], ident[:])
 
         gather_values(0)
-        cast_queries(0)
-        quantise_queries(0)
-        v_got.append(nested("v_got1", BF16, 2))
         gather_values(1)
         cast_queries(1)
-        kb_first = last_column(nested("kb_cols0", F32, 4)[:, 0:3], kb_banks[0][:, 0:3])
-        kb_last = last_column(nested("kb_last", F32, 4)[:, 0:1], kb_banks[0][:, 3:4])
-        kb_second = last_column(nested("kb_cols1", F32, 4)[:, 0:4], kb_banks[1])
-        kb_cols = [[kb_first[:, t : t + 1] for t in range(3)] + [kb_last], [kb_second[:, t : t + 1] for t in range(4)]]
+        kb_all = [last_column(nested(f"kb_cols{g}", F32, 4)[:, 0:4], kb_banks[g]) for g in range(2)]
+        kb_cols = [[kb_all[g][:, t : t + 1] for t in range(4)] for g in range(2)]
         vs_cols0 = last_column(nested("vs_cols0", F32, 4)[:, 0:4], vs_bank0)
+
+        tanh = nested("tanh", F32, 4)
+        nc.scalar.activation(tanh, og_sb, ACT.Tanh, bias=silu0[:], scale=0.5)
+        v_bf = nested("v_bf", BF16, 2)
+        nc.scalar.copy(v_bf.bitcast(F32).rearrange("p (g e u) -> p g e u", g=2, u=2), v_bank[:].rearrange("p g u e -> p g e u"))
+        gate = tile("gate", [P, 2 * DV], F32)
+        nc.scalar.activation(gate[:], tanh, ACT.Copy, bias=1.0 / 32.0, scale=1.0 / 32.0)
 
         k_got = {}
         k_splits = [tile("k_split0", [P, 2048], U8)[:], nested("k_split1", U8, 1)]
@@ -228,37 +227,26 @@ def tile_attend_silu_kb_gate_topkq256n1024t2048_kernel(tc, qT, k_words, k_scales
                 bias=kb_cols[g][t],
             )
 
-        warm = ps.tile([P, 2, NQ], F32, name="score3")
-        for i in range(4):
-            nc.tensor.matmul_mx(
-                out=warm[:, i % 2, :],
-                lhsT=q_codes[:, 128 * (i % 2) : 128 * (i % 2 + 1)].bitcast(FP8X4),
-                lhsT_scale=q_plane[:, 128 * (i % 2) : 128 * (i % 2 + 1)],
-                rhs=q_codes[:, 0:NQ].bitcast(FP8X4),
-                rhs_scale=q_plane[:, 0:NQ],
-                start=True,
-                stop=True,
-            )
         gather_keys(0, nested("k_got0", U32, 4))
-        gather_keys(1, nested("k_got1", U32, 4))
+        gather_keys(1, tile("k_got1", [P, 256], U32)[:])
         split_keys(0)
         split_keys(1)
-        gather_keys(2, nested("k_got2", U32, 4))
+        q_codes = nested("q_codes", U32, 4)
+        quantise_queries(0)
         quantise_queries(1)
+        gather_keys(2, nested("k_got2", U32, 4))
         gather_keys(3, nested("k_got3", U32, 4))
         split_keys(2)
         split_keys(3)
         vs_got1 = gather_row(vs_pool, 1, nested("vs_got1", F32, 4))
 
-        p0 = nested("p0", F32, 4).rearrange("p (c t i) -> p c t i", t=4, i=4)
+        p0 = tile("p0", [P, NQ // 4, 4, 4], F32)[:]
         scores = [ps.tile([P, NQ], F32, name=f"score{t}") for t in range(4)]
         for t in range(4):
             score_tile(0, t, scores[t], [(0, 0)])
         for t in range(4):
             score_tile(0, t, scores[t], [(0, 1), (1, 0), (1, 1)])
             silu(p0, scores[t], 0, t, 0, NQ)
-        v_bf = nested("v_bf", BF16, 2)
-        nc.scalar.copy(v_bf.bitcast(F32).rearrange("p (g e u) -> p g e u", g=2, u=2), v_bank[:].rearrange("p g u e -> p g e u"))
         scores = [ps.tile([P, NQ], F32, name=("bank_a", "bank_c", "score0", "score1")[t]) for t in range(4)]
         for t in range(4):
             score_tile(1, t, scores[t], [(0, 0), (0, 1), (1, 0), (1, 1)])
@@ -277,15 +265,11 @@ def tile_attend_silu_kb_gate_topkq256n1024t2048_kernel(tc, qT, k_words, k_scales
         w_places = nested("w_places", BF16, 2)[:, 0 : 4 * (NQ - VECTOR_QUERIES)].rearrange("p (t c i) -> p t c i", t=4, i=4)
         for t in range(4):
             nc.scalar.activation(w_places[:, t], p0[:, VECTOR_QUERIES // 4 :, t, :], ACT.Copy, scale=vs_cols0[:, t : t + 1])
-        tanh = nested("tanh", F32, 4)
-        nc.scalar.activation(tanh, og_sb[:].rearrange("p h e -> p (h e)"), ACT.Tanh, bias=silu0[:], scale=0.5)
         nc.scalar.copy(
             w_bf0[:, 4 * VECTOR_QUERIES :].rearrange("p (c i t) -> p c t i", i=4, t=4),
             w_places.rearrange("p t c i -> p c t i"),
         )
-        gate = tile("gate", [P, 2 * DV], F32)
-        nc.scalar.activation(gate[:], tanh, ACT.Copy, bias=1.0 / 32.0, scale=1.0 / 32.0)
-        v_codes = tile("s_got", [P, 2 * DV], U32)[:]
+        v_codes = nested("v_codes", U32, 4)
         v_plane = tile("v_plane", [P, 2 * DV], U8)
         nc.vector.quantize_mx(out=v_codes.bitcast(FP8X4), scales=v_plane[:], in_=v_bf)
         w_codes = [tile(f"w_codes{g}", [P, NQ], U32) for g in range(2)]

@@ -18,7 +18,7 @@ FP4X4 = mybir.dt.float4_e2m1fn_x4
 ACT = mybir.ActivationFunctionType
 ALU = mybir.AluOpType
 P = 128
-VECTOR_QUERIES = 160
+VECTOR_QUERIES = 128
 
 NESTED = {
     "v_raw0": (4096, None),
@@ -33,7 +33,6 @@ NESTED = {
     "q_raw1": (4096, None),
     "k_got2": (1024, "q_raw1"),
     "vs_got1": (2048, "k_got2"),
-    "w_places": (1024, "vs_got1"),
     "k_got3": (1024, "q_raw1"),
     "k_split1": (2048, "q_raw1"),
     "kb_cols0": (64, "q_raw1"),
@@ -262,12 +261,11 @@ def tile_attend_silu_kb_gate_topkq256n1024t2048_kernel(tc, qT, k_words, k_scales
             vs_bank0[:, :, P - 1].unsqueeze(1).unsqueeze(3).to_broadcast([P, VECTOR_QUERIES // 4, 4, 4]),
             ALU.mult,
         )
-        w_places = nested("w_places", BF16, 2)[:, 0 : 4 * (NQ - VECTOR_QUERIES)].rearrange("p (t c i) -> p t c i", t=4, i=4)
-        for t in range(4):
-            nc.scalar.activation(w_places[:, t], p0[:, VECTOR_QUERIES // 4 :, t, :], ACT.Copy, scale=vs_cols0[:, t : t + 1])
-        nc.scalar.copy(
-            w_bf0[:, 4 * VECTOR_QUERIES :].rearrange("p (c i t) -> p c t i", i=4, t=4),
-            w_places.rearrange("p t c i -> p c t i"),
+        nc.gpsimd.tensor_tensor(
+            w_bf0[:, 4 * VECTOR_QUERIES :].rearrange("p (c i t) -> p c i t", i=4, t=4),
+            p0[:, VECTOR_QUERIES // 4 :].rearrange("p c t i -> p c i t"),
+            vs_cols0.unsqueeze(1).unsqueeze(1).to_broadcast([P, (NQ - VECTOR_QUERIES) // 4, 4, 4]),
+            ALU.mult,
         )
         v_codes = nested("v_codes", U32, 4)
         v_plane = tile("v_plane", [P, 2 * DV], U8)
@@ -291,11 +289,11 @@ def tile_attend_silu_kb_gate_topkq256n1024t2048_kernel(tc, qT, k_words, k_scales
                 in_=w_bf[g][:, 512 * h : 512 * (h + 1)],
             )
 
+        quantise_weights(0, 0)
+        quantise_weights(0, 1)
         weigh(0)
         weigh(1)
-        quantise_weights(0, 0)
         quantise_weights(1, 0)
-        quantise_weights(0, 1)
         quantise_weights(1, 1)
 
         for h in range(2):

@@ -18,7 +18,6 @@ FP4X4 = mybir.dt.float4_e2m1fn_x4
 ACT = mybir.ActivationFunctionType
 ALU = mybir.AluOpType
 P = 128
-VECTOR_QUERIES = 128
 
 NESTED = {
     "v_raw0": (4096, None),
@@ -34,6 +33,7 @@ NESTED = {
     "k_got2": (1024, "q_raw1"),
     "vs_got1": (2048, "k_got2"),
     "k_got3": (1024, "q_raw1"),
+    "w_first": (1024, "k_got3"),
     "k_split1": (2048, "q_raw1"),
     "kb_cols0": (64, "q_raw1"),
     "v_codes": (1024, "kb_cols0"),
@@ -244,27 +244,31 @@ def tile_attend_silu_kb_gate_topkq256n1024t2048_kernel(tc, qT, k_words, k_scales
         for t in range(4):
             score_tile(0, t, scores[t], [(0, 0)])
         for t in range(4):
-            score_tile(0, t, scores[t], [(0, 1), (1, 0), (1, 1)])
-            silu(p0, scores[t], 0, t, 0, NQ)
-        scores = [ps.tile([P, NQ], F32, name=("bank_a", "bank_c", "score0", "score1")[t]) for t in range(4)]
+            score_tile(0, t, scores[t], [(0, 1)])
+            silu(p0, scores[t], 0, t, 0, 128)
+        scores = [ps.tile([P, NQ], F32, name=("bank_a", "bank_c", "bank_d", "score0")[t]) for t in range(4)]
+        for t in range(4):
+            score_tile(0, t, scores[t], [(1, 0), (1, 1)])
+            silu(p0, scores[t], 0, t, 128, NQ)
+        scores = [ps.tile([P, NQ], F32, name=("score1", "score2", "score3", "bank_a")[t]) for t in range(4)]
         for t in range(4):
             score_tile(1, t, scores[t], [(0, 0), (0, 1), (1, 0), (1, 1)])
         p1 = tile("p1", [P, NQ // 4, 4, 4], F32)[:]
         for t in range(4):
             silu(p1, scores[t], 1, t, 0, NQ)
-        vs_bank1 = turn(vs_got1, "score2")
+        vs_bank1 = turn(vs_got1, "bank_c")
 
-        w_bf0 = tile("w_bf0", [P, 4 * NQ], BF16)[:]
-        nc.vector.tensor_tensor(
-            w_bf0[:, 0 : 4 * VECTOR_QUERIES].rearrange("p (c i t) -> p c t i", i=4, t=4),
-            p0[:, 0 : VECTOR_QUERIES // 4],
-            vs_bank0[:, :, P - 1].unsqueeze(1).unsqueeze(3).to_broadcast([P, VECTOR_QUERIES // 4, 4, 4]),
+        w_bf0 = [nested("w_first", BF16, 2), tile("w_second", [P, 512], BF16)[:]]
+        nc.gpsimd.tensor_tensor(
+            w_bf0[0].rearrange("p (c i t) -> p c i t", i=4, t=4),
+            p0[:, 0:32].rearrange("p c t i -> p c i t"),
+            vs_cols0.unsqueeze(1).unsqueeze(1).to_broadcast([P, 32, 4, 4]),
             ALU.mult,
         )
-        nc.gpsimd.tensor_tensor(
-            w_bf0[:, 4 * VECTOR_QUERIES :].rearrange("p (c i t) -> p c i t", i=4, t=4),
-            p0[:, VECTOR_QUERIES // 4 :].rearrange("p c t i -> p c i t"),
-            vs_cols0.unsqueeze(1).unsqueeze(1).to_broadcast([P, (NQ - VECTOR_QUERIES) // 4, 4, 4]),
+        nc.vector.tensor_tensor(
+            w_bf0[1].rearrange("p (c i t) -> p c t i", i=4, t=4),
+            p0[:, 32:64],
+            vs_bank0[:, :, P - 1].unsqueeze(1).unsqueeze(3).to_broadcast([P, 32, 4, 4]),
             ALU.mult,
         )
         v_codes = nested("v_codes", U32, 4)
@@ -272,11 +276,11 @@ def tile_attend_silu_kb_gate_topkq256n1024t2048_kernel(tc, qT, k_words, k_scales
         nc.vector.quantize_mx(out=v_codes.bitcast(FP8X4), scales=v_plane[:], in_=v_bf)
         w_codes = [tile(f"w_codes{g}", [P, NQ], U32) for g in range(2)]
         w_plane = [tile(f"w_plane{g}", [P, NQ], U8) for g in range(2)]
-        w_bf = [w_bf0, tile("w_bf1", [P, 4 * NQ], BF16)[:]]
+        w_bf = [w_bf0, [tile(f"w_bf1{h}", [P, 512], BF16)[:] for h in range(2)]]
 
         def weigh(h):
             nc.vector.tensor_tensor(
-                w_bf[1][:, 512 * h : 512 * (h + 1)].rearrange("p (c i t) -> p c t i", i=4, t=4),
+                w_bf[1][h].rearrange("p (c i t) -> p c t i", i=4, t=4),
                 p1[:, 32 * h : 32 * (h + 1)],
                 vs_bank1[:, :, P - 1].unsqueeze(1).unsqueeze(3).to_broadcast([P, 32, 4, 4]),
                 ALU.mult,
@@ -286,18 +290,18 @@ def tile_attend_silu_kb_gate_topkq256n1024t2048_kernel(tc, qT, k_words, k_scales
             nc.vector.quantize_mx(
                 out=w_codes[g][:, 128 * h : 128 * (h + 1)].bitcast(FP8X4),
                 scales=w_plane[g][:, 128 * h : 128 * (h + 1)],
-                in_=w_bf[g][:, 512 * h : 512 * (h + 1)],
+                in_=w_bf[g][h],
             )
 
-        quantise_weights(0, 0)
         quantise_weights(0, 1)
+        quantise_weights(0, 0)
         weigh(0)
         weigh(1)
         quantise_weights(1, 0)
         quantise_weights(1, 1)
 
         for h in range(2):
-            y = ps.tile([P, DV], F32, name=("score3", "bank_d")[h])
+            y = ps.tile([P, DV], F32, name=("score0", "bank_d")[h])
             for g in range(2):
                 nc.tensor.matmul_mx(
                     out=y[:],

@@ -18,6 +18,7 @@ FP4X4 = mybir.dt.float4_e2m1fn_x4
 ACT = mybir.ActivationFunctionType
 ALU = mybir.AluOpType
 P = 128
+GPSIMD_QUERIES = 96
 
 NESTED = {
     "v_raw0": (4096, None),
@@ -27,8 +28,8 @@ NESTED = {
     "vs_got0": (2048, "v_raw1"),
     "s_got": (1024, None),
     "q_bf0": (2048, "s_got"),
-    "k_got0": (1024, None),
-    "q_codes": (2048, "k_got0"),
+    "q_raw0": (4096, None),
+    "k_got0": (2048, "q_raw0"),
     "q_raw1": (4096, None),
     "k_got2": (1024, "q_raw1"),
     "vs_got1": (2048, "k_got2"),
@@ -93,7 +94,7 @@ def tile_attend_silu_kb_gate_topkq256n1024t2048_kernel(tc, qT, k_words, k_scales
         v_raw = [nested(f"v_raw{c}", F32, 4) for c in range(2)]
         for c in range(2):
             nc.sync.dma_start(v_raw[c], vT[:, T // 2 * c : T // 2 * (c + 1)])
-        q_raw = [tile("q_raw0", [P, 4, NQ], F32)[:], nested("q_raw1", F32, 4).rearrange("p (j n) -> p j n", j=4)]
+        q_raw = [nested(f"q_raw{o}", F32, 4).rearrange("p (j n) -> p j n", j=4) for o in range(2)]
         q_rows = qT[0].rearrange("(o p j) n -> o p j n", o=2, j=4)
         nc.sync.dma_start(q_raw[0], q_rows[0])
         vs_pool = tile("zero", [P, T], F32)
@@ -226,12 +227,14 @@ def tile_attend_silu_kb_gate_topkq256n1024t2048_kernel(tc, qT, k_words, k_scales
                 bias=kb_cols[g][t],
             )
 
-        gather_keys(0, nested("k_got0", U32, 4))
-        gather_keys(1, tile("k_got1", [P, 256], U32)[:])
-        split_keys(0)
-        split_keys(1)
-        q_codes = nested("q_codes", U32, 4)
+        q_codes = tile("q_codes", [P, 2 * NQ], U32)[:]
+        k_got0 = nested("k_got0", U32, 4)
+        nc.vector.tensor_copy(k_got0, k_pool[:].bitcast(U32).indirect(offsets[:, 0:32]))
         quantise_queries(0)
+        nc.vector.tensor_copy(
+            k_splits[0].bitcast(U16).rearrange("p (o t b r) -> p o t b r", o=2, t=4, r=8),
+            k_got0.bitcast(U16).rearrange("p (b t r o) -> p o t b r", o=2, t=4, r=8),
+        )
         quantise_queries(1)
         gather_keys(2, nested("k_got2", U32, 4))
         gather_keys(3, nested("k_got3", U32, 4))
@@ -246,10 +249,18 @@ def tile_attend_silu_kb_gate_topkq256n1024t2048_kernel(tc, qT, k_words, k_scales
         for t in range(4):
             score_tile(0, t, scores[t], [(0, 1)])
             silu(p0, scores[t], 0, t, 0, 128)
+        w_bf0 = [nested("w_first", BF16, 2), tile("w_second", [P, 512], BF16)[:]]
+        w_places = tile("w_places", [P, 4, (128 - GPSIMD_QUERIES) // 4, 4], BF16)[:]
+        for t in range(4):
+            nc.scalar.activation(w_places[:, t], p0[:, GPSIMD_QUERIES // 4 : 32, t, :], ACT.Copy, scale=vs_cols0[:, t : t + 1])
         scores = [ps.tile([P, NQ], F32, name=("bank_a", "bank_c", "bank_d", "score0")[t]) for t in range(4)]
         for t in range(4):
             score_tile(0, t, scores[t], [(1, 0), (1, 1)])
             silu(p0, scores[t], 0, t, 128, NQ)
+        nc.scalar.copy(
+            w_bf0[0][:, 4 * GPSIMD_QUERIES :].rearrange("p (c i t) -> p c t i", i=4, t=4),
+            w_places.rearrange("p t c i -> p c t i"),
+        )
         scores = [ps.tile([P, NQ], F32, name=("score1", "score2", "score3", "bank_a")[t]) for t in range(4)]
         for t in range(4):
             score_tile(1, t, scores[t], [(0, 0), (0, 1), (1, 0), (1, 1)])
@@ -258,11 +269,10 @@ def tile_attend_silu_kb_gate_topkq256n1024t2048_kernel(tc, qT, k_words, k_scales
             silu(p1, scores[t], 1, t, 0, NQ)
         vs_bank1 = turn(vs_got1, "bank_c")
 
-        w_bf0 = [nested("w_first", BF16, 2), tile("w_second", [P, 512], BF16)[:]]
         nc.gpsimd.tensor_tensor(
-            w_bf0[0].rearrange("p (c i t) -> p c i t", i=4, t=4),
-            p0[:, 0:32].rearrange("p c t i -> p c i t"),
-            vs_cols0.unsqueeze(1).unsqueeze(1).to_broadcast([P, 32, 4, 4]),
+            w_bf0[0][:, 0 : 4 * GPSIMD_QUERIES].rearrange("p (c i t) -> p c i t", i=4, t=4),
+            p0[:, 0 : GPSIMD_QUERIES // 4].rearrange("p c t i -> p c i t"),
+            vs_cols0.unsqueeze(1).unsqueeze(1).to_broadcast([P, GPSIMD_QUERIES // 4, 4, 4]),
             ALU.mult,
         )
         nc.vector.tensor_tensor(

@@ -18,7 +18,7 @@ FP4X4 = mybir.dt.float4_e2m1fn_x4
 ACT = mybir.ActivationFunctionType
 ALU = mybir.AluOpType
 P = 128
-GPSIMD_QUERIES = 96
+GPSIMD_END = 104
 
 NESTED = {
     "v_raw0": (4096, None),
@@ -29,12 +29,12 @@ NESTED = {
     "s_got": (1024, None),
     "q_bf0": (2048, "s_got"),
     "q_raw0": (4096, None),
-    "k_got0": (2048, "q_raw0"),
+    "k_split0": (2048, "q_raw0"),
     "q_raw1": (4096, None),
     "k_got2": (1024, "q_raw1"),
     "vs_got1": (2048, "k_got2"),
     "k_got3": (1024, "q_raw1"),
-    "w_first": (1024, "k_got3"),
+    "w_bf0": (2048, "k_got3"),
     "k_split1": (2048, "q_raw1"),
     "kb_cols0": (64, "q_raw1"),
     "v_codes": (1024, "kb_cols0"),
@@ -187,7 +187,7 @@ def tile_attend_silu_kb_gate_topkq256n1024t2048_kernel(tc, qT, k_words, k_scales
         nc.scalar.activation(gate[:], tanh, ACT.Copy, bias=1.0 / 32.0, scale=1.0 / 32.0)
 
         k_got = {}
-        k_splits = [tile("k_split0", [P, 2048], U8)[:], nested("k_split1", U8, 1)]
+        k_splits = [nested(f"k_split{g}", U8, 1) for g in range(2)]
 
         def gather_keys(quarter, got):
             k_got[quarter] = got
@@ -228,7 +228,7 @@ def tile_attend_silu_kb_gate_topkq256n1024t2048_kernel(tc, qT, k_words, k_scales
             )
 
         q_codes = tile("q_codes", [P, 2 * NQ], U32)[:]
-        k_got0 = nested("k_got0", U32, 4)
+        k_got0 = tile("k_got0", [P, 512], U32)[:]
         nc.vector.tensor_copy(k_got0, k_pool[:].bitcast(U32).indirect(offsets[:, 0:32]))
         quantise_queries(0)
         nc.vector.tensor_copy(
@@ -249,18 +249,10 @@ def tile_attend_silu_kb_gate_topkq256n1024t2048_kernel(tc, qT, k_words, k_scales
         for t in range(4):
             score_tile(0, t, scores[t], [(0, 1)])
             silu(p0, scores[t], 0, t, 0, 128)
-        w_bf0 = [nested("w_first", BF16, 2), tile("w_second", [P, 512], BF16)[:]]
-        w_places = tile("w_places", [P, 4, (128 - GPSIMD_QUERIES) // 4, 4], BF16)[:]
-        for t in range(4):
-            nc.scalar.activation(w_places[:, t], p0[:, GPSIMD_QUERIES // 4 : 32, t, :], ACT.Copy, scale=vs_cols0[:, t : t + 1])
         scores = [ps.tile([P, NQ], F32, name=("bank_a", "bank_c", "bank_d", "score0")[t]) for t in range(4)]
         for t in range(4):
             score_tile(0, t, scores[t], [(1, 0), (1, 1)])
             silu(p0, scores[t], 0, t, 128, NQ)
-        nc.scalar.copy(
-            w_bf0[0][:, 4 * GPSIMD_QUERIES :].rearrange("p (c i t) -> p c t i", i=4, t=4),
-            w_places.rearrange("p t c i -> p c t i"),
-        )
         scores = [ps.tile([P, NQ], F32, name=("score1", "score2", "score3", "bank_a")[t]) for t in range(4)]
         for t in range(4):
             score_tile(1, t, scores[t], [(0, 0), (0, 1), (1, 0), (1, 1)])
@@ -269,16 +261,17 @@ def tile_attend_silu_kb_gate_topkq256n1024t2048_kernel(tc, qT, k_words, k_scales
             silu(p1, scores[t], 1, t, 0, NQ)
         vs_bank1 = turn(vs_got1, "bank_c")
 
+        w_all0 = nested("w_bf0", BF16, 2)
         nc.gpsimd.tensor_tensor(
-            w_bf0[0][:, 0 : 4 * GPSIMD_QUERIES].rearrange("p (c i t) -> p c i t", i=4, t=4),
-            p0[:, 0 : GPSIMD_QUERIES // 4].rearrange("p c t i -> p c i t"),
-            vs_cols0.unsqueeze(1).unsqueeze(1).to_broadcast([P, GPSIMD_QUERIES // 4, 4, 4]),
+            w_all0[:, 0 : 4 * GPSIMD_END].rearrange("p (c i t) -> p c i t", i=4, t=4),
+            p0[:, 0 : GPSIMD_END // 4].rearrange("p c t i -> p c i t"),
+            vs_cols0.unsqueeze(1).unsqueeze(1).to_broadcast([P, GPSIMD_END // 4, 4, 4]),
             ALU.mult,
         )
         nc.vector.tensor_tensor(
-            w_bf0[1].rearrange("p (c i t) -> p c t i", i=4, t=4),
-            p0[:, 32:64],
-            vs_bank0[:, :, P - 1].unsqueeze(1).unsqueeze(3).to_broadcast([P, 32, 4, 4]),
+            w_all0[:, 4 * GPSIMD_END :].rearrange("p (c i t) -> p c t i", i=4, t=4),
+            p0[:, GPSIMD_END // 4 :],
+            vs_bank0[:, :, P - 1].unsqueeze(1).unsqueeze(3).to_broadcast([P, (NQ - GPSIMD_END) // 4, 4, 4]),
             ALU.mult,
         )
         v_codes = nested("v_codes", U32, 4)
@@ -286,29 +279,28 @@ def tile_attend_silu_kb_gate_topkq256n1024t2048_kernel(tc, qT, k_words, k_scales
         nc.vector.quantize_mx(out=v_codes.bitcast(FP8X4), scales=v_plane[:], in_=v_bf)
         w_codes = [tile(f"w_codes{g}", [P, NQ], U32) for g in range(2)]
         w_plane = [tile(f"w_plane{g}", [P, NQ], U8) for g in range(2)]
-        w_bf = [w_bf0, [tile(f"w_bf1{h}", [P, 512], BF16)[:] for h in range(2)]]
+        w_bf1 = [tile(f"w_bf1{h}", [P, 512], BF16)[:] for h in range(2)]
 
         def weigh(h):
             nc.vector.tensor_tensor(
-                w_bf[1][h].rearrange("p (c i t) -> p c t i", i=4, t=4),
+                w_bf1[h].rearrange("p (c i t) -> p c t i", i=4, t=4),
                 p1[:, 32 * h : 32 * (h + 1)],
                 vs_bank1[:, :, P - 1].unsqueeze(1).unsqueeze(3).to_broadcast([P, 32, 4, 4]),
                 ALU.mult,
             )
 
-        def quantise_weights(g, h):
+        def quantise_weights(h):
             nc.vector.quantize_mx(
-                out=w_codes[g][:, 128 * h : 128 * (h + 1)].bitcast(FP8X4),
-                scales=w_plane[g][:, 128 * h : 128 * (h + 1)],
-                in_=w_bf[g][h],
+                out=w_codes[1][:, 128 * h : 128 * (h + 1)].bitcast(FP8X4),
+                scales=w_plane[1][:, 128 * h : 128 * (h + 1)],
+                in_=w_bf1[h],
             )
 
-        quantise_weights(0, 1)
-        quantise_weights(0, 0)
+        nc.vector.quantize_mx(out=w_codes[0][:].bitcast(FP8X4), scales=w_plane[0][:], in_=w_all0)
         weigh(0)
         weigh(1)
-        quantise_weights(1, 0)
-        quantise_weights(1, 1)
+        quantise_weights(0)
+        quantise_weights(1)
 
         for h in range(2):
             y = ps.tile([P, DV], F32, name=("score0", "bank_d")[h])

@@ -19,6 +19,8 @@ ACT = mybir.ActivationFunctionType
 ALU = mybir.AluOpType
 P = 128
 GPSIMD_END = 104
+VECTOR_END = 192
+SCALAR_START = 216
 
 NESTED = {
     "v_raw0": (4096, None),
@@ -34,7 +36,8 @@ NESTED = {
     "k_got2": (1024, "q_raw1"),
     "vs_got1": (2048, "k_got2"),
     "k_got3": (1024, "q_raw1"),
-    "w_bf0": (2048, "k_got3"),
+    "w_early": (1536, "k_got3"),
+    "w_late": (512, "w_early"),
     "k_split1": (2048, "q_raw1"),
     "kb_cols0": (64, "q_raw1"),
     "v_codes": (1024, "kb_cols0"),
@@ -261,7 +264,7 @@ def tile_attend_silu_kb_gate_topkq256n1024t2048_kernel(tc, qT, k_words, k_scales
             silu(p1, scores[t], 1, t, 0, NQ)
         vs_bank1 = turn(vs_got1, "bank_c")
 
-        w_all0 = nested("w_bf0", BF16, 2)
+        w_all0 = nested("w_early", BF16, 2)
         nc.gpsimd.tensor_tensor(
             w_all0[:, 0 : 4 * GPSIMD_END].rearrange("p (c i t) -> p c i t", i=4, t=4),
             p0[:, 0 : GPSIMD_END // 4].rearrange("p c t i -> p c i t"),
@@ -270,8 +273,8 @@ def tile_attend_silu_kb_gate_topkq256n1024t2048_kernel(tc, qT, k_words, k_scales
         )
         nc.vector.tensor_tensor(
             w_all0[:, 4 * GPSIMD_END :].rearrange("p (c i t) -> p c t i", i=4, t=4),
-            p0[:, GPSIMD_END // 4 :],
-            vs_bank0[:, :, P - 1].unsqueeze(1).unsqueeze(3).to_broadcast([P, (NQ - GPSIMD_END) // 4, 4, 4]),
+            p0[:, GPSIMD_END // 4 : VECTOR_END // 4],
+            vs_bank0[:, :, P - 1].unsqueeze(1).unsqueeze(3).to_broadcast([P, (VECTOR_END - GPSIMD_END) // 4, 4, 4]),
             ALU.mult,
         )
         v_codes = nested("v_codes", U32, 4)
@@ -281,13 +284,16 @@ def tile_attend_silu_kb_gate_topkq256n1024t2048_kernel(tc, qT, k_words, k_scales
         w_plane = [tile(f"w_plane{g}", [P, NQ], U8) for g in range(2)]
         w_bf1 = [tile(f"w_bf1{h}", [P, 512], BF16)[:] for h in range(2)]
 
-        def weigh(h):
+        def weigh(h, end):
             nc.vector.tensor_tensor(
-                w_bf1[h].rearrange("p (c i t) -> p c t i", i=4, t=4),
-                p1[:, 32 * h : 32 * (h + 1)],
-                vs_bank1[:, :, P - 1].unsqueeze(1).unsqueeze(3).to_broadcast([P, 32, 4, 4]),
+                w_bf1[h][:, 0 : 4 * (end - 128 * h)].rearrange("p (c i t) -> p c t i", i=4, t=4),
+                p1[:, 32 * h : end // 4],
+                vs_bank1[:, :, P - 1].unsqueeze(1).unsqueeze(3).to_broadcast([P, end // 4 - 32 * h, 4, 4]),
                 ALU.mult,
             )
+
+        def quantise_first(q0, q1, w):
+            nc.vector.quantize_mx(out=w_codes[0][:, q0:q1].bitcast(FP8X4), scales=w_plane[0][:, q0:q1], in_=w)
 
         def quantise_weights(h):
             nc.vector.quantize_mx(
@@ -296,10 +302,28 @@ def tile_attend_silu_kb_gate_topkq256n1024t2048_kernel(tc, qT, k_words, k_scales
                 in_=w_bf1[h],
             )
 
-        nc.vector.quantize_mx(out=w_codes[0][:].bitcast(FP8X4), scales=w_plane[0][:], in_=w_all0)
-        weigh(0)
-        weigh(1)
+        quantise_first(0, 128, w_all0[:, 0:512])
+        quantise_first(128, VECTOR_END, w_all0[:, 512 : 4 * VECTOR_END])
+        w_late = nested("w_late", BF16, 2)
+        nc.gpsimd.tensor_tensor(
+            w_late.rearrange("p (c i t) -> p c i t", i=4, t=4),
+            p0[:, VECTOR_END // 4 :].rearrange("p c t i -> p c i t"),
+            vs_cols0.unsqueeze(1).unsqueeze(1).to_broadcast([P, (NQ - VECTOR_END) // 4, 4, 4]),
+            ALU.mult,
+        )
+        vs_cols1 = tile("vs_cols1", [P, 4], F32)[:]
+        nc.vector.tensor_copy(vs_cols1, vs_bank1[:, :, P - 1])
+        weigh(0, 128)
+        weigh(1, SCALAR_START)
+        w_places = tile("w_places", [P, 4, (NQ - SCALAR_START) // 4, 4], BF16)[:]
+        for t in range(4):
+            nc.scalar.activation(w_places[:, t], p1[:, SCALAR_START // 4 :, t, :], ACT.Copy, scale=vs_cols1[:, t : t + 1])
+        nc.scalar.copy(
+            w_bf1[1][:, 4 * (SCALAR_START - 128) :].rearrange("p (c i t) -> p c t i", i=4, t=4),
+            w_places.rearrange("p t c i -> p c t i"),
+        )
         quantise_weights(0)
+        quantise_first(VECTOR_END, NQ, w_late)
         quantise_weights(1)
 
         for h in range(2):

@@ -33,8 +33,6 @@ NESTED = {
     "q_raw0": (4096, None),
     "k_split0": (2048, "q_raw0"),
     "q_raw1": (4096, None),
-    "k_got2": (1024, "q_raw1"),
-    "vs_got1": (2048, "k_got2"),
     "k_got3": (1024, "q_raw1"),
     "w_early": (1536, "k_got3"),
     "w_late": (512, "w_early"),
@@ -45,6 +43,8 @@ NESTED = {
     "vs_cols0": (64, "q_raw1"),
     "tanh": (1024, "q_raw1"),
     "v_bf": (2048, "q_raw1"),
+    "k_first": (3072, None),
+    "vs_got1": (2048, "k_first"),
 }
 
 
@@ -77,14 +77,14 @@ def tile_attend_silu_kb_gate_topkq256n1024t2048_kernel(tc, qT, k_words, k_scales
         offsets = sb.tile([P, N // 16], U16, name="offsets")
         nc.sync.dma_start(offsets[:], offs)
 
+        s_pool = tile("s_pool", [P, T], U8)
+        nc.scalar.dma_start(s_pool[96:P, :].bitcast(I32), k_scales.rearrange("o f t -> f o t").bitcast(I32))
         zero = tile("zero", [P, 1], F32)
         nc.vector.memset(zero[:], 0.0)
         silu0 = tile("silu0", [P, 1], F32)
         nc.scalar.activation(silu0[:], zero[:], ACT.Silu)
 
-        s_pool = tile("s_pool", [P, T], U8)
         nc.gpsimd.memset(s_pool[0:96, :].bitcast(I32), 0)
-        nc.sync.dma_start(s_pool[96:P, :].bitcast(I32), k_scales.rearrange("o f t -> f o t").bitcast(I32))
         kb_pool = tile("kb_pool", [P, T], F32)
         nc.gpsimd.memset(kb_pool[0 : P - 1, :].bitcast(I32), 0)
         nc.sync.dma_start(kb_pool[P - 1 : P, :], kb[0:1, :])
@@ -99,12 +99,12 @@ def tile_attend_silu_kb_gate_topkq256n1024t2048_kernel(tc, qT, k_words, k_scales
             nc.sync.dma_start(v_raw[c], vT[:, T // 2 * c : T // 2 * (c + 1)])
         q_raw = [nested(f"q_raw{o}", F32, 4).rearrange("p (j n) -> p j n", j=4) for o in range(2)]
         q_rows = qT[0].rearrange("(o p j) n -> o p j n", o=2, j=4)
-        nc.sync.dma_start(q_raw[0], q_rows[0])
         vs_pool = tile("zero", [P, T], F32)
         nc.gpsimd.memset(vs_pool[0 : P - 1, :].bitcast(I32), 0)
         nc.sync.dma_start(vs_pool[P - 1 : P, :], vs[0:1, :])
         k_pool = tile("k_pool", [P, T], I32)
         nc.sync.dma_start(k_pool[:], k_words[0].rearrange("p t b -> p (t b)").bitcast(I32))
+        nc.sync.dma_start(q_raw[0], q_rows[0])
         nc.sync.dma_start(q_raw[1], q_rows[1])
         og_sb = tile("og_sb", [P, 2 * DV], F32)[:]
         nc.sync.dma_start(og_sb.rearrange("p (h e) -> p h e", h=2), og[0].rearrange("(h p) e -> p h e", h=2))
@@ -231,15 +231,16 @@ def tile_attend_silu_kb_gate_topkq256n1024t2048_kernel(tc, qT, k_words, k_scales
             )
 
         q_codes = tile("q_codes", [P, 2 * NQ], U32)[:]
-        k_got0 = tile("k_got0", [P, 512], U32)[:]
-        nc.vector.tensor_copy(k_got0, k_pool[:].bitcast(U32).indirect(offsets[:, 0:32]))
+        k_first = nested("k_first", U32, 4)
+        nc.vector.tensor_copy(k_first, k_pool[:].bitcast(U32).indirect(offsets[:, 0:48]))
+        k_got0 = k_first[:, 0:512]
+        k_got[2] = k_first[:, 512:768]
         quantise_queries(0)
         nc.vector.tensor_copy(
             k_splits[0].bitcast(U16).rearrange("p (o t b r) -> p o t b r", o=2, t=4, r=8),
             k_got0.bitcast(U16).rearrange("p (b t r o) -> p o t b r", o=2, t=4, r=8),
         )
         quantise_queries(1)
-        gather_keys(2, nested("k_got2", U32, 4))
         gather_keys(3, nested("k_got3", U32, 4))
         split_keys(2)
         split_keys(3)

@@ -21,6 +21,7 @@ P = 128
 GPSIMD_END = 104
 VECTOR_END = 192
 SCALAR_START = 216
+CAST_SPLIT = 176
 
 NESTED = {
     "v_raw0": (4096, None),
@@ -30,6 +31,8 @@ NESTED = {
     "vs_got0": (2048, "v_raw1"),
     "s_got": (1024, None),
     "q_bf0": (2048, "s_got"),
+    "k_got2": (1024, "q_bf0"),
+    "vs_got1": (2048, "k_got2"),
     "q_raw0": (4096, None),
     "k_split0": (2048, "q_raw0"),
     "q_raw1": (4096, None),
@@ -43,8 +46,7 @@ NESTED = {
     "vs_cols0": (64, "q_raw1"),
     "tanh": (1024, "q_raw1"),
     "v_bf": (2048, "q_raw1"),
-    "k_first": (3072, None),
-    "vs_got1": (2048, "k_first"),
+    "k_first": (2048, None),
 }
 
 
@@ -147,15 +149,17 @@ def tile_attend_silu_kb_gate_topkq256n1024t2048_kernel(tc, qT, k_words, k_scales
         vs_bank0 = turn(gather_row(vs_pool, 0, nested("vs_got0", F32, 4)), "bank_b")
 
         q_bf = [nested("q_bf0", BF16, 2).rearrange("p (n t) -> p n t", t=4), tile("q_bf1", [P, NQ, 4], BF16)[:]]
-        nc.gpsimd.tensor_scalar(q_bf[0], q_raw[0].rearrange("p t n -> p n t"), 1.0, 0.0, ALU.mult, ALU.add)
+        nc.gpsimd.tensor_scalar(
+            q_bf[0][:, 0:CAST_SPLIT, :], q_raw[0][:, :, 0:CAST_SPLIT].rearrange("p t n -> p n t"), 1.0, 0.0, ALU.mult, ALU.add
+        )
         q_plane = tile("q_plane", [P, 2 * NQ], U8)
         v_got = [tile(f"v_got{g}", [P, 512], BF16)[:] for g in range(2)]
         v_bank = ps.tile([P, 2, 2, P], F32, name="bank_d")
 
-        def cast_queries(o):
+        def cast_queries(o, q0):
             nc.scalar.copy(
-                q_bf[o].rearrange("p (c i) t -> p c t i", i=4),
-                q_raw[o].rearrange("p t (c i) -> p c t i", i=4),
+                q_bf[o][:, q0:, :].rearrange("p (c i) t -> p c t i", i=4),
+                q_raw[o][:, :, q0:].rearrange("p t (c i) -> p c t i", i=4),
             )
 
         def quantise_queries(o):
@@ -177,7 +181,8 @@ def tile_attend_silu_kb_gate_topkq256n1024t2048_kernel(tc, qT, k_words, k_scales
 
         gather_values(0)
         gather_values(1)
-        cast_queries(1)
+        cast_queries(0, CAST_SPLIT)
+        cast_queries(1, 0)
         kb_all = [last_column(nested(f"kb_cols{g}", F32, 4)[:, 0:4], kb_banks[g]) for g in range(2)]
         kb_cols = [[kb_all[g][:, t : t + 1] for t in range(4)] for g in range(2)]
         vs_cols0 = last_column(nested("vs_cols0", F32, 4)[:, 0:4], vs_bank0)
@@ -232,14 +237,14 @@ def tile_attend_silu_kb_gate_topkq256n1024t2048_kernel(tc, qT, k_words, k_scales
 
         q_codes = tile("q_codes", [P, 2 * NQ], U32)[:]
         k_first = nested("k_first", U32, 4)
-        nc.vector.tensor_copy(k_first, k_pool[:].bitcast(U32).indirect(offsets[:, 0:48]))
-        k_got0 = k_first[:, 0:512]
-        k_got[2] = k_first[:, 512:768]
+        nc.vector.tensor_copy(k_first, k_pool[:].bitcast(U32).indirect(offsets[:, 0:32]))
+        k_got0 = k_first
         quantise_queries(0)
         nc.vector.tensor_copy(
             k_splits[0].bitcast(U16).rearrange("p (o t b r) -> p o t b r", o=2, t=4, r=8),
             k_got0.bitcast(U16).rearrange("p (b t r o) -> p o t b r", o=2, t=4, r=8),
         )
+        gather_keys(2, nested("k_got2", U32, 4))
         quantise_queries(1)
         gather_keys(3, nested("k_got3", U32, 4))
         split_keys(2)
@@ -248,15 +253,21 @@ def tile_attend_silu_kb_gate_topkq256n1024t2048_kernel(tc, qT, k_words, k_scales
 
         p0 = tile("p0", [P, NQ // 4, 4, 4], F32)[:]
         scores = [ps.tile([P, NQ], F32, name=f"score{t}") for t in range(4)]
+        second = [ps.tile([P, NQ], F32, name=name) for name in ("bank_a", "bank_c")]
         for t in range(4):
             score_tile(0, t, scores[t], [(0, 0)])
+        for t in range(2):
+            score_tile(0, t, second[t], [(1, 0)])
         for t in range(4):
             score_tile(0, t, scores[t], [(0, 1)])
             silu(p0, scores[t], 0, t, 0, 128)
-        scores = [ps.tile([P, NQ], F32, name=("bank_a", "bank_c", "bank_d", "score0")[t]) for t in range(4)]
-        for t in range(4):
-            score_tile(0, t, scores[t], [(1, 0), (1, 1)])
-            silu(p0, scores[t], 0, t, 128, NQ)
+        for t in range(2):
+            score_tile(0, t, second[t], [(1, 1)])
+            silu(p0, second[t], 0, t, 128, NQ)
+        for t in range(2, 4):
+            late = ps.tile([P, NQ], F32, name=("bank_d", "score0")[t - 2])
+            score_tile(0, t, late, [(1, 0), (1, 1)])
+            silu(p0, late, 0, t, 128, NQ)
         scores = [ps.tile([P, NQ], F32, name=("score1", "score2", "score3", "bank_a")[t]) for t in range(4)]
         for t in range(4):
             score_tile(1, t, scores[t], [(0, 0), (0, 1), (1, 0), (1, 1)])

@@ -204,10 +204,10 @@ def tile_attend_silu_kb_gate_topkq256n1024t2048_kernel(tc, qT, k_words, k_scales
         def split_keys(quarter):
             g, half = divmod(quarter, 2)
             nc.vector.tensor_copy(
-                k_splits[g].bitcast(U16).rearrange("p (o t b r) -> p o t b r", o=2, t=4, r=8)[
-                    :, :, :, 8 * half : 8 * (half + 1), :
+                k_splits[g].bitcast(U16).rearrange("p (o t b r) -> p b t o r", o=2, t=4, r=8)[
+                    :, 8 * half : 8 * (half + 1)
                 ],
-                k_got[quarter].bitcast(U16).rearrange("p (b t r o) -> p o t b r", o=2, t=4, r=8),
+                k_got[quarter].bitcast(U16).rearrange("p (b t r o) -> p b t o r", o=2, t=4, r=8),
             )
 
         def score_tile(g, t, scores, passes):
@@ -241,8 +241,8 @@ def tile_attend_silu_kb_gate_topkq256n1024t2048_kernel(tc, qT, k_words, k_scales
         k_got0 = k_first
         quantise_queries(0)
         nc.vector.tensor_copy(
-            k_splits[0].bitcast(U16).rearrange("p (o t b r) -> p o t b r", o=2, t=4, r=8),
-            k_got0.bitcast(U16).rearrange("p (b t r o) -> p o t b r", o=2, t=4, r=8),
+            k_splits[0].bitcast(U16).rearrange("p (o t b r) -> p b t o r", o=2, t=4, r=8),
+            k_got0.bitcast(U16).rearrange("p (b t r o) -> p b t o r", o=2, t=4, r=8),
         )
         gather_keys(2, nested("k_got2", U32, 4))
         quantise_queries(1)

from contextlib import ExitStack

import concourse.mybir as mybir
from concourse.masks import make_identity

T, N, D, DV, NQ = 2048, 1024, 1024, 128, 256
FLOPS = 2 * NQ * N * (D + DV)
BYTES = 4 * D * NQ + 128 * T * 4 + 32 * T + 4 * DV * T + 2 * 4 * T + 2 * 4 * NQ * DV + 128 * 64 * 2

F32 = mybir.dt.float32
BF16 = mybir.dt.bfloat16
I32 = mybir.dt.int32
U32 = mybir.dt.uint32
U16 = mybir.dt.uint16
U8 = mybir.dt.uint8
FP8X4 = mybir.dt.float8_e4m3fn_x4
FP4X4 = mybir.dt.float4_e2m1fn_x4
ACT = mybir.ActivationFunctionType
ALU = mybir.AluOpType
P = 128
GPSIMD_END = 104
VECTOR_END = 192
SCALAR_START = 216
CAST_SPLIT = 176

NESTED = {
    "v_raw0": (4096, None),
    "s_first": (1024, "v_raw0"),
    "kb_got1": (2048, "v_raw0"),
    "v_raw1": (4096, None),
    "vs_got0": (2048, "v_raw1"),
    "s_got": (1024, None),
    "q_bf0": (2048, "s_got"),
    "k_got2": (1024, "q_bf0"),
    "vs_got1": (2048, "k_got2"),
    "q_raw0": (4096, None),
    "k_split0": (2048, "q_raw0"),
    "q_raw1": (4096, None),
    "k_got3": (1024, "q_raw1"),
    "w_early": (1536, "k_got3"),
    "w_late": (512, "w_early"),
    "k_split1": (2048, "q_raw1"),
    "kb_cols0": (64, "q_raw1"),
    "v_codes": (1024, "kb_cols0"),
    "kb_cols1": (64, "q_raw1"),
    "vs_cols0": (64, "q_raw1"),
    "tanh": (1024, "q_raw1"),
    "v_bf": (2048, "q_raw1"),
    "k_first": (2048, None),
}


def nested_bytes(name):
    return NESTED[name][0] + sum(nested_bytes(c) for c in NESTED if NESTED[c][1] == name)


def nested_offset(name):
    parent = NESTED[name][1]
    names = list(NESTED)
    before = [c for c in names[: names.index(name)] if NESTED[c][1] == parent]
    start = 0 if parent is None else nested_offset(parent) + NESTED[parent][0]
    return start + sum(nested_bytes(c) for c in before)


def tile_attend_silu_kb_gate_topkq256n1024t2048_kernel(tc, qT, k_words, k_scales, vT, vs, kb, og, offs, out):
    nc = tc.nc
    with ExitStack() as ctx:
        sb = ctx.enter_context(tc.tile_pool(name="sb", bufs=1))
        ps = ctx.enter_context(tc.psum_pool(name="ps", bufs=1))
        relay = ctx.enter_context(tc.tile_pool(name="relay", bufs=1))

        def nested(name, dtype, size):
            whole = relay.tile([P, nested_bytes(name) // size], dtype, name=name, align_bytes=64, offset=nested_offset(name))
            return whole[:, 0 : NESTED[name][0] // size]

        def tile(name, shape, dtype):
            return sb.tile(shape, dtype, name=name, align_bytes=64)

        offsets = sb.tile([P, N // 16], U16, name="offsets")
        nc.sync.dma_start(offsets[:], offs)

        s_pool = tile("s_pool", [P, T], U8)
        nc.scalar.dma_start(s_pool[96:P, :].bitcast(I32), k_scales.rearrange("o f t -> f o t").bitcast(I32))
        zero = tile("zero", [P, 1], F32)
        nc.vector.memset(zero[:], 0.0)
        silu0 = tile("silu0", [P, 1], F32)
        nc.scalar.activation(silu0[:], zero[:], ACT.Silu)

        nc.gpsimd.memset(s_pool[0:96, :].bitcast(I32), 0)
        kb_pool = tile("kb_pool", [P, T], F32)
        nc.gpsimd.memset(kb_pool[0 : P - 1, :].bitcast(I32), 0)
        nc.sync.dma_start(kb_pool[P - 1 : P, :], kb[0:1, :])
        k_planes_all = tile("k_planes", [P, 2 * N + 4], U8)
        nc.vector.memset(k_planes_all[:].bitcast(I32), 0)
        k_planes = k_planes_all[:, 0 : 2 * N].rearrange("p (o n) -> p o n", o=2)
        ident = tile("ident", [P, P], F32)
        make_identity(nc, ident[:])

        v_raw = [nested(f"v_raw{c}", F32, 4) for c in range(2)]
        for c in range(2):
            nc.sync.dma_start(v_raw[c], vT[:, T // 2 * c : T // 2 * (c + 1)])
        q_raw = [nested(f"q_raw{o}", F32, 4).rearrange("p (j n) -> p j n", j=4) for o in range(2)]
        q_rows = qT[0].rearrange("(o p j) n -> o p j n", o=2, j=4)
        vs_pool = tile("zero", [P, T], F32)
        nc.gpsimd.memset(vs_pool[0 : P - 1, :].bitcast(I32), 0)
        nc.sync.dma_start(vs_pool[P - 1 : P, :], vs[0:1, :])
        k_pool = tile("k_pool", [P, T], I32)
        nc.sync.dma_start(k_pool[:], k_words[0].rearrange("p t b -> p (t b)").bitcast(I32))
        nc.sync.dma_start(q_raw[0], q_rows[0])
        nc.sync.dma_start(q_raw[1], q_rows[1])
        og_sb = tile("og_sb", [P, 2 * DV], F32)[:]
        nc.sync.dma_start(og_sb.rearrange("p (h e) -> p h e", h=2), og[0].rearrange("(h p) e -> p h e", h=2))

        def turn(got, bank_name):
            bank = ps.tile([P, 4, P], F32, name=bank_name)
            for t in range(4):
                nc.tensor.transpose(bank[:, t, :], got[:, P * t : P * (t + 1)], ident[:])
            return bank

        def last_column(cols, bank):
            nc.scalar.copy(cols, bank[:, :, P - 1])
            return cols

        def gather_row(pool, g, got):
            nc.vector.tensor_copy(
                got.bitcast(U32).rearrange("p (t b r) -> p b t r", t=4, r=8),
                pool[:].bitcast(U32).indirect(offsets[:, 32 * g : 32 * (g + 1)]),
            )
            return got

        s_got = nested("s_got", U8, 1)
        nc.vector.tensor_copy(s_got, s_pool[:].indirect(offsets[:]))
        kb_banks = [turn(gather_row(kb_pool, 0, tile("kb_got0", [P, 512], F32)[:]), "bank_a")]

        v_pool = tile("v_pool", [P, T], BF16)
        for c in range(2):
            nc.scalar.copy(v_pool[:, T // 2 * c : T // 2 * (c + 1)], v_raw[c])
        s_first = nested("s_first", U8, 1)
        nc.vector.tensor_copy(
            s_first.bitcast(I32).rearrange("p (g t b w) -> p g t b w", g=2, t=4, w=2),
            s_got.bitcast(I32).rearrange("p (g b t w) -> p g t b w", g=2, t=4, w=2),
        )
        for quad in range(4):
            nc.sync.dma_start(
                k_planes[32 * quad : 32 * quad + 4].bitcast(I32),
                s_first[96 + 8 * quad : 96 + 8 * quad + 8, :].bitcast(I32),
            )
        kb_banks.append(turn(gather_row(kb_pool, 1, nested("kb_got1", F32, 4)), "bank_c"))
        vs_bank0 = turn(gather_row(vs_pool, 0, nested("vs_got0", F32, 4)), "bank_b")

        q_bf = [nested("q_bf0", BF16, 2).rearrange("p (n t) -> p n t", t=4), tile("q_bf1", [P, NQ, 4], BF16)[:]]
        nc.gpsimd.tensor_scalar(
            q_bf[0][:, 0:CAST_SPLIT, :], q_raw[0][:, :, 0:CAST_SPLIT].rearrange("p t n -> p n t"), 1.0, 0.0, ALU.mult, ALU.add
        )
        q_plane = tile("q_plane", [P, 2 * NQ], U8)
        v_got = [tile(f"v_got{g}", [P, 512], BF16)[:] for g in range(2)]
        v_bank = ps.tile([P, 2, 2, P], F32, name="bank_d")

        def cast_queries(o, q0):
            nc.scalar.copy(
                q_bf[o][:, q0:, :].rearrange("p (c i) t -> p c t i", i=4),
                q_raw[o][:, :, q0:].rearrange("p t (c i) -> p c t i", i=4),
            )

        def quantise_queries(o):
            nc.vector.quantize_mx(
                out=q_codes[:, NQ * o : NQ * (o + 1)].bitcast(FP8X4),
                scales=q_plane[:, NQ * o : NQ * (o + 1)],
                in_=q_bf[o].rearrange("p n t -> p (n t)"),
            )

        def gather_values(g):
            nc.scalar.activation(
                v_got[g].rearrange("p (b r t) -> p b t r", r=8, t=4),
                v_pool[:].indirect(offsets[:, 32 * g : 32 * (g + 1)]),
                ACT.Copy,
            )
            pairs = v_got[g].bitcast(F32).rearrange("p (s u) -> p s u", u=2)
            for u in range(2):
                nc.tensor.transpose(v_bank[:, g, u, :], pairs[:, :, u], ident[:])

        gather_values(0)
        gather_values(1)
        cast_queries(0, CAST_SPLIT)
        cast_queries(1, 0)
        kb_all = [last_column(nested(f"kb_cols{g}", F32, 4)[:, 0:4], kb_banks[g]) for g in range(2)]
        kb_cols = [[kb_all[g][:, t : t + 1] for t in range(4)] for g in range(2)]
        vs_cols0 = last_column(nested("vs_cols0", F32, 4)[:, 0:4], vs_bank0)

        tanh = nested("tanh", F32, 4)
        nc.scalar.activation(tanh, og_sb, ACT.Tanh, bias=silu0[:], scale=0.5)
        v_bf = nested("v_bf", BF16, 2)
        nc.scalar.copy(v_bf.bitcast(F32).rearrange("p (g e u) -> p g e u", g=2, u=2), v_bank[:].rearrange("p g u e -> p g e u"))
        gate = tile("gate", [P, 2 * DV], F32)
        nc.scalar.activation(gate[:], tanh, ACT.Copy, bias=1.0 / 32.0, scale=1.0 / 32.0)

        k_got = {}
        k_splits = [nested(f"k_split{g}", U8, 1) for g in range(2)]

        def gather_keys(quarter, got):
            k_got[quarter] = got
            nc.vector.tensor_copy(got, k_pool[:].bitcast(U32).indirect(offsets[:, 16 * quarter : 16 * (quarter + 1)]))

        def split_keys(quarter):
            g, half = divmod(quarter, 2)
            nc.vector.tensor_copy(
                k_splits[g].bitcast(U16).rearrange("p (o t b r) -> p b t o r", o=2, t=4, r=8)[
                    :, 8 * half : 8 * (half + 1)
                ],
                k_got[quarter].bitcast(U16).rearrange("p (b t r o) -> p b t o r", o=2, t=4, r=8),
            )

        def score_tile(g, t, scores, passes):
            for h, o in passes:
                if True:
                    k0 = 1024 * o + 256 * t
                    s0 = 512 * g + 128 * t
                    q0 = NQ * o + 128 * h
                    nc.tensor.matmul_mx(
                        out=scores[:, 128 * h : 128 * (h + 1)],
                        lhsT=k_splits[g][:, k0 : k0 + 256].bitcast(FP4X4),
                        lhsT_scale=k_planes[:, o, s0 : s0 + 128],
                        rhs=q_codes[:, q0 : q0 + 128].bitcast(FP8X4),
                        rhs_scale=q_plane[:, q0 : q0 + 128],
                        start=(o == 0),
                        stop=(o == 1),
                    )
            return scores

        def silu(p_g, scores, g, t, q0, q1):
            nc.scalar.activation(
                p_g[:, q0 // 4 : q1 // 4, t, :],
                scores[:, q0:q1].rearrange("p (c i) -> p c i", i=4),
                ACT.Silu,
                bias=kb_cols[g][t],
            )

        q_codes = tile("q_codes", [P, 2 * NQ], U32)[:]
        k_first = nested("k_first", U32, 4)
        nc.vector.tensor_copy(k_first, k_pool[:].bitcast(U32).indirect(offsets[:, 0:32]))
        k_got0 = k_first
        quantise_queries(0)
        nc.vector.tensor_copy(
            k_splits[0].bitcast(U16).rearrange("p (o t b r) -> p b t o r", o=2, t=4, r=8),
            k_got0.bitcast(U16).rearrange("p (b t r o) -> p b t o r", o=2, t=4, r=8),
        )
        gather_keys(2, nested("k_got2", U32, 4))
        quantise_queries(1)
        gather_keys(3, nested("k_got3", U32, 4))
        split_keys(2)
        split_keys(3)
        vs_got1 = gather_row(vs_pool, 1, nested("vs_got1", F32, 4))

        p0 = tile("p0", [P, NQ // 4, 4, 4], F32)[:]
        scores = [ps.tile([P, NQ], F32, name=f"score{t}") for t in range(4)]
        second = [ps.tile([P, NQ], F32, name=name) for name in ("bank_a", "bank_c")]
        for t in range(4):
            score_tile(0, t, scores[t], [(0, 0)])
        for t in range(2):
            score_tile(0, t, second[t], [(1, 0)])
        for t in range(4):
            score_tile(0, t, scores[t], [(0, 1)])
            silu(p0, scores[t], 0, t, 0, 128)
        for t in range(2):
            score_tile(0, t, second[t], [(1, 1)])
            silu(p0, second[t], 0, t, 128, NQ)
        for t in range(2, 4):
            late = ps.tile([P, NQ], F32, name=("bank_d", "score0")[t - 2])
            score_tile(0, t, late, [(1, 0), (1, 1)])
            silu(p0, late, 0, t, 128, NQ)
        scores = [ps.tile([P, NQ], F32, name=("score1", "score2", "score3", "bank_a")[t]) for t in range(4)]
        for t in range(4):
            score_tile(1, t, scores[t], [(0, 0), (0, 1), (1, 0), (1, 1)])
        p1 = tile("p1", [P, NQ // 4, 4, 4], F32)[:]
        for t in range(4):
            silu(p1, scores[t], 1, t, 0, NQ)
        vs_bank1 = turn(vs_got1, "bank_c")

        w_all0 = nested("w_early", BF16, 2)
        nc.gpsimd.tensor_tensor(
            w_all0[:, 0 : 4 * GPSIMD_END].rearrange("p (c i t) -> p c i t", i=4, t=4),
            p0[:, 0 : GPSIMD_END // 4].rearrange("p c t i -> p c i t"),
            vs_cols0.unsqueeze(1).unsqueeze(1).to_broadcast([P, GPSIMD_END // 4, 4, 4]),
            ALU.mult,
        )
        nc.vector.tensor_tensor(
            w_all0[:, 4 * GPSIMD_END :].rearrange("p (c i t) -> p c t i", i=4, t=4),
            p0[:, GPSIMD_END // 4 : VECTOR_END // 4],
            vs_bank0[:, :, P - 1].unsqueeze(1).unsqueeze(3).to_broadcast([P, (VECTOR_END - GPSIMD_END) // 4, 4, 4]),
            ALU.mult,
        )
        v_codes = nested("v_codes", U32, 4)
        v_plane = tile("v_plane", [P, 2 * DV], U8)
        nc.vector.quantize_mx(out=v_codes.bitcast(FP8X4), scales=v_plane[:], in_=v_bf)
        w_codes = [tile(f"w_codes{g}", [P, NQ], U32) for g in range(2)]
        w_plane = [tile(f"w_plane{g}", [P, NQ], U8) for g in range(2)]
        w_bf1 = [tile(f"w_bf1{h}", [P, 512], BF16)[:] for h in range(2)]

        def weigh(h, end):
            nc.vector.tensor_tensor(
                w_bf1[h][:, 0 : 4 * (end - 128 * h)].rearrange("p (c i t) -> p c t i", i=4, t=4),
                p1[:, 32 * h : end // 4],
                vs_bank1[:, :, P - 1].unsqueeze(1).unsqueeze(3).to_broadcast([P, end // 4 - 32 * h, 4, 4]),
                ALU.mult,
            )

        def quantise_first(q0, q1, w):
            nc.vector.quantize_mx(out=w_codes[0][:, q0:q1].bitcast(FP8X4), scales=w_plane[0][:, q0:q1], in_=w)

        def quantise_weights(h):
            nc.vector.quantize_mx(
                out=w_codes[1][:, 128 * h : 128 * (h + 1)].bitcast(FP8X4),
                scales=w_plane[1][:, 128 * h : 128 * (h + 1)],
                in_=w_bf1[h],
            )

        quantise_first(0, 128, w_all0[:, 0:512])
        quantise_first(128, VECTOR_END, w_all0[:, 512 : 4 * VECTOR_END])
        w_late = nested("w_late", BF16, 2)
        nc.gpsimd.tensor_tensor(
            w_late.rearrange("p (c i t) -> p c i t", i=4, t=4),
            p0[:, VECTOR_END // 4 :].rearrange("p c t i -> p c i t"),
            vs_cols0.unsqueeze(1).unsqueeze(1).to_broadcast([P, (NQ - VECTOR_END) // 4, 4, 4]),
            ALU.mult,
        )
        vs_cols1 = tile("vs_cols1", [P, 4], F32)[:]
        nc.vector.tensor_copy(vs_cols1, vs_bank1[:, :, P - 1])
        weigh(0, 128)
        weigh(1, SCALAR_START)
        w_places = tile("w_places", [P, 4, (NQ - SCALAR_START) // 4, 4], BF16)[:]
        for t in range(4):
            nc.scalar.activation(w_places[:, t], p1[:, SCALAR_START // 4 :, t, :], ACT.Copy, scale=vs_cols1[:, t : t + 1])
        nc.scalar.copy(
            w_bf1[1][:, 4 * (SCALAR_START - 128) :].rearrange("p (c i t) -> p c t i", i=4, t=4),
            w_places.rearrange("p t c i -> p c t i"),
        )
        quantise_weights(0)
        quantise_first(VECTOR_END, NQ, w_late)
        quantise_weights(1)

        for h in range(2):
            y = ps.tile([P, DV], F32, name=("score0", "bank_d")[h])
            for g in range(2):
                nc.tensor.matmul_mx(
                    out=y[:],
                    lhsT=w_codes[g][:, 128 * h : 128 * (h + 1)].bitcast(FP8X4),
                    lhsT_scale=w_plane[g][:, 128 * h : 128 * (h + 1)],
                    rhs=v_codes[:, DV * g : DV * (g + 1)].bitcast(FP8X4),
                    rhs_scale=v_plane[:, DV * g : DV * (g + 1)],
                    start=(g == 0),
                    stop=(g == 1),
                )
            res = tile(f"res{h}", [P, DV], F32)
            nc.vector.tensor_tensor(res[:], y[:], gate[:, DV * h : DV * (h + 1)], ALU.mult)
            queue = nc.scalar if h == 0 else nc.sync
            queue.dma_start(out[0, 128 * h : 128 * (h + 1), :], res[:])
